import numpy as np, ml_dtypes
CORES = [6,15,38,47]
N = 4
BF = ml_dtypes.bfloat16
S, SETS, SH, B, L, RO, NS, EPS = 4096, 8, 3, 451, 256, 5, 8, 140
def sky(rng):
    c = rng.integers(0, 16, (N, 8, 16, S)); t = rng.integers(0, S, (N, 8, 16, SETS * B))
    return c, np.where(rng.random(t.shape) < 0.0625, S, t)
def pack(c, t, v):
    return {"cvec": np.ascontiguousarray(c).reshape(N, 128, S).astype(np.float32).astype(BF), "tsee": np.ascontiguousarray(t).reshape(N, 128, SETS * B).astype(np.int32),
            "obs": np.ascontiguousarray(v).reshape(N, 128, NS * L).astype(np.float32).astype(BF)}
def uneven(rng, shape):
    k = shape[:-2] + (1, shape[-1]); m = rng.choice(np.array([0, 1, 2, 4, 7, 11, 15]), k)
    x = np.minimum((rng.random(shape) * (m + 1)).astype(np.int64), m)
    return np.where(rng.random(k) < 0.25, 15 - x, x)
def sized(n):
    w = np.indices((15, 15, 15, 15)).reshape(4, -1).T; at = np.unique(np.sum(w * w, axis=1), return_index=True)[1]
    return np.concatenate([15 * (np.arange(12) < n[..., None] // 225), w[at[n % 225]]], axis=-1)
def setup_inputs(rng):
    c, t = sky(rng); P = 24; pool = rng.integers(0, 16, (8, SETS, 16, P)); size = rng.integers(NS + 2, P + 1, (1, 8, 1, 1))
    pick = np.argsort(rng.random((N, 8, L, P)) + (np.arange(P) >= size), axis=-1)[..., :NS]
    v = pool[np.arange(8).reshape(1, 8, 1, 1), (np.arange(L) % SETS).reshape(1, 1, L, 1), :, pick]
    v = v.transpose(0, 1, 4, 3, 2); near = rng.random((N, 8, 1, NS, L)) < 0.25
    return pack(c, t, np.clip(v + near * rng.integers(-1, 2, v.shape), 0, 15))
def setup_inputs_spread(rng):
    c = uneven(rng, (N, 8, 16, S)); v = uneven(rng, (N, 8, 16, NS * L)).reshape(N, 8, 16, NS, L)
    u = rng.random((N, 8, 16, SETS * B)); t = np.minimum((S * u * u * u * u).astype(np.int64), S - 1)
    return pack(c, np.where(rng.random(t.shape) < 0.08, S, t), v)
def setup_inputs_ends(rng):
    c = 15 * (rng.random((N, 8, 16, S)) < rng.choice(np.array([0.0, 0.25, 0.5, 0.75, 1.0]), (N, 8, 1, S)))
    c[:, 1::2, :, 0] = 15; c[..., S - 1] = 15
    kind = rng.integers(0, 4, (N, 8, 1, 1, L)); kind[..., 0] = 1; kind[..., L - 1] = 0; kind[..., L - 1 - SETS] = 0
    some = rng.random((N, 8, 16, NS, L)) < 0.5; bit = rng.random((N, 8, 1, NS, L)) < 0.5
    v = 15 * np.where(kind == 0, True, np.where(kind == 1, False, np.where(kind == 2, some, bit)))
    u = rng.random((N, 8, 16, SETS * B)); t = np.where(u < 0.4, 0, np.where(u < 0.7, S, np.where(u < 0.8, S - 1, rng.integers(1, S, u.shape))))
    tv = t.reshape(N, 8, 16, SETS, B); m = rng.random((N, 8, 1, SETS)) < 0.5; m[..., SETS - 1] = True
    late = np.array([S] * 13 + [0, S - 1, S - 1]).reshape(1, 1, 16, 1)
    tv[..., B - 1] = np.where(m, late, tv[..., B - 1])
    return pack(c, tv.reshape(N, 8, 16, SETS * B), v)
def setup_inputs_corners(rng):
    c, t = sky(rng); x = np.zeros((10, 16), np.int64)
    x[0, 0:6] = 15; x[1, 0:6] = 15; x[2, 3:6] = 15; x[3, 0:6] = 15; x[4, 0:3] = 15; x[4, 6:9] = 15; x[5, 0:3] = 15; x[6, 3:9] = 15; x[7, 6:9] = 15
    x[1, 12] = EPS // 10; x[1, 13] = EPS % 10; x[3, 12] = (EPS + 1) // 10; x[3, 13] = (EPS + 1) % 10; x[4:6, 12] = 10; x[4:6, 13] = 1
    for k, n in ((8, 675 - EPS), (9, 674 - EPS)):
        x[k, 0:2] = 15; x[k, 2] = n // 15 - 30; x[k, 3:6] = 15; x[k, 12] = (n % 15) // 10; x[k, 13] = (n % 15) % 10
    nm = np.zeros((N, 8, 10), np.int64)
    for q in range(N):
        for g in range(8):
            nm[q, g] = rng.permutation(np.concatenate([np.array([0, S - 1]), 1 + rng.permutation(S - 2)[:8]])); c[q, g][:, nm[q, g]] = x.T
    pt = np.array([[0, 0, 0, 0, 0, 0], [16, 16, 0, 0, 0, 0], [16, 15, 0, 0, 0, 0], [15, 16, 0, 0, 0, 0], [0, 16, 16, 0, 0, 0], [16, 0, 15, 0, 0, 0], [15, 0, 16, 0, 0, 0], [0, 15, 16, 0, 0, 0],
                   [1, 0, 0, 0, 0, 0], [0, 1, 0, 0, 0, 0], [0, 0, 1, 0, 0, 0], [1, 1, 0, 0, 1, 0], [1, 1, 1, 0, 1, 2], [2, 3, 0, 0, 0, 0], [3, 2, 0, 0, 1, 0], [0, 3, 2, 0, 0, 3], [0, 2, 3, 0, 0, 1],
                   [2, 0, 3, 0, 0, 0], [3, 0, 2, 0, 0, 2], [5, 5, 5, 0, 5, 10], [5, 6, 5, 0, 5, 11], [8, 8, 8, 0, 4, 8], [1, 1, 1, 0, 0, 0], [16, 16, 16, 0, 0, 0], [15, 15, 15, 0, 0, 0], [16, 16, 1, 0, 0, 0], [2, 16, 2, 0, 0, 1], [16, 0, 16, 0, 0, 0]])
    kd = rng.integers(0, len(pt), (N, 8, SETS, 5)); pos = np.argsort(rng.random((N, 8, SETS, 5, 16)), axis=-1)
    pos = np.where(rng.random((N, 8, SETS, 5, 1)) < 0.25, 15 - np.arange(16), pos); w = pt[kd][..., None, :]
    hold = ((pos[..., None] - w[..., 3:]) % 16) < w[..., :3]; way = rng.integers(0, 3, pos.shape)
    qi = np.arange(N).reshape(N, 1, 1, 1, 1); gi = np.arange(8).reshape(1, 8, 1, 1, 1)
    na = nm[qi, gi, np.where(hold[..., 0], np.array([0, 1, 8])[way], np.array([2, 3, 9])[way])]
    na = np.where((kd[..., None] == 0) & (rng.random(pos.shape) < 0.5), S, na)
    nb = nm[qi, gi, np.where(hold[..., 2], 4, 5)]; ne = nm[qi, gi, np.where(hold[..., 1], 6, 7)]
    tv = t.reshape(N, 8, 16, SETS, B)
    for k in range(5):
        for y, z in ((na, 1), (nb, 6), (ne, 11)): tv[..., (15 * (k + z)) >> SH] = y[:, :, :, k].transpose(0, 1, 3, 2)
    k = rng.integers(1, 6, (N, 8, L)); v = np.zeros((N, 8, 16, NS, L), np.int64)
    v[:, :, 9:12, 0] = 15; v[:, :, 0:6, 1] = 15; v[:, :, 9, 1] = k; v[:, :, 0:3, 2] = 15; v[:, :, 6:9, 2] = 15; v[:, :, 10, 2] = k + 5; v[:, :, 3:9, 3] = 15; v[:, :, 11, 3] = k + 10
    v[:, :, :, 4:] = np.take_along_axis(v, rng.integers(1, 4, (N, 8, 1, NS - 4, L)), 3)
    v = np.where(rng.random((N, 8, 1, 1, L)) < 0.2, rng.integers(0, 16, v.shape), v)
    return pack(c, tv.reshape(N, 8, 16, SETS * B), v)
def setup_inputs_crowd(rng):
    M = NS + N; base = rng.integers(0, 16, (8, SETS, 16, M)); D = np.einsum("ghfj,ghfk->ghjk", base, base)
    c, t = sky(rng); nm = np.argsort(rng.random((N, 8, S)), axis=-1)[..., :SETS * M].reshape(N, 8, SETS, M); tv = t.reshape(N, 8, 16, SETS, B)
    gi = np.arange(8).reshape(8, 1, 1); hi = np.arange(SETS).reshape(1, SETS, 1); pi = np.arange(16).reshape(1, 1, 16)
    for q in range(N):
        for g in range(8): c[q, g][:, nm[q, g].reshape(-1)] = base[g].transpose(1, 0, 2).reshape(16, -1)
        kind = rng.integers(0, 3, (8, SETS, 1)); miss = rng.integers(0, 16, (8, SETS, 1))
        prs = [(k, k + z) for k in list(range(M - 2, -1, -1)) + [q + N] for z in (3, 2, 1) if k + z < M] + [(q, j) for j in list(range(q)) + list(range(M - 1, q, -1))]
        for k, j in prs:
            know = np.where(kind == 0, True, np.where(kind == 1, pi != miss, rng.random((8, SETS, 16)) < 0.6)); bn = (D[:, :, k, j] >> SH)[:, :, None]
            tv[q, gi, pi, hi, bn] = np.where(know, nm[q, :, :, j][:, :, None], tv[q, gi, pi, hi, bn])
    v = np.zeros((N, 8, 16, NS, L), np.int64); hl = np.arange(L) % SETS
    for r in range(N):
        o = np.zeros((8, L, NS), np.int64) + np.arange(NS) + r
        o[2::4, :, 2:] = 2 + r + np.argsort(rng.random((2, L, NS - 2)), axis=-1)
        odd = (np.arange(L) // SETS) % 2 == 1; o[3::4, odd, 1] = 2 + r; o[3::4, odd, 2] = 1 + r
        v[r] = base[gi, hl.reshape(1, L, 1), :, o].transpose(0, 3, 2, 1)
        for g in (1, 5):
            ln = np.arange(SETS) + SETS * rng.integers(0, L // SETS, SETS); v[r, g][:, :, ln] = rng.integers(0, 16, (16, NS, SETS))
    return pack(c, tv.reshape(N, 8, 16, SETS * B), v)
def setup_inputs_full(rng):
    d = setup_inputs(rng); c = d["cvec"].astype(np.float32).astype(np.int64).reshape(N, 8, 16, S); t = d["tsee"].astype(np.int64).reshape(N, 8, 16, SETS * B); v = d["obs"].astype(np.float32).astype(np.int64).reshape(N, 8, 16, NS, L)
    lane = np.arange(L); lo = ((EPS + 1) >> SH) + 1; hi = (2923 - EPS) >> SH
    for g in (0, 2, 5, 7):
        bn = np.argsort(rng.random((SETS, hi - lo)), axis=1)[:, :L // SETS] + lo
        D = ((bn << SH) + rng.integers(0, 1 << SH, bn.shape)).T.reshape(L)
        if g >= 5: D[1] = EPS; D[2] = EPS + 1
        col = B * (lane % SETS) + (D >> SH)
        for q in range(N):
            nm = rng.permutation(S)[:8 * L].reshape(L, 8)
            off = rng.integers(1 - EPS, EPS, (L, 8)); off[:, :4] = np.array([EPS, -EPS, EPS + 1, -EPS - 1])
            x = sized(np.maximum(D[:, None] + off, 0)); x = np.take_along_axis(x, np.argsort(rng.random(x.shape), axis=-1), -1)
            c[q, g][:, nm.reshape(-1)] = x.reshape(-1, 16).T
            h0 = rng.integers(0, 16, L); h0[0] = 0; h0[L - 1] = 15
            good = rng.random((L, 16)) < rng.random((L, 1)) * (g > 0); good[L - 1] = False; good[lane, h0] = True
            on = np.array([0, 1, 4, 5, 6, 7])[(rng.integers(0, 6, (L, 1)) + np.arange(16)) % 6]
            name = np.take_along_axis(nm, np.where(good, on, rng.integers(2, 4, (L, 16))), 1)
            name = np.where(~good & (rng.random((L, 16)) < 0.25), S, name)
            if g >= 5: name[1] = np.where(np.arange(16) < h0[1], nm[1, 2], S)
            t[q, g][:, col] = name.T
            y = sized(D); y = np.take_along_axis(y, np.argsort(rng.random(y.shape), axis=-1), -1); v[q, g] = y.T[:, None, :]
    return pack(c, t, v)
def check_inputs(d):
    bad = []
    for k, hi in (("cvec", 15), ("tsee", S), ("obs", 15)):
        x = np.asarray(d[k]).astype(np.float32)
        if not np.all((x >= 0) & (x <= hi) & (x == np.floor(x))): bad.append("range of " + k)
    return bad
def reference(cvec, tsee, obs):
    c = cvec.astype(np.float32).astype(np.int32).reshape(N, 8, 16, S); c = np.concatenate([c, np.zeros((N, 8, 16, 1), np.int32)], axis=3)
    t = tsee.astype(np.int64).reshape(N, 8, 16, SETS * B); v = obs.astype(np.float32).astype(np.int64).reshape(N, 8, 16, NS, L)
    gram = np.einsum("rgfjl,rgfkl->rgjkl", v, v)
    st = np.zeros((N, 4, 8, L), np.int64) + np.arange(4).reshape(1, 4, 1, 1)
    gi = np.arange(8).reshape(8, 1); ln = np.arange(L).reshape(1, L); first = B * (ln % SETS)
    out = np.zeros((N, 8, RO, 3, L), np.float32)
    for rnd in range(RO):
        for q in range(N):
            r = (q - rnd) % N
            o, a, b, e = st[r, 0], st[r, 1], st[r, 2], st[r, 3]; G = gram[r]
            col = [first + (G[gi, o, z, ln] >> SH) for z in (a, b, e)]
            nam = [np.take_along_axis(t[q], k[:, None, :], 2) for k in col]
            vec = [np.take_along_axis(c[q], k.reshape(8, 1, 16 * L), 2).reshape(8, 16, 16, L) for k in nam]
            hold = [np.abs(np.sum(vec[i] * vec[j], axis=1) - G[gi, y, z, ln][:, None, :]) <= EPS for i, j, y, z in ((0, 1, a, b), (0, 2, a, e), (1, 2, b, e))]
            every = hold[0] & hold[1] & hold[2]; found = np.any(every, axis=1); p = np.argmax(every, axis=1)
            for k in range(3): out[q, :, rnd, k] = np.where(found, np.take_along_axis(nam[k], p[:, None, :], 1)[:, 0], -1)
            if rnd == RO - 1: continue
            for g in range(8):
                w = np.nonzero(found[g])[0]; cs, at = np.unique(col[0][g, w], return_index=True); t[q, g, p[g, w[at]], cs] = S
            ab, ac, bc = [np.sum(k, axis=1) for k in hold]
            spike = np.argmin(np.stack([ab + ac, ab + bc, ac + bc]), axis=0); nxt = rnd + 4
            st[r] = np.stack([np.where(found, a, o), np.where(found, b, np.where(spike == 0, nxt, a)), np.where(found, e, np.where(spike == 1, nxt, b)), np.where(found, nxt, np.where(spike == 2, nxt, e))])
    return {"yn": out.reshape(N, 8, RO * 3 * L)}

@@ -1,0 +1,486 @@
+import numpy as np
+from concourse.mybir import AluOpType, ActivationFunctionType
+
+ALU = AluOpType
+ACT = ActivationFunctionType
+RO, NB, DUMP = 5, 451, 128
+W = 233.0
+MAGIC = 1.5 * 2.0 ** 39
+OBSW = [2048, 1280, 1536, 1792]
+
+AB_PLAIN = [True, True]
+C_PLAIN = [True, True]
+COSTS = [(0.001, 0.0006, 1.56, 1.0, 0.12, 0.07, 3.0), (0.001, 0.0006, 1.2, 1.0, 0.15, 0.1, 4.0), (0.001, 0.0008, 1.9, 1.0, 0.12, 0.07, 3.0)]
+EV_ON, FIRST_ON = "V", "V"
+CHUNKS = [(0, 64), (64, 128)]
+SEARCH, SEED = 6000, 1
+ORDER = {}
+
+SCRATCH = {
+    "cv": ("sbuf", [128, 4112], "bfloat16"),
+    "obs0": ("sbuf", [128, OBSW[0]], "bfloat16"), "obs1": ("sbuf", [128, OBSW[1]], "bfloat16"),
+    "obs2": ("sbuf", [128, OBSW[2]], "bfloat16"), "obs3": ("sbuf", [128, OBSW[3]], "bfloat16"),
+    "ybuf": ("sbuf", [128, 48 * RO], "float32"),
+    "pidx": ("sbuf", [128, 8], "int32"), "pand": ("sbuf", [128, 8], "int32"), "pcol": ("sbuf", [128, 8], "float32"),
+    "xr": ("sbuf", [128, 144], "float32"), "gr": ("sbuf", [128, 128], "float32"), "dr": ("sbuf", [128, 128], "float32"),
+    "z233": ("sbuf", [128, 144], "bfloat16"), "z125": ("sbuf", [128, 144], "bfloat16"),
+    "zneg": ("sbuf", [128, 144], "bfloat16"), "z32": ("sbuf", [128, 144], "float32"),
+    "bo233": ("sbuf", [128, 128], "bfloat16"), "bo125": ("sbuf", [128, 128], "bfloat16"),
+    "idb": ("sbuf", [128, 128], "bfloat16"), "idf": ("sbuf", [128, 128], "float32"),
+    "tr1": ("sbuf", [128, 128], "bfloat16"), "tr2": ("sbuf", [128, 128], "bfloat16"), "tri": ("sbuf", [128, 128], "bfloat16"),
+    "ci": ("sbuf", [128, 256], "float32"), "cb": ("sbuf", [128, 256], "float32"), "consth": ("sbuf", [128, 256], "float32"),
+    "cl0": ("sbuf", [128, 32], "float32"), "constl": ("sbuf", [128, 32], "float32"),
+    "jl0": ("sbuf", [128, 8], "float32"), "jl": ("sbuf", [128, 8], "float32"),
+    "tie": ("sbuf", [128, 128], "float32"),
+    "mr0": ("sbuf", [128, 8], "float32"), "mrep": ("sbuf", [128, 8], "uint16"),
+    "kr0": ("sbuf", [128, 16], "float32"), "krep": ("sbuf", [128, 16], "uint16"),
+    "clo": ("sbuf", [128, 8], "float32"), "cdl": ("sbuf", [128, 8], "float32"), "cd2": ("sbuf", [128, 8], "float32"),
+    "cd3": ("sbuf", [128, 8], "float32"), "coff": ("sbuf", [128, 8], "uint16"),
+}
+for _s in range(2):
+    for _n, _w, _d in (("tb", DUMP + 4 * NB, "int32"), ("il0", 64, "float32"), ("st", 40 * RO, "int32"),
+                       ("st16", 32, "uint16"), ("ov", 512, "bfloat16"), ("dp", 768, "bfloat16"), ("coll", 32, "int32"),
+                       ("col16", 32, "uint16"), ("nm16", 384, "uint16"), ("ga", 2048, "bfloat16"), ("gb", 2048, "bfloat16"),
+                       ("gcc", 2048, "bfloat16"), ("pr0", 2048, "bfloat16"), ("pr1", 2048, "bfloat16"), ("pr2", 2048, "bfloat16"),
+                       ("fl", 512, "bfloat16"), ("first", 128, "bfloat16"), ("kt", 32, "float32"),
+                       ("cand", 128, "float32"), ("cp", 128, "float32"), ("c3", 32, "int32"),
+                       ("c2", 64, "float32"), ("ns", 32 * (RO - 1), "int32"), ("colh", 256, "int32"), ("key", 8, "float32"),
+                       ("eq", 256, "bfloat16"), ("so", 8, "float32"), ("so16", 8, "uint16"), ("ncol", 128, "int32"),
+                       ("mk", 384, "float32"), ("fm1", 32, "float32")):
+        SCRATCH["%s_%d" % (_n, _s)] = ("sbuf", [128, _w], _d)
+    for _n in ("px", "p1", "p2", "p3"):
+        SCRATCH["%s_%d" % (_n, _s)] = ("psum", [128, 512], "float32")
+
+SEMAPHORES = (["cV", "cS", "cP", "cG", "lobs", "lcv", "lt0", "lt1", "sent", "ao1", "ao2", "ao3", "ahelp"]
+              + ["as%d_%d" % (t, s) for t in range(1, RO) for s in range(2)] + ["out%d" % k for k in range(3 * RO)])
+
+
+def bits(engines):
+    m = 0
+    for e in engines:
+        m |= 1 << e
+    return m
+
+
+def helper_of(core, T, topo):
+    for h in topo.cores_of(core):
+        if T.rank_of(h) is None and topo.die(h) == topo.die(core) and all(topo.may_write(h, d) for d in T.cores if d != core):
+            return h
+    raise ValueError("no helper")
+
+
+def helper_program(g, core, owner, T, topo):
+    n = len(T.cores); r = T.rank_of(owner)
+    far = topo.engines(owner, T.cores[(r + 1) % n])
+    g.wait_ge(T.sem.ahelp, len([e for e in topo.engines(owner, core) if e not in far]))
+    total = 0
+    for k in (2, 3):
+        dst = T.cores[(r + k) % n]; rid, pid, _ = topo.addr(dst)
+        g.remote_dma(T["obs%d" % k][:], T.obs3[:, 0:OBSW[k]], T.sem["ao%d" % k], T.sem.sent, pid, rid, topo.mask(core, dst))
+        total += len(topo.engines(core, dst))
+    g.wait_ge(T.sem.sent, total)
+
+
+def build_ops(g, core, T, topo, cost):
+    ops = []; tag = [None, 0]
+    CY, PCY, RG, CP, _, _, LAT_R = cost
+    V, S, P = g.vector, g.scalar, g.tensor
+    n = len(T.cores); rank = T.rank_of(core)
+    nxt = T.cores[(rank + 1) % n]; prv = T.cores[(rank - 1) % n]
+
+    def op(eng, fn, rd, wr, dur, bank=None, sem=None, ext=None, lat=0.0):
+        ops.append({"eng": eng, "fn": fn, "rd": rd, "wr": wr, "dur": dur, "bank": bank, "sem": sem, "ext": ext, "lat": lat,
+                    "typ": (tag[0], len(ops) - tag[1])})
+
+    def vd(x):
+        return 0.03 + max(64, x) * CY
+
+    def ts(out, in0, s1, s2, o0, o1, rd, wr, x, bank=None, ext=None):
+        if o1 is None:
+            op("V", lambda: V.tensor_scalar(out, in0, s1, None, o0), rd, wr, vd(x), bank, ext=ext)
+        else:
+            op("V", lambda: V.tensor_scalar(out, in0, s1, s2, o0, o1), rd, wr, vd(x), bank, ext=ext)
+
+    def tt(out, in0, in1, o, rd, wr, x, bank=None):
+        op("V", lambda: V.tensor_tensor(out, in0, in1, o), rd, wr, vd(x), bank)
+
+    def cp(out, in_, rd, wr, x, bank=None, ext=None):
+        op("V", lambda: V.tensor_copy(out, in_), rd, wr, vd(x), bank, ext=ext)
+
+    def ms(ap, c, wr, x=64):
+        op("V", lambda: V.memset(ap, c), [], wr, vd(x))
+
+    def sg(out, in_, rd, wr, x, ext=None):
+        op("S", lambda: S.activation(out, in_, ACT.Copy), rd, wr, 0.07 + x * RG * CY, ext=ext)
+
+    def io(name, out, pat, base, cm, x, flt=True):
+        if flt:
+            op("G", lambda: g.iota(out, pat, base, cm, allow_small_or_imprecise_dtypes=True), [], [name], 0.13 + 2 * x * CY)
+        else:
+            op("G", lambda: g.iota(out, pat, base, cm), [], [name], 0.13 + 2 * x * CY)
+
+    def mm(lst, rd, bank, cyc):
+        def fn():
+            last = None
+            for (o, l, r, a, b) in lst:
+                last = P.matmul(o, l, r, a, b)
+            return last
+        op("P", fn, rd, [], 0.05 + cyc * PCY, bank)
+
+    def dma(eng, pairs, rd, wr, sem, lat):
+        q = {"Y": g.sync, "S": g.scalar}[eng]
+
+        def fn():
+            for (o, i) in pairs:
+                q.dma_start(o, i).then_inc(T.sem[sem], 16)
+        op(eng, fn, rd, wr, 0.06 * len(pairs), sem=(sem, 16 * len(pairs)), lat=lat)
+
+    def rdma(out, in_, sem, dst, engines, rd, wr, lat):
+        rid, pid, _ = topo.addr(dst)
+        op("G", lambda: g.remote_dma(out, in_, T.sem[sem], T.sem.sent, pid, rid, bits(engines)), rd, wr, 0.3, sem=("sent", len(engines)), lat=lat)
+
+    def esel(z, u):
+        return z[:, 15 - u:143 - u]
+
+    def tpieces(s):
+        return [(T["tb_%d" % s][:, DUMP + NB * k:DUMP + NB * (k + 1)], T.tsee[:, NB * (2 * k + s):NB * (2 * k + s + 1)]) for k in range(4)]
+    dma("Y", [(T.obs0[:], T.obs[:])], [], ["obs0"], "lobs", 3.5)
+    dma("S", tpieces(0), [], ["tbl0"], "lt0", 8.0)
+    dma("Y", [(T.cv[:, 0:4096], T.cvec[:])], [], ["cvl"], "lcv", 9.5)
+    dma("Y", tpieces(1), ["cvl"], ["tbl1"], "lt1", 5.5)
+    far = topo.engines(core, nxt); hp = helper_of(core, T, topo)
+    near = [e for e in topo.engines(core, hp) if e not in far]
+    rdma(T.obs1[:], T.obs0[:, 0:OBSW[1]], "ao1", nxt, far, ["obs0", "cvl", "tbl0"], ["obs1"], 9.0)
+    rdma(T.obs3[:], T.obs0[:, 0:OBSW[3]], "ahelp", hp, near, ["obs0", "cvl", "tbl0", "o1sent"], ["obs2", "obs3"], 20.0)
+    nin = len(topo.engines(prv, core))
+    obs_ext = {1: ("ao1", nin)}
+    for k in (2, 3):
+        obs_ext[k] = ("ao%d" % k, len(topo.engines(helper_of(T.cores[(rank - k) % n], T, topo), core)))
+
+    pc = T.pcol
+    U, C8, HI, G16, U16, U2 = [pc[:, k:k + 1] for k in range(6)]
+    io("pidx", T.pidx[:, 0:1], [[0, 1]], 0, 1, 1, False)
+    for k, a in enumerate((15, 7, 8, 112)):
+        ts(T.pand[:, k:k + 1], T.pidx[:, 0:1], a, None, ALU.bitwise_and, None, ["pidx"], ["pand%d" % k], 1)
+    cp(pc[:, 0:4], T.pand[:, 0:4], ["pand%d" % k for k in range(4)], ["pc"], 4)
+    ts(U16, U, 16.0, None, ALU.mult, None, ["pc"], ["u16"], 1)
+    ts(U2, U, 2.0, None, ALU.mult, None, ["pc"], ["u2"], 1)
+    for s in range(2):
+        il0, st = T["il0_%d" % s], T["st_%d" % s]
+        io("il0%d" % s, il0[:], [[256, 8], [2, 8]], s, 0, 64)
+        ts(st[:, 0:40], il0[:, 0:40], U16, None, ALU.add, None, ["il0%d" % s, "u16"], ["st%d_0" % s, "stn%d_0" % s], 40)
+        for t in range(1, RO - 1):
+            ts(st[:, 40 * t + 32:40 * t + 40], il0[:, 8 * (t + 4):8 * (t + 5)], U16, None, ALU.add, None, ["il0%d" % s, "u16"], ["stn%d_%d" % (s, t)], 8)
+        ms(T["tb_%d" % s][:, 0:DUMP], 0, ["tbd%d" % s], 128)
+    ms(T.cv[:, 4096:4112], 0.0, ["cvz"])
+    io("xr", T.xr[:], [[1, 144]], -15, 0, 144)
+    for nm, w in (("z125", 0.125), ("z233", W), ("zneg", -2048.0), ("z32", 2.0 ** -12)):
+        ts(T[nm][:], T.xr[:], G16, w, ALU.is_equal, ALU.mult, ["xr", "pc"], [nm], 144)
+    io("gr", T.gr[:], [[16, 8], [0, 16]], 0, 0, 128)
+    ts(T.bo233[:], T.gr[:], G16, -W, ALU.is_equal, ALU.mult, ["gr", "pc"], ["bo233"], 128)
+    ts(T.bo125[:], T.gr[:], G16, 0.125, ALU.is_equal, ALU.mult, ["gr", "pc"], ["bo125"], 128)
+    io("dr", T.dr[:], [[1, 128]], 0, -1, 128)
+    ts(T.idb[:], T.dr[:], 0.0, None, ALU.is_equal, None, ["dr"], ["idb"], 128)
+    ts(T.idf[:], T.dr[:], 0.0, None, ALU.is_equal, None, ["dr"], ["idf"], 128)
+    ts(T.tr1[:], T.dr[:], 0.0, -8.0, ALU.is_gt, ALU.mult, ["dr"], ["tr1"], 128)
+    tt(T.tr2[:], T.tr1[:], T.bo125[:], ALU.mult, ["tr1", "bo125"], ["tr2"], 128)
+    tt(T.tri[:], T.tr2[:], T.idb[:], ALU.add, ["tr2", "idb"], ["tri"], 128)
+    io("cl0", T.cl0[:], [[0, 8], [NB, 4]], DUMP, 0, 32)
+    ts(T.constl[:], T.cl0[:], -0.4375, None, ALU.add, None, ["cl0"], ["constl"], 32)
+    for h in range(2):
+        io("ci%d" % h, T.ci[:, 128 * h:128 * h + 128], [[1, 2], [0, 4], [2, 16]], -h, 0, 128)
+    io("cb", T.cb[:], [[0, 4], [NB, 4], [0, 16]], DUMP, 0, 256)
+    ts(T.ci[:], T.ci[:], U2, 8192.0, ALU.is_le, ALU.mult, ["ci0", "ci1", "u2"], ["ci0", "ci1"], 256)
+    ts(T.cb[:], T.cb[:], -0.4375, None, ALU.add, None, ["cb"], ["cb"], 256)
+    tt(T.consth[:], T.ci[:], T.cb[:], ALU.add, ["ci0", "ci1", "cb"], ["consth"], 512)
+    io("jl0", T.jl0[:], [[16, 8]], 0, 0, 8)
+    ts(T.jl[:], T.jl0[:], U, None, ALU.add, None, ["jl0", "pc"], ["jl"], 8)
+    io("tie", T.tie[:, 0:96], [[4096, 3], [0, 32]], 4096, 0, 96)
+    ms(T.tie[:, 96:128], 0.0, ["tie2"])
+    io("mr0", T.mr0[:], [[8, 4], [0, 2]], 0, 0, 8)
+    ts(T.mrep[:], T.mr0[:], C8, None, ALU.add, None, ["mr0", "pc"], ["mrep"], 8)
+    io("kr0", T.kr0[:], [[4, 2], [0, 2], [1, 4]], 0, 0, 16)
+    cp(T.krep[:], T.kr0[:], ["kr0"], ["krep"], 16)
+    src = [[0, 1, 2, 4], [0, 1, 4, 3], [0, 4, 2, 3], [1, 2, 3, 4]]
+    for k in range(4):
+        lo0, lo1 = src[k][0], src[k][2]
+        io("clo%d" % k, T.clo[:, 2 * k:2 * k + 2], [[8 * (lo1 - lo0), 2]], 8 * lo0, 0, 2)
+        d0, d1 = src[k][1] - lo0, src[k][3] - lo1
+        io("cdl%d" % k, T.cdl[:, 2 * k:2 * k + 2], [[d1 - d0, 2]], d0, 0, 2)
+    ts(T.cd2[:], T.cdl[:], HI, C8, ALU.mult, ALU.add, ["cdl%d" % k for k in range(4)] + ["pc"], ["cd2"], 8)
+    tt(T.cd3[:], T.cd2[:], T.clo[:], ALU.add, ["cd2"] + ["clo%d" % k for k in range(4)], ["cd3"], 8)
+    cp(T.coff[:], T.cd3[:], ["cd3"], ["coff"], 8)
+
+    for t in range(RO):
+        last = t == RO - 1
+        for s in range(2):
+            tag[0], tag[1] = (s, 0 if t == 0 else 2 if last else 1), len(ops)
+
+            def B(x):
+                return T["%s_%d" % (x, s)]
+
+            def R(x):
+                return "%s%d" % (x, s)
+            tb = B("tb")[:]; tbr = [R("tb"), R("tbl"), R("tbd")]
+            st = B("st"); stn = "st%d_%d" % (s, t)
+            ext = ("as%d_%d" % (t, s), nin) if t else None
+            cp(B("st16")[:], st[:, 40 * t:40 * t + 32], [stn], [R("st16")], 32, ext=ext)
+            ob = t % n
+            win = T["obs%d" % ob][:, 0:(1024 if t == 0 else OBSW[ob])]
+            ov, dp = B("ov"), B("dp")
+            sg(ov[:], win.indirect(B("st16")[:]), [R("st16"), "obs%d" % ob], [R("ov")], 512, ext=obs_ext.get(ob))
+            tt(dp[:, 0:128], ov[:, 0:128], ov[:, 384:512], ALU.mult, [R("ov")], [R("dp0")], 128 * CP)
+            tt(dp[:, 128:384], ov[:, 0:256], ov[:, 256:512], ALU.mult, [R("ov")], [R("dp1")], 256 * CP)
+            tt(dp[:, 384:768], ov[:, 0:384], ov[:, 128:512], ALU.mult, [R("ov")], [R("dp2")], 384 * CP)
+            dpr = [R("dp0"), R("dp1"), R("dp2")]
+            p1, p2, p3, px = B("p1"), B("p2"), B("p3"), B("px")
+            mm([(p1[:, 0:32], esel(T.z125, u), dp[:, u:512:16], u == 0, u == 15) for u in range(16)], dpr + ["z125"], R("p1"), 1024)
+            tt(B("coll")[:], p1[:, 0:32], T.constl[:], ALU.add, ["constl"], [R("coll")], 32, R("p1"))
+            c16 = B("col16"); nm = B("nm16")
+            cp(c16[:], B("coll")[:], [R("coll")], [R("col16")], 32)
+            offs = [c16[:, 24:32], c16[:, 8:16], c16[:, 0:8]]
+            cp(nm[:, 0:128], tb.indirect(offs[0]), tbr + [R("col16")], [R("nma")], 128 * RG)
+            cp(nm[:, 128:384], tb.indirect(c16[:, 0:16]), tbr + [R("col16")], [R("nmb")], 256 * RG)
+            if not last:
+                tt(B("cand")[:], st[:, 40 * t:40 * t + 40].indirect(T.coff[:]), T.tie[:], ALU.add,
+                   [stn, "stn%d_%d" % (s, t), "coff", R("st16"), "tie", "tie2"], [R("cand")], 128 * RG)
+                mm([(p1[:, 128 + 128 * h:256 + 128 * h], T.bo125[:], dp[:, 384:512], True, True) for h in range(2)], dpr + ["bo125"], R("p1"), 256)
+                tt(B("colh")[:], p1[:, 128:384], T.consth[:], ALU.add, ["consth"], [R("colh")], 256, R("p1"))
+            cw = T.cv[:, 0:4112]; cvr = ["cvl", "cvz"]
+            dcol = [512, 256, 640]
+            for ch, (l0, l1) in enumerate(CHUNKS):
+                sl = slice(16 * l0, 16 * l1); ne = 16 * (l1 - l0)
+                oa, oc, obb = [nm[:, 128 * k + l0:128 * k + l1] for k in range(3)]
+                ga, gb, gc = B("ga")[:, sl], B("gb")[:, sl], B("gcc")[:, sl]
+                ra, rb, rc = R("ga%d" % ch), R("gb%d" % ch), R("gc%d" % ch)
+                sg(ga, cw.indirect(oa), cvr + [R("nma")], [ra], ne)
+                sg(gb, cw.indirect(obb), cvr + [R("nmb")], [rb], ne)
+                if C_PLAIN[ch]:
+                    sg(gc, cw.indirect(oc), cvr + [R("nmb")], [rc], ne)
+                for q in range(3):
+                    pr = B("pr%d" % q); rp = R("pr%d_%d" % (q, ch))
+                    in1, r1 = (gb, rb) if q == 2 else (ga, ra)
+                    if (AB_PLAIN if q == 0 else C_PLAIN)[ch]:
+                        in0, r0 = (gb, rb) if q == 0 else (gc, rc)
+                        tt(pr[:, sl], in0, in1, ALU.mult, [r0, r1], [rp], ne * CP)
+                    else:
+                        tt(pr[:, sl], cw.indirect(obb if q == 0 else oc), in1, ALU.mult, cvr + [R("nmb"), r1], [rp], ne * RG)
+                    o = px[:, 128 * q + l0:128 * q + l1]
+                    lst = [(o, T.bo233[:], dp[:, dcol[q] + l0:dcol[q] + l1], True, False)]
+                    lst += [(o, esel(T.z233, p), pr[:, 16 * l0 + p:16 * l1:16], False, p == 15) for p in range(16)]
+                    mm(lst, [rp, "bo233", "z233"] + dpr, R("px"), 17 * max(64, l1 - l0))
+            fl = B("fl"); kt = B("kt"); first = B("first")
+
+            def act(out, in_, scale, bias, rd, wr, bank):
+                op("S", lambda: S.activation(out, in_, ACT.Relu, bias=bias, scale=scale), rd, wr, 0.07 + 128 * CY, bank)
+            ts(fl[:, 0:384], px[:, 0:384], MAGIC, MAGIC, ALU.add, ALU.is_equal, [], [R("fl")], 384, R("px"))
+            mm([(p2[:, 0:128], T.idb[:], fl[:, 128 * q:128 * q + 128], q == 0, q == 2) for q in range(3)], [R("fl"), "idb"], R("p2"), 384)
+            if EV_ON == "V":
+                ts(fl[:, 384:512], p2[:, 0:128], 3.0, 32.0, ALU.is_equal, ALU.mult, [], [R("ev")], 128, R("p2"))
+            else:
+                act(fl[:, 384:512], p2[:, 0:128], 32.0, -64.0, [], [R("ev")], R("p2"))
+            if last:
+                mm([(p2[:, 280:288], esel(T.z125, u), fl[:, 384 + u:512:16], u == 0, u == 15) for u in range(16)], [R("ev"), "z125"], R("p2"), 1024)
+            else:
+                mm([(p2[:, 256:288], esel(T.z125, u), fl[:, u:512:16], u == 0, u == 15) for u in range(16)], [R("fl"), R("ev"), "z125"], R("p2"), 1024)
+            mm([(p3[:, 128:256], T.tri[:], fl[:, 384:512], True, True)], [R("ev"), "tri"], R("p3"), 128)
+            k0 = 24 if last else 0
+            ts(kt[:, k0:32], p2[:, 256 + k0:288], 8.0 * 16384.0, None, ALU.mult, None, [], [R("kt")], 32, R("p2"))
+            if FIRST_ON == "V":
+                ts(first[:], p3[:, 128:256], 32.0, 4096.0, ALU.is_equal, ALU.mult, [], [R("first")], 128, R("p3"))
+            else:
+                act(first[:], p3[:, 128:256], 128.0, 0.0, [], [R("first")], R("p3"))
+            if not last:
+                cpr, c2, c3 = B("cp"), B("c2"), B("c3")
+                ns = B("ns")[:, 32 * t:32 * t + 32]
+                tt(cpr[:], kt[:].indirect(T.mrep[:]), B("cand")[:], ALU.add, [R("kt"), R("cand"), "mrep"], [R("cp")], 128 * RG)
+                tt(c2[:], cpr[:, 0:64], cpr[:, 64:128], ALU.max, [R("cp")], [R("c2")], 128)
+                tt(c3[:], c2[:, 0:32], c2[:, 32:64], ALU.max, [R("c2")], [R("c3")], 64)
+                ts(ns, c3[:], 4095, None, ALU.bitwise_and, None, [R("c3")], [R("ns%d" % t)], 32)
+                rdma(st[:, 40 * (t + 1):40 * (t + 1) + 32], ns, "as%d_%d" % (t + 1, s), nxt, far, [R("ns%d" % t)], ["st%d_%d" % (s, t + 1)], LAT_R)
+                key, eq = B("key"), B("eq")
+                tt(key[:], kt[:, 24:32], B("coll")[:, 24:32], ALU.min, [R("kt"), R("coll")], [R("key")], 16)
+                tt(eq[:], key[:].indirect(T.krep[:]), B("colh")[:], ALU.is_equal, [R("key"), R("colh"), "krep"], [R("eq")], 256 * RG)
+                lst = [(p3[:, 0:8], T.idf[:], key[:], True, False)]
+                lst += [(p3[:, 0:8], esel(T.zneg, u), eq[:, 128 * h + u:128 * h + 128:16], False, h == 1 and u == 15) for h in range(2) for u in range(16)]
+                mm(lst, [R("eq"), R("key"), "idf", "zneg"], R("p3"), 2300)
+                tt(B("so")[:], p3[:, 0:8], T.jl[:], ALU.max, ["jl"], [R("so")], 8, R("p3"))
+                cp(B("so16")[:], B("so")[:], [R("so")], [R("so16")], 8)
+                tt(B("ncol")[:], tb.indirect(offs[0]), first[:], ALU.max, tbr + [R("col16"), R("first")], [R("ncol")], 128 * RG)
+            mk = B("mk")
+            for m in range(3):
+                tt(mk[:, 128 * m:128 * m + 128], tb.indirect(offs[m]), first[:], ALU.mult, tbr + [R("col16"), R("first")], [R("mk%d" % m)], 128 * RG)
+            if not last:
+                cp(tb.indirect(B("so16")[:]), B("ncol")[:], [R("so16"), R("ncol"), R("tbl"), R("tbd")], [R("tb")], 128 * 3.8)
+            for k in range(4):
+                mm([(p3[:, 32:56], esel(T.z32, u), mk[:, u:384:16], u == 0, u == 15) for u in range(4 * k, 4 * k + 4)],
+                   [R("mk0"), R("mk1"), R("mk2"), "z32"], R("p3"), 1024)
+            ts(B("fm1")[:], kt[:, 24:32].indirect(T.mrep[:, 0:2]), 1.0, -1.0, ALU.min, ALU.add, [R("kt"), "mrep"], [R("fm1")], 64)
+            tt(T.ybuf[:, 48 * t + s:48 * t + 48:2], p3[:, 32:56], B("fm1")[:, 0:24], ALU.add, [R("fm1")], ["y%d_%d" % (t, s)], 24, R("p3"))
+        for m in range(3):
+            k = 3 * t + m
+            dma("S" if last and m == 1 else "Y", [(T.yn[:, 256 * k:256 * k + 256], T.ybuf[:, 16 * k:16 * k + 16])],
+                ["y%d_0" % t, "y%d_1" % t], [], "out%d" % k, 2.5)
+    return ops
+
+
+def find_deps(ops):
+    writer, readers, bank = {}, {}, {}
+    deps = []
+    for i, o in enumerate(ops):
+        d = {}
+        for r in o["rd"]:
+            if r in writer:
+                d[writer[r]] = True
+        for w in o["wr"]:
+            if w in writer:
+                d[writer[w]] = True
+            for j in readers.get(w, []):
+                d[j] = True
+        if o["bank"] is not None:
+            if o["bank"] in bank:
+                d.setdefault(bank[o["bank"]], False)
+            bank[o["bank"]] = i
+        d.pop(i, None)
+        deps.append(d)
+        for r in o["rd"]:
+            readers.setdefault(r, []).append(i)
+        for w in o["wr"]:
+            writer[w] = i; readers[w] = []
+    return deps
+
+
+def order_queues(variants, deps):
+    ops = variants[0]; n = len(ops)
+    eng = ["VSPGY".index(o["eng"]) for o in ops]
+    tabs = []
+    for v, c in zip(variants, COSTS):
+        pre = [[(j, v[j]["lat"] + c[4] if (eng[j] != eng[i] or v[j]["sem"]) else (c[5] if h and eng[i] != 2 else 0.0))
+                for j, h in deps[i].items()] for i in range(n)]
+        tabs.append(([o["dur"] for o in v], [o["lat"] for o in v], pre))
+    dur, lat, pre = tabs[0]
+    succ = [[] for _ in range(n)]
+    for i in range(n):
+        for j, gp in pre[i]:
+            succ[j].append((i, gp))
+    base = [0.0] * n
+    for i in range(n - 1, -1, -1):
+        base[i] = dur[i] + max([gp + base[k] for k, gp in succ[i]] + [lat[i]])
+
+    def schedule(prio, look):
+        left = [len(d) for d in deps]
+        ready = [0.0] * n; cand = [[] for _ in range(5)]; free = [0.0] * 5; order = []
+        for i in range(n):
+            if not left[i]:
+                cand[eng[i]].append(i)
+        for _ in range(n):
+            bt, be = 1e30, 0
+            for e in range(5):
+                if cand[e]:
+                    t0 = max(free[e], min([ready[i] for i in cand[e]]))
+                    if t0 < bt:
+                        bt, be = t0, e
+            lim = bt + look; bi, bp = -1, -1e30
+            for i in cand[be]:
+                if ready[i] <= lim and prio[i] > bp:
+                    bi, bp = i, prio[i]
+            f = max(free[be], ready[bi]) + dur[bi]; free[be] = f
+            cand[be].remove(bi); order.append(bi)
+            for k, gp in succ[bi]:
+                if f + gp > ready[k]:
+                    ready[k] = f + gp
+                left[k] -= 1
+                if not left[k]:
+                    cand[eng[k]].append(k)
+        return order
+
+    def replay(order, tab):
+        d, lt, pr = tab
+        fin = [0.0] * n; free = [0.0] * 5
+        for i in order:
+            t0 = free[eng[i]]
+            for j, gp in pr[i]:
+                if fin[j] + gp > t0:
+                    t0 = fin[j] + gp
+            fin[i] = free[eng[i]] = t0 + d[i]
+        return fin, max(fin[i] + lt[i] for i in range(n))
+
+    kinds = sorted(set(o["typ"] for o in ops if o["typ"][0] is not None)); kid = {k: x for x, k in enumerate(kinds)}
+    of = [kid.get(o["typ"], -1) for o in ops]
+    rng = np.random.default_rng(SEED)
+
+    def score(shift, look):
+        order = schedule([base[i] + (shift[of[i]] if of[i] >= 0 else 0.0) for i in range(n)], look)
+        return sum(replay(order, tab)[1] for tab in tabs), order
+    best = None
+    for lagv in (6.0, 9.0, 12.0, 15.0):
+        for look in (0.05, 0.15, 0.3):
+            shift = [-lagv * k[0][0] for k in kinds]
+            sc, order = score(shift, look)
+            if best is None or sc < best[0]:
+                best = (sc, order, shift, look)
+    cur = best
+    for it in range(SEARCH):
+        shift = list(cur[2]); look = cur[3]
+        for x in rng.integers(0, len(kinds), int(rng.integers(1, 6))):
+            shift[int(x)] += float(rng.normal()) * 4.0
+        if rng.random() < 0.05:
+            look = float(rng.choice([0.05, 0.1, 0.15, 0.2, 0.3]))
+        sc, order = score(shift, look)
+        if sc < cur[0] + 1.5 * (1.0 - it / SEARCH) * rng.random():
+            cur = (sc, order, shift, look)
+            if sc < best[0]:
+                best = cur
+    return best[1], [replay(best[1], tab) for tab in tabs]
+
+
+def rank_program(g, core, T, topo):
+    rank = T.rank_of(core)
+    if rank is None:
+        for c in T.cores:
+            if helper_of(c, T, topo) == core:
+                helper_program(g, core, c, T, topo)
+        return
+    variants = [build_ops(g, core, T, topo, c) for c in COSTS]
+    ops = variants[0]
+    deps = find_deps(ops)
+    if "all" not in ORDER:
+        ORDER["all"] = order_queues(variants, deps)[0]
+    order = ORDER["all"]
+    queue = {"V": g.vector, "S": g.scalar, "P": g.tensor, "G": g, "Y": g.sync}
+    pos = {i: k for k, i in enumerate(order)}
+    waits = {}; seen = {}; need = set()
+    for i in order:
+        e = ops[i]["eng"]; w = {}
+        for j, hard in deps[i].items():
+            f = ops[j]["eng"]
+            if ops[j]["sem"] or (f == e and (e == "P" or not hard)):
+                continue
+            if pos[j] > seen.get((e, f), -1) and pos[j] > pos.get(w.get(f), -1):
+                w[f] = j
+        for f, j in w.items():
+            seen[(e, f)] = pos[j]; need.add(j)
+        waits[i] = w
+    count = {}; num = {e: 0 for e in "VSPG"}
+    for i in order:
+        if i in need:
+            num[ops[i]["eng"]] += 1; count[i] = num[ops[i]["eng"]]
+    done = set(); total = {}; waited = {}
+    for i in order:
+        o = ops[i]; e = o["eng"]; q = queue[e]
+        sems = [ops[j]["sem"] for j in deps[i] if ops[j]["sem"] and ops[j]["sem"][0] != "sent"]
+        if o["ext"]:
+            sems.append(o["ext"])
+        for (nm, v) in sems:
+            if (e, nm) not in done:
+                done.add((e, nm)); q.wait_ge(T.sem[nm], v); waited[nm] = v
+        for f, j in waits[i].items():
+            q.wait_ge(T.sem["c" + f], count[j])
+        ins = o["fn"]()
+        if i in need:
+            ins.then_inc(T.sem["c" + e], 1)
+        if o["sem"]:
+            total[o["sem"][0]] = total.get(o["sem"][0], 0) + o["sem"][1]
+    for nm, v in total.items():
+        if waited.get(nm, 0) < v:
+            g.wait_ge(T.sem[nm], v)

@@ -3,115 +3,122 @@ from concourse.mybir import AluOpType, ActivationFunctionType
 
 ALU = AluOpType
 ACT = ActivationFunctionType
-RO, NB, DUMP = 5, 451, 128
+RO, NB, TW = 5, 451, 512
 W = 233.0
 MAGIC = 1.5 * 2.0 ** 39
-OBSW = [2048, 1280, 1536, 1792]
+M23, M27 = 1.5 * 2.0 ** 23, 1.5 * 2.0 ** 27
+NEXT = [[1, 2, 3, 4], [0, 4, 2, 3], [0, 1, 2, 4], [0, 1, 4, 3]]
+PAIRS = [(0, 1), (0, 2), (0, 3), (1, 2), (1, 3), (2, 3)]
+STAR = [(0, 6), (0, 10), (1, 6), (1, 2)]
+LATER = [(4, 5), (4, 6), (4, 7), (5, 6), (5, 7), (6, 7)]
+XOFF = [0, 2, 4, 5, 6, 7]
 
-AB_PLAIN = [True, True]
-C_PLAIN = [True, True]
-COSTS = [(0.001, 0.0006, 1.56, 1.0, 0.12, 0.07, 3.0), (0.001, 0.0006, 1.2, 1.0, 0.15, 0.1, 4.0), (0.001, 0.0008, 1.9, 1.0, 0.12, 0.07, 3.0)]
-EV_ON, FIRST_ON = "V", "V"
-CHUNKS = [(0, 64), (64, 128)]
-SEARCH, SEED = 6000, 1
+NS, NH, NC, NL = 2, 4, 8, 128
+HL, HC = 64, 4
+GP = 64
+PP = 64
+SPLIT_NM = 0
+FUSE = [[0, 0, 0, 0]] * 5
+ABS_ON = "V"
+SIGN_ON = "S"
+FIRST_ON = "V"
+DUP = True
+DUP_SO = True
+EQ_ON = "V"
+OUT_ON = "V"
+YF_ON = "V"
+FIRST_CALL = 10.0
+COSTS = [(0.00090, 0.00050, 1.35, 3.8, 0.2, 0.12, 4.5), (0.00087, 0.00044, 1.56, 3.8, 0.1, 0.06, 3.0), (0.00085, 0.00045, 1.1, 2.0, 0.15, 0.1, 3.5), (0.0011, 0.00055, 1.95, 5.0, 0.1, 0.06, 3.0)]
+WEIGHT = [1.0, 1.0, 1.5, 0.7]
+SEARCH = 1500
+SEED = 1
+SWAPS = 12000
+HEAT = 0.1
 ORDER = {}
 
+
+def source(case, pair):
+    x, y = sorted((NEXT[case][pair[0]], NEXT[case][pair[1]]))
+    return STAR[0][1] + x if y == 4 else PAIRS.index((x, y))
+
+
+MD, MS, MH, RD, RF, NM = 0, 3, 6, 12, 15, 17
+
 SCRATCH = {
-    "cv": ("sbuf", [128, 4112], "bfloat16"),
-    "obs0": ("sbuf", [128, OBSW[0]], "bfloat16"), "obs1": ("sbuf", [128, OBSW[1]], "bfloat16"),
-    "obs2": ("sbuf", [128, OBSW[2]], "bfloat16"), "obs3": ("sbuf", [128, OBSW[3]], "bfloat16"),
-    "ybuf": ("sbuf", [128, 48 * RO], "float32"),
-    "pidx": ("sbuf", [128, 8], "int32"), "pand": ("sbuf", [128, 8], "int32"), "pcol": ("sbuf", [128, 8], "float32"),
-    "xr": ("sbuf", [128, 144], "float32"), "gr": ("sbuf", [128, 128], "float32"), "dr": ("sbuf", [128, 128], "float32"),
-    "z233": ("sbuf", [128, 144], "bfloat16"), "z125": ("sbuf", [128, 144], "bfloat16"),
-    "zneg": ("sbuf", [128, 144], "bfloat16"), "z32": ("sbuf", [128, 144], "float32"),
-    "bo233": ("sbuf", [128, 128], "bfloat16"), "bo125": ("sbuf", [128, 128], "bfloat16"),
-    "idb": ("sbuf", [128, 128], "bfloat16"), "idf": ("sbuf", [128, 128], "float32"),
-    "tr1": ("sbuf", [128, 128], "bfloat16"), "tr2": ("sbuf", [128, 128], "bfloat16"), "tri": ("sbuf", [128, 128], "bfloat16"),
-    "ci": ("sbuf", [128, 256], "float32"), "cb": ("sbuf", [128, 256], "float32"), "consth": ("sbuf", [128, 256], "float32"),
-    "cl0": ("sbuf", [128, 32], "float32"), "constl": ("sbuf", [128, 32], "float32"),
-    "jl0": ("sbuf", [128, 8], "float32"), "jl": ("sbuf", [128, 8], "float32"),
-    "tie": ("sbuf", [128, 128], "float32"),
-    "mr0": ("sbuf", [128, 8], "float32"), "mrep": ("sbuf", [128, 8], "uint16"),
-    "kr0": ("sbuf", [128, 16], "float32"), "krep": ("sbuf", [128, 16], "uint16"),
-    "clo": ("sbuf", [128, 8], "float32"), "cdl": ("sbuf", [128, 8], "float32"), "cd2": ("sbuf", [128, 8], "float32"),
-    "cd3": ("sbuf", [128, 8], "float32"), "coff": ("sbuf", [128, 8], "uint16"),
+    "cv": ("sbuf", [128, 4112], "bfloat16"), "ob": ("sbuf", [128, 2048], "bfloat16"),
+    "ovf": ("sbuf", [128, 1024], "bfloat16"), "ovg": ("sbuf", [128, 1024], "bfloat16"), "dp": ("sbuf", [128, 28, 256], "bfloat16"),
+    "ybuf": ("sbuf", [128, 48 * RO], "float32"), "tg": ("sbuf", [128, 8], "float32"), "pe": ("sbuf", [128, 8], "float32"),
+    "pidx": ("sbuf", [128, 8], "int32"), "pand": ("sbuf", [128, 8], "int32"), "pc": ("sbuf", [128, 32], "float32"),
+    "xr": ("sbuf", [128, 144], "float32"), "gr": ("sbuf", [128, 128], "float32"),
+    "zs": ("sbuf", [128, 4 * 144], "bfloat16"), "sq": ("sbuf", [128, 20 * 128], "bfloat16"),
+    "gw0": ("sbuf", [128, 3, 8, 16], "bfloat16"), "gw1": ("sbuf", [128, 8, 16], "bfloat16"),
+    "gw": ("sbuf", [128, 384], "bfloat16"), "rf": ("sbuf", [128, 256], "float32" if YF_ON == "S" else "bfloat16"),
+    "zf": ("sbuf", [128, 144], "float32"), "mkf": ("sbuf", [128, 24, 2, 16], "float32"), "mk": ("sbuf", [128, 24, 2, 16], "float16"),
+    "hq": ("sbuf", [128, 3, 256], "float16"), "codes": ("sbuf", [128, NM, 8, 16], "bfloat16"), "mats": ("sbuf", [128, 128 * NM], "bfloat16"),
+    "ci": ("sbuf", [128, 256], "bfloat16"), "hb": ("sbuf", [128, 256], "bfloat16"), "mask": ("sbuf", [128, 256], "bfloat16"),
+    "cb": ("sbuf", [128, 32], "bfloat16"), "cf": ("sbuf", [128, 32], "bfloat16"),
+    "jl0": ("sbuf", [128, 16], "float32"), "jl": ("sbuf", [128, 16], "float32"),
+    "il0": ("sbuf", [128, 128], "float32"), "il": ("sbuf", [128, 128], "uint16"),
 }
-for _s in range(2):
-    for _n, _w, _d in (("tb", DUMP + 4 * NB, "int32"), ("il0", 64, "float32"), ("st", 40 * RO, "int32"),
-                       ("st16", 32, "uint16"), ("ov", 512, "bfloat16"), ("dp", 768, "bfloat16"), ("coll", 32, "int32"),
-                       ("col16", 32, "uint16"), ("nm16", 384, "uint16"), ("ga", 2048, "bfloat16"), ("gb", 2048, "bfloat16"),
-                       ("gcc", 2048, "bfloat16"), ("pr0", 2048, "bfloat16"), ("pr1", 2048, "bfloat16"), ("pr2", 2048, "bfloat16"),
-                       ("fl", 512, "bfloat16"), ("first", 128, "bfloat16"), ("kt", 32, "float32"),
-                       ("cand", 128, "float32"), ("cp", 128, "float32"), ("c3", 32, "int32"),
-                       ("c2", 64, "float32"), ("ns", 32 * (RO - 1), "int32"), ("colh", 256, "int32"), ("key", 8, "float32"),
-                       ("eq", 256, "bfloat16"), ("so", 8, "float32"), ("so16", 8, "uint16"), ("ncol", 128, "int32"),
-                       ("mk", 384, "float32"), ("fm1", 32, "float32")):
-        SCRATCH["%s_%d" % (_n, _s)] = ("sbuf", [128, _w], _d)
-    for _n in ("px", "p1", "p2", "p3"):
-        SCRATCH["%s_%d" % (_n, _s)] = ("psum", [128, 512], "float32")
+ZS = ["z1", "z125", "z233", "zl"]
+SQ = ["one", "idb", "idn", "idk", "id16", "bd", "bd233", "bdq0", "bdq1", "bdq2", "bda", "bdf", "bdk", "tr", "tri", "pfm", "cpg", "pg", "zero"]
+for _s in range(NS):
+    for _n, _w, _d in (("tb", [NH * TW], "int32"),
+                       ("xi", [XOFF[RO] * NL], "float16"), ("xo", [XOFF[RO] * NL], "float16"),
+                       ("y", [3 * NL], "float16"), ("yf", [3 * NL], "float32" if YF_ON == "S" else "float16"),
+                       ("coli", [RO, 2, 16], "uint16"), ("colo", [RO, 2, 16], "uint16"), ("colf", [16], "float16"),
+                       ("nm16", [3 * NL], "uint16"), ("nmf", [3 * NL], "float16"),
+                       ("gv", [48 * NL], "bfloat16"), ("pr", [48 * NL], "bfloat16"),
+                       ("ab", [3 * NL], "bfloat16"), ("nf", [3 * NL], "bfloat16"), ("v", [2 * NL], "bfloat16"), ("f", [NL], "bfloat16"),
+                       ("ae", [2 * NL], "bfloat16"), ("eq", [2 * NL], "bfloat16"), ("so", [32], "float32"), ("so16", [8], "uint16"),
+                       ("ncol", [NL], "int32")):
+        SCRATCH["%s_%d" % (_n, _s)] = ("sbuf", [128] + _w, _d)
+for _b in range(8):
+    SCRATCH["ps%d" % _b] = ("psum", [128, 512], "float32")
+PSUM = {"px0": (0, 0), "yd0": (0, 192), "x": (0, 0), "px1": (1, 0), "yd1": (1, 192), "yf": (1, 0), "xo": (1, 0),
+        "ev0": (2, 0), "f0": (2, 128), "col0": (2, 192), "ev1": (2, 208), "f1": (2, 336), "col1": (2, 400), "y": (2, 416),
+        "d": (3, 0), "so": (3, 256), "x0": (3, 0)}
 
-SEMAPHORES = (["cV", "cS", "cP", "cG", "lobs", "lcv", "lt0", "lt1", "sent", "ao1", "ao2", "ao3", "ahelp"]
-              + ["as%d_%d" % (t, s) for t in range(1, RO) for s in range(2)] + ["out%d" % k for k in range(3 * RO)])
-
-
-def bits(engines):
-    m = 0
-    for e in engines:
-        m |= 1 << e
-    return m
-
-
-def helper_of(core, T, topo):
-    for h in topo.cores_of(core):
-        if T.rank_of(h) is None and topo.die(h) == topo.die(core) and all(topo.may_write(h, d) for d in T.cores if d != core):
-            return h
-    raise ValueError("no helper")
-
-
-def helper_program(g, core, owner, T, topo):
-    n = len(T.cores); r = T.rank_of(owner)
-    far = topo.engines(owner, T.cores[(r + 1) % n])
-    g.wait_ge(T.sem.ahelp, len([e for e in topo.engines(owner, core) if e not in far]))
-    total = 0
-    for k in (2, 3):
-        dst = T.cores[(r + k) % n]; rid, pid, _ = topo.addr(dst)
-        g.remote_dma(T["obs%d" % k][:], T.obs3[:, 0:OBSW[k]], T.sem["ao%d" % k], T.sem.sent, pid, rid, topo.mask(core, dst))
-        total += len(topo.engines(core, dst))
-    g.wait_ge(T.sem.sent, total)
+SEMAPHORES = (["cV", "cS", "cP", "cG", "lob0", "lob1", "lcv", "sent"] + ["lt%d" % s for s in range(NS)]
+              + ["a%s%d_%d" % (k, t, s) for k in "cdy" for t in range(1, RO) for s in range(NS)] + ["ah1", "ah2"]
+              + ["out%d" % k for k in range(3 * RO)])
 
 
 def build_ops(g, core, T, topo, cost):
-    ops = []; tag = [None, 0]
-    CY, PCY, RG, CP, _, _, LAT_R = cost
+    ops = []; tag = [None, 0]; ext = {}; first = []
+    CY, PCY, RG, RS, _, _, LAT_R = cost
     V, S, P = g.vector, g.scalar, g.tensor
     n = len(T.cores); rank = T.rank_of(core)
     nxt = T.cores[(rank + 1) % n]; prv = T.cores[(rank - 1) % n]
+    nin = len(topo.engines(prv, core))
 
-    def op(eng, fn, rd, wr, dur, bank=None, sem=None, ext=None, lat=0.0):
-        ops.append({"eng": eng, "fn": fn, "rd": rd, "wr": wr, "dur": dur, "bank": bank, "sem": sem, "ext": ext, "lat": lat,
-                    "typ": (tag[0], len(ops) - tag[1])})
+    def op(eng, fn, rd, wr, dur, bank=None, sem=None, lat=0.0):
+        ops.append({"eng": eng, "fn": fn, "rd": rd, "wr": wr, "dur": dur, "bank": bank, "sem": sem, "lat": lat,
+                    "ext": [ext[r] for r in rd if r in ext], "typ": (tag[0], len(ops) - tag[1])})
 
-    def vd(x):
-        return 0.03 + max(64, x) * CY
+    def vd(x, gath=False):
+        return (0.05 if gath else 0.03) + max(64, x) * CY
 
-    def ts(out, in0, s1, s2, o0, o1, rd, wr, x, bank=None, ext=None):
+    def ts(out, in0, s1, s2, o0, o1, rd, wr, x, bank=None):
         if o1 is None:
-            op("V", lambda: V.tensor_scalar(out, in0, s1, None, o0), rd, wr, vd(x), bank, ext=ext)
+            op("V", lambda: V.tensor_scalar(out, in0, s1, None, o0), rd, wr, vd(x), bank)
         else:
-            op("V", lambda: V.tensor_scalar(out, in0, s1, s2, o0, o1), rd, wr, vd(x), bank, ext=ext)
+            op("V", lambda: V.tensor_scalar(out, in0, s1, s2, o0, o1), rd, wr, vd(x), bank)
 
-    def tt(out, in0, in1, o, rd, wr, x, bank=None):
-        op("V", lambda: V.tensor_tensor(out, in0, in1, o), rd, wr, vd(x), bank)
+    def tt(out, in0, in1, o, rd, wr, x, bank=None, gath=False):
+        op("V", lambda: V.tensor_tensor(out, in0, in1, o), rd, wr, vd(x, gath), bank)
 
-    def cp(out, in_, rd, wr, x, bank=None, ext=None):
-        op("V", lambda: V.tensor_copy(out, in_), rd, wr, vd(x), bank, ext=ext)
+    def cp(out, in_, rd, wr, x, bank=None, gath=False):
+        op("V", lambda: V.tensor_copy(out, in_), rd, wr, vd(x, gath), bank)
 
     def ms(ap, c, wr, x=64):
         op("V", lambda: V.memset(ap, c), [], wr, vd(x))
 
-    def sg(out, in_, rd, wr, x, ext=None):
-        op("S", lambda: S.activation(out, in_, ACT.Copy), rd, wr, 0.07 + x * RG * CY, ext=ext)
+    def sg(out, in_, rd, wr, x):
+        op("S", lambda: S.activation(out, in_, ACT.Copy), rd, wr, 0.065 + x * RG * CY)
+
+    def act(out, in_, func, bias, scale, rd, wr, x, bank=None):
+        op("S", lambda: S.activation(out, in_, func, bias=bias, scale=scale), rd, wr, 0.1 + max(64, x) * CY, bank)
 
     def io(name, out, pat, base, cm, x, flt=True):
         if flt:
@@ -119,13 +126,17 @@ def build_ops(g, core, T, topo, cost):
         else:
             op("G", lambda: g.iota(out, pat, base, cm), [], [name], 0.13 + 2 * x * CY)
 
-    def mm(lst, rd, bank, cyc):
+    def diag(name, src, cmp, fill):
+        op("G", lambda: g.affine_select(sq(name), sq(src), [[1, 128]], cmp, fill, 0, -1), [src], [name], 0.17 + 256 * CY)
+
+    def mm(lst, rd, bank, first=True, last=True):
         def fn():
-            last = None
-            for (o, l, r, a, b) in lst:
-                last = P.matmul(o, l, r, a, b)
-            return last
-        op("P", fn, rd, [], 0.05 + cyc * PCY, bank)
+            ins = None
+            for grp in lst:
+                for k, (o, l, r, _) in enumerate(grp):
+                    ins = P.matmul(o, l, r, first and k == 0, last and k == len(grp) - 1)
+            return ins
+        op("P", fn, rd, [], 0.03 + sum(max(64, x[3]) for grp in lst for x in grp) * PCY, bank)
 
     def dma(eng, pairs, rd, wr, sem, lat):
         q = {"Y": g.sync, "S": g.scalar}[eng]
@@ -133,194 +144,367 @@ def build_ops(g, core, T, topo, cost):
         def fn():
             for (o, i) in pairs:
                 q.dma_start(o, i).then_inc(T.sem[sem], 16)
-        op(eng, fn, rd, wr, 0.06 * len(pairs), sem=(sem, 16 * len(pairs)), lat=lat)
+        op(eng, fn, rd, wr, 0.06 * len(pairs), bank="queue" + eng, sem=(sem, 16 * len(pairs)), lat=lat)
 
-    def rdma(out, in_, sem, dst, engines, rd, wr, lat):
-        rid, pid, _ = topo.addr(dst)
-        op("G", lambda: g.remote_dma(out, in_, T.sem[sem], T.sem.sent, pid, rid, bits(engines)), rd, wr, 0.3, sem=("sent", len(engines)), lat=lat)
+    def rdma(out, in_, sem, rd, wr, lat):
+        rid, pid, _ = topo.addr(nxt)
+        op("G", lambda: g.remote_dma(out, in_, T.sem[sem], T.sem.sent, pid, rid, topo.mask(core, nxt)), rd, wr, 0.3,
+           sem=("sent", len(topo.engines(core, nxt))), lat=lat)
+        ops[-1]["after"] = first[0:1]
+        first.append(len(ops) - 1)
+        for w in wr:
+            ext[w] = (sem, nin)
 
-    def esel(z, u):
-        return z[:, 15 - u:143 - u]
+    def zz(name):
+        k = ZS.index(name)
+        return T.zs[:, 144 * k:144 * k + 144]
 
-    def tpieces(s):
-        return [(T["tb_%d" % s][:, DUMP + NB * k:DUMP + NB * (k + 1)], T.tsee[:, NB * (2 * k + s):NB * (2 * k + s + 1)]) for k in range(4)]
-    dma("Y", [(T.obs0[:], T.obs[:])], [], ["obs0"], "lobs", 3.5)
-    dma("S", tpieces(0), [], ["tbl0"], "lt0", 8.0)
-    dma("Y", [(T.cv[:, 0:4096], T.cvec[:])], [], ["cvl"], "lcv", 9.5)
-    dma("Y", tpieces(1), ["cvl"], ["tbl1"], "lt1", 5.5)
-    far = topo.engines(core, nxt); hp = helper_of(core, T, topo)
-    near = [e for e in topo.engines(core, hp) if e not in far]
-    rdma(T.obs1[:], T.obs0[:, 0:OBSW[1]], "ao1", nxt, far, ["obs0", "cvl", "tbl0"], ["obs1"], 9.0)
-    rdma(T.obs3[:], T.obs0[:, 0:OBSW[3]], "ahelp", hp, near, ["obs0", "cvl", "tbl0", "o1sent"], ["obs2", "obs3"], 20.0)
-    nin = len(topo.engines(prv, core))
-    obs_ext = {1: ("ao1", nin)}
-    for k in (2, 3):
-        obs_ext[k] = ("ao%d" % k, len(topo.engines(helper_of(T.cores[(rank - k) % n], T, topo), core)))
+    def esel(name, u):
+        k = ZS.index(name)
+        return T.zs[:, 144 * k + 15 - u:144 * k + 143 - u]
 
-    pc = T.pcol
-    U, C8, HI, G16, U16, U2 = [pc[:, k:k + 1] for k in range(6)]
+    def sq(name, a=0, b=128, step=1):
+        k = SQ.index(name)
+        return T.sq[:, 128 * k + a:128 * k + b:step]
+
+    def mat(k):
+        return T.mats[:, 128 * k:128 * k + 128]
+
+    def psum(s, place):
+        b, c0 = PSUM[place]; b += 4 * s
+        return (lambda a, z, step=1: T["ps%d" % b][:, c0 + a:c0 + z:step]), "ps%d" % b
+
+    def tload(eng, s, rd, lat):
+        dma(eng, [(T["tb_%d" % s][:, TW * k:TW * k + NB], T.tsee[:, NB * (NS * k + s):NB * (NS * k + s + 1)]) for k in range(NH)],
+            rd, ["tb%d" % s], "lt%d" % s, lat)
+    dma("Y", [(T.ob[:, 0:1024], T.obs[:, 0:1024])], [], ["ob0"], "lob0", 2.8)
+    dma("Y", [(T.ob[:, 1024:2048], T.obs[:, 1024:2048])], [], ["ob1"], "lob1", 3.8)
+    tload("S", 0, [], 8.0)
+    dma("Y", [(T.cv[:, 0:4096], T.cvec[:])], [], ["cvl"], "lcv", 9.0)
+    tload("Y", 1, ["cvl"], 4.5)
+
+    pc = T.pc
+    U, K4, G16, ODD = [pc[:, k:k + 1] for k in range(4)]
+    col = {}
+
+    def pcol(name, in0, s1, s2, o0, o1, rd):
+        col[name] = pc[:, 4 + len(col):5 + len(col)]
+        ts(col[name], in0, s1, s2, o0, o1, ["pc"] + rd, [name], 1)
+        return col[name]
     io("pidx", T.pidx[:, 0:1], [[0, 1]], 0, 1, 1, False)
-    for k, a in enumerate((15, 7, 8, 112)):
+    for k, a in enumerate((15, 3, 112, 1)):
         ts(T.pand[:, k:k + 1], T.pidx[:, 0:1], a, None, ALU.bitwise_and, None, ["pidx"], ["pand%d" % k], 1)
     cp(pc[:, 0:4], T.pand[:, 0:4], ["pand%d" % k for k in range(4)], ["pc"], 4)
-    ts(U16, U, 16.0, None, ALU.mult, None, ["pc"], ["u16"], 1)
-    ts(U2, U, 2.0, None, ALU.mult, None, ["pc"], ["u2"], 1)
-    for s in range(2):
-        il0, st = T["il0_%d" % s], T["st_%d" % s]
-        io("il0%d" % s, il0[:], [[256, 8], [2, 8]], s, 0, 64)
-        ts(st[:, 0:40], il0[:, 0:40], U16, None, ALU.add, None, ["il0%d" % s, "u16"], ["st%d_0" % s, "stn%d_0" % s], 40)
-        for t in range(1, RO - 1):
-            ts(st[:, 40 * t + 32:40 * t + 40], il0[:, 8 * (t + 4):8 * (t + 5)], U16, None, ALU.add, None, ["il0%d" % s, "u16"], ["stn%d_%d" % (s, t)], 8)
-        ms(T["tb_%d" % s][:, 0:DUMP], 0, ["tbd%d" % s], 128)
-    ms(T.cv[:, 4096:4112], 0.0, ["cvz"])
+
+    def scol(name, in_, scale, bias, rd):
+        return pcol(name, in_, scale, bias, ALU.mult, ALU.add, rd)
+    U16 = pcol("u16", U, 16.0, None, ALU.mult, None, [])
+    io("il0", T.il0[:], [[1, NS], [256, 8], [NS, NC]], 0, 0, 128)
+    ts(T.il[:], T.il0[:], U16, None, ALU.add, None, ["il0", "u16"], ["il"], 128)
     io("xr", T.xr[:], [[1, 144]], -15, 0, 144)
-    for nm, w in (("z125", 0.125), ("z233", W), ("zneg", -2048.0), ("z32", 2.0 ** -12)):
-        ts(T[nm][:], T.xr[:], G16, w, ALU.is_equal, ALU.mult, ["xr", "pc"], [nm], 144)
+    io("cb", T.cb[:, 0:3 * HC], [[0, 3], [TW, NH]], 0, 0, 12)
+    io("one", sq("one"), [[0, 128]], 1, 0, 128)
+    ms(T.cf[:, 0:3 * HC], -0.4375, ["cf"])
+    ms(T.cv[:, 4096:4112], 0.0, ["cvz"])
+    diag("idb", "one", ALU.is_equal, 0.0)
     io("gr", T.gr[:], [[16, 8], [0, 16]], 0, 0, 128)
-    ts(T.bo233[:], T.gr[:], G16, -W, ALU.is_equal, ALU.mult, ["gr", "pc"], ["bo233"], 128)
-    ts(T.bo125[:], T.gr[:], G16, 0.125, ALU.is_equal, ALU.mult, ["gr", "pc"], ["bo125"], 128)
-    io("dr", T.dr[:], [[1, 128]], 0, -1, 128)
-    ts(T.idb[:], T.dr[:], 0.0, None, ALU.is_equal, None, ["dr"], ["idb"], 128)
-    ts(T.idf[:], T.dr[:], 0.0, None, ALU.is_equal, None, ["dr"], ["idf"], 128)
-    ts(T.tr1[:], T.dr[:], 0.0, -8.0, ALU.is_gt, ALU.mult, ["dr"], ["tr1"], 128)
-    tt(T.tr2[:], T.tr1[:], T.bo125[:], ALU.mult, ["tr1", "bo125"], ["tr2"], 128)
-    tt(T.tri[:], T.tr2[:], T.idb[:], ALU.add, ["tr2", "idb"], ["tri"], 128)
-    io("cl0", T.cl0[:], [[0, 8], [NB, 4]], DUMP, 0, 32)
-    ts(T.constl[:], T.cl0[:], -0.4375, None, ALU.add, None, ["cl0"], ["constl"], 32)
+    ts(zz("z1"), T.xr[:], G16, None, ALU.is_equal, None, ["xr", "pc"], ["z1"], 144)
+    ts(sq("bd"), T.gr[:], G16, None, ALU.is_equal, None, ["gr", "pc"], ["bd"], 128)
+    k0 = pcol("k0", K4, 0.0, 0.125, ALU.is_equal, ALU.mult, [])
+    e15 = pcol("e15", U, 15.0, None, ALU.is_equal, None, [])
+    io("tg", T.tg[:, 0:3], [[1, 3]], 3, 0, 3)
+    ts(T.pe[:, 0:3], T.tg[:, 0:3], U, e15, ALU.is_equal, ALU.subtract, ["tg", "pc", "e15"], ["wq0", "wq1", "wq2"], 3)
+    wq = [T.pe[:, q:q + 1] for q in range(3)]
+    wa1 = pcol("wa1", U, 0.0, -2.0, ALU.is_equal, ALU.mult, [])
+    wa = scol("wa", e15, -7.0 / 2048, wa1, ["e15", "wa1"])
+    if YF_ON == "S":
+        cx0 = pcol("cx0", U, 6.0, 8192.0, ALU.is_lt, ALU.mult, [])
+        cX = scol("cX", cx0, 1.0, -2048.0, ["cx0"])
+    else:
+        cX = scol("cX", e15, -8192.0, 6144.0, ["e15"])
+    for nm, w, rd in (("z125", 0.125, []), ("z233", W, []), ("zl", k0, ["k0"])):
+        act(zz(nm), zz("z1"), ACT.Identity, 0.0, w, ["z1"] + rd, [nm], 144)
+    sv = 1.0 if SIGN_ON == "S" else 2.0
+    for nm, src, w, rd in ([("bd233", "bd", -W, []), ("idn", "idb", -1.0, []), ("idk", "idb", 4096.0, []), ("id16", "idb", 16.0, []),
+                            ("bda", "bd", wa, ["wa"]), ("bdf", "bd", -1.0, []), ("bdk", "bd", -4096.0 * sv, [])]
+                           + [("bdq%d" % q, "bd233", wq[q], ["wq%d" % q]) for q in range(3)]):
+        act(sq(nm), sq(src), ACT.Identity, 0.0, w, [src] + rd, [nm], 128)
+    diag("tr", "bdk", ALU.is_gt, 0.0)
+    diag("tri", "tr", ALU.not_equal, 4096.0 * sv)
+    cF = scol("cF", U, -4096.0, 4096.0, [])
+    ms(T.gw0[:], 0.0, ["gw0"], 192)
+    for k, (q, rows, w) in enumerate(((0, slice(1, 3), 1), (0, slice(4, 6), 1), (1, slice(0, 4, 3), 1), (1, slice(2, 6, 3), -1),
+                                      (2, slice(0, 2), -1), (2, slice(3, 5), -1))):
+        io("gw0%d" % k, T.gw0[:, q, :, rows], [[0, 16]], w, 0, 16)
+        ops[-1]["rd"].append("gw0")
+    io("gw1", T.gw1[:], [[0, 8], [-2, 2], [0, 8]], 1, 0, 128)
+    io("gw1", T.gw1[:, :, 4:8], [[0, 32]], -1, 0, 32)
+    for q in range(3):
+        tt(T.gw[:, 128 * q:128 * q + 128], T.gw0[:, q], sq("bd"), ALU.mult, ["gw0%d" % (2 * q), "gw0%d" % (2 * q + 1), "bd"], ["gw%d_" % q], 128)
+    tt(sq("pfm"), T.gw1[:], sq("bd"), ALU.mult, ["gw1", "bd"], ["pfm"], 128)
+    io("cpg", sq("cpg"), [[16, 8], [1, 4], [0, 4]], -1, 0, 128)
+    kp2 = pcol("kp2", K4, 2.0, G16, ALU.min, ALU.add, [])
+    sg0 = scol("sg0", ODD, -8192.0 * sv, 4096.0 * sv, [])
+    sgn = pcol("sgn", U, 6.0, sg0, ALU.is_lt, ALU.mult, ["sg0"])
+    ts(sq("pg"), sq("cpg"), kp2, sgn, ALU.is_equal, ALU.mult, ["cpg", "kp2", "sgn"], ["pg"], 64)
+    kp = scol("kp", K4, 1.0, G16, [])
+    kq = T.tg[:, 4:5]
+    io("kq", kq, [[0, 1]], 0, 1, 1)
+
+    cd = T.codes; made = {"d": [], "s": [], "r": []}
+
+    def code(kind, out, pat, base, x, over=()):
+        made[kind].append("c%s%d" % (kind, len(made[kind])))
+        io(made[kind][-1], out, pat, base, 0, x)
+        ops[-1]["rd"] += list(over)
+    new = [4 * case + NEXT[case].index(4) for case in range(4)]
+    pairs = [slice(new[0], new[2] + 1, new[2] - new[0]), slice(new[1], new[3] + 1, new[3] - new[1])]
+    for case in range(4):
+        for b in range(3):
+            src = [source(case, PAIRS[3 * k + b]) for k in range(2)]
+            code("d", cd[:, MD + b, :, 4 * case:4 * case + 4], [[16, 8], [src[1] - src[0], 4]], src[0], 32)
+        code("s", cd[:, MS:MH, :, 4 * case:4 * case + 4], [[4, 3], [16, 8], [1, 4]], 2 + NEXT[case][0], 96)
+    code("s", cd[:, MH:RD], [[0, 768]], -1, 768)
+    for x in pairs:
+        code("s", cd[:, MS:MH, :, x], [[0, 48]], -1, 48, made["s"][0:4])
+        code("s", cd[:, MH:RD, :, x], [[1, 6], [16, 8], [0, 2]], 0, 96, made["s"][4:5])
+    code("r", cd[:, RD:RF], [[0, 384]], -1, 384)
+    for b in range(3):
+        code("r", cd[:, RD + b, :, b:6:3], [[16, 8], [1, 2]], 0, 16, made["r"][0:1])
+    io("cf2", cd[:, RF:NM], [[-4, 2], [16, 8], [1, 16]], -6, 0, 256)
+    for name, m0, m1, key, kn in (("d", MD, MS, kq, "kq"), ("s", MS, RD, kq, "kq"), ("r", RD, RF, kp, "kp")):
+        ts(T.mats[:, 128 * m0:128 * m1], cd[:, m0:m1], key, None, ALU.is_equal, None, made[name] + [kn], ["m" + name], 64 * (m1 - m0))
+    ts(T.rf[:], cd[:, RF:NM], kp, None, ALU.is_equal, None, ["cf2", "kp"], ["rf"], 256 if YF_ON == "S" else 128)
+    if OUT_ON == "S":
+        act(T.zf[:], zz("z1"), ACT.Identity, 0.0, 1.0, ["z1"], ["zf"], 144)
+    U2 = scol("u2", U, 2.0, 0.0, [])
     for h in range(2):
-        io("ci%d" % h, T.ci[:, 128 * h:128 * h + 128], [[1, 2], [0, 4], [2, 16]], -h, 0, 128)
-    io("cb", T.cb[:], [[0, 4], [NB, 4], [0, 16]], DUMP, 0, 256)
-    ts(T.ci[:], T.ci[:], U2, 8192.0, ALU.is_le, ALU.mult, ["ci0", "ci1", "u2"], ["ci0", "ci1"], 256)
-    ts(T.cb[:], T.cb[:], -0.4375, None, ALU.add, None, ["cb"], ["cb"], 256)
-    tt(T.consth[:], T.ci[:], T.cb[:], ALU.add, ["ci0", "ci1", "cb"], ["consth"], 512)
-    io("jl0", T.jl0[:], [[16, 8]], 0, 0, 8)
-    ts(T.jl[:], T.jl0[:], U, None, ALU.add, None, ["jl0", "pc"], ["jl"], 8)
-    io("tie", T.tie[:, 0:96], [[4096, 3], [0, 32]], 4096, 0, 96)
-    ms(T.tie[:, 96:128], 0.0, ["tie2"])
-    io("mr0", T.mr0[:], [[8, 4], [0, 2]], 0, 0, 8)
-    ts(T.mrep[:], T.mr0[:], C8, None, ALU.add, None, ["mr0", "pc"], ["mrep"], 8)
-    io("kr0", T.kr0[:], [[4, 2], [0, 2], [1, 4]], 0, 0, 16)
-    cp(T.krep[:], T.kr0[:], ["kr0"], ["krep"], 16)
-    src = [[0, 1, 2, 4], [0, 1, 4, 3], [0, 4, 2, 3], [1, 2, 3, 4]]
-    for k in range(4):
-        lo0, lo1 = src[k][0], src[k][2]
-        io("clo%d" % k, T.clo[:, 2 * k:2 * k + 2], [[8 * (lo1 - lo0), 2]], 8 * lo0, 0, 2)
-        d0, d1 = src[k][1] - lo0, src[k][3] - lo1
-        io("cdl%d" % k, T.cdl[:, 2 * k:2 * k + 2], [[d1 - d0, 2]], d0, 0, 2)
-    ts(T.cd2[:], T.cdl[:], HI, C8, ALU.mult, ALU.add, ["cdl%d" % k for k in range(4)] + ["pc"], ["cd2"], 8)
-    tt(T.cd3[:], T.cd2[:], T.clo[:], ALU.add, ["cd2"] + ["clo%d" % k for k in range(4)], ["cd3"], 8)
-    cp(T.coff[:], T.cd3[:], ["cd3"], ["coff"], 8)
+        io("ci%d" % h, T.ci[:, NL * h:NL * h + NL], [[-1, 2], [0, NH], [2, 16]], h, 0, NL)
+    io("hb", T.hb[:], [[0, 4], [-8192, NH], [0, 16]], -8192, 0, 2 * NL)
+    ts(T.ci[:], T.ci[:], U2, -1.0, ALU.subtract, ALU.max, ["ci0", "ci1", "u2"], ["ci0", "ci1"], NL)
+    ts(T.ci[:], T.ci[:], 1.0, -8192.0, ALU.min, ALU.mult, ["ci0", "ci1"], ["ci0", "ci1"], NL)
+    tt(T.mask[:], T.ci[:], T.hb[:], ALU.add, ["ci0", "ci1", "hb"], ["mask"], 2 * NL)
+    io("jl0", T.jl0[:], [[0, 2], [16, 2], [TW, NH]], 464 - 2048, 0, 16)
+    act(T.jl[:], T.jl0[:], ACT.Identity, U, 1.0, ["jl0", "pc"], ["jl"], 16)
+
+    def columns(s, a, z, src, rd, add, out, wr):
+        ps, bank = psum(s, "col%d" % a); o = ps(0, 3 * HC)
+        mm([[(o, sq("idb"), T.cb[:, 0:3 * HC], 12), (o, sq("idb"), T.cf[:, 0:3 * HC], 12)]
+            + [(o, esel(z, u), src(u), 12) for u in range(16)]], rd + [z, "idb", "cb", "cf"], bank)
+        ts(out, o, M23 + add, M23, ALU.add, ALU.subtract, [], [wr], 12, bank)
+
+    dp = T.dp
+    for s in range(NS):
+        for h in range(2):
+            sg(T.ovf[:, 512 * h:512 * h + 512] if s == 0 else T.ovg[:, 512 * h:512 * h + 512],
+               T.ob[:, 0:1024 * (h + 1)].indirect(T.il[:, 64 * s + 32 * h:64 * s + 32 * h + 32]), ["il", "ob0", "ob%d" % h], ["ov%d%d" % (s, h)], 512)
+    at = {}
+    for j0, d, cnt, x in [(0, 1, 3, 0), (0, 2, 2, 4), (0, 3, 1, 8), (3, 1, 4, 9), (2, 2, 4, 13), (1, 3, 4, 17), (0, 4, 4, 21), (0, 5, 3, 25), (0, 6, 2, 6), (0, 7, 1, 3)]:
+        for s, ov in enumerate((T.ovf, T.ovg)):
+            tt(dp[:, x:x + cnt, NL * s:NL * s + NL], ov[:, NL * j0:NL * (j0 + cnt)], ov[:, NL * (j0 + d):NL * (j0 + d + cnt)], ALU.mult,
+               ["ov%d0" % s] + (["ov%d1" % s] if j0 + d + cnt > 4 else []), ["dp%d_%d" % (x, s)], NL * cnt)
+        for k in range(cnt):
+            at[(j0 + k, j0 + k + d)] = (x + k, "dp%d_" % x)
+    ps, bank = psum(1, "px0")
+    mm([[(ps(0, 256), esel("z1", r), dp[:, at[pair][0], :], 256) for r, pair in enumerate(LATER)]],
+       ["z1"] + [at[pair][1] + str(s) for pair in LATER[0:3] for s in range(NS)], bank)
+    ts(T.hq[:, 0], ps(0, 256), -2048.0, None, ALU.add, None, [], ["h0"], 256, bank)
+    for t in range(2):
+        rdma(T.hq[:, t + 1], T.hq[:, t], "ah%d" % (t + 1), ["h%d" % t], ["h%d" % (t + 1)], LAT_R + 1.0)
+        ops[-1]["dur"] += FIRST_CALL * (1 - t)
+    rows = [list(enumerate(PAIRS)), []]
+    for j, (b, r0) in enumerate(STAR):
+        rows[b] += [(r0 + k, (k, 4 + j)) for k in range(4)]
+    for s in range(NS):
+        for a in range(2):
+            l0 = NL * s + HL * a
+            columns(s, a, "z125", lambda u: dp[:, 0:9:4, l0 + u:l0 + HL:16], ["dp%d_%d" % (x, s) for x in (0, 4, 8)], 0.0,
+                    T["coli_%d" % s][:, 0, a, 0:3 * HC], "col%d%d_0" % (s, a))
+        ps, bank = psum(s, "x0")
+        mm([[(ps(NL * b, NL * b + NL), esel("z1", r), dp[:, at[pair][0], NL * s:NL * s + NL], NL) for r, pair in rows[b]] for b in range(2)],
+           ["z1"] + sorted(set(x[1] + str(s) for x in at.values())), bank)
+        ts(T["xi_%d" % s][:, 0:2 * NL], ps(0, 2 * NL), -2048.0, None, ALU.add, None, [], ["x%d_0" % s, "q%d_0" % s], 2 * NL, bank)
 
     for t in range(RO):
         last = t == RO - 1
-        for s in range(2):
-            tag[0], tag[1] = (s, 0 if t == 0 else 2 if last else 1), len(ops)
+        for s in range(NS):
+            tag[0], tag[1] = (s, t), len(ops)
 
             def B(x):
                 return T["%s_%d" % (x, s)]
 
             def R(x):
                 return "%s%d" % (x, s)
-            tb = B("tb")[:]; tbr = [R("tb"), R("tbl"), R("tbd")]
-            st = B("st"); stn = "st%d_%d" % (s, t)
-            ext = ("as%d_%d" % (t, s), nin) if t else None
-            cp(B("st16")[:], st[:, 40 * t:40 * t + 32], [stn], [R("st16")], 32, ext=ext)
-            ob = t % n
-            win = T["obs%d" % ob][:, 0:(1024 if t == 0 else OBSW[ob])]
-            ov, dp = B("ov"), B("dp")
-            sg(ov[:], win.indirect(B("st16")[:]), [R("st16"), "obs%d" % ob], [R("ov")], 512, ext=obs_ext.get(ob))
-            tt(dp[:, 0:128], ov[:, 0:128], ov[:, 384:512], ALU.mult, [R("ov")], [R("dp0")], 128 * CP)
-            tt(dp[:, 128:384], ov[:, 0:256], ov[:, 256:512], ALU.mult, [R("ov")], [R("dp1")], 256 * CP)
-            tt(dp[:, 384:768], ov[:, 0:384], ov[:, 128:512], ALU.mult, [R("ov")], [R("dp2")], 384 * CP)
-            dpr = [R("dp0"), R("dp1"), R("dp2")]
-            p1, p2, p3, px = B("p1"), B("p2"), B("p3"), B("px")
-            mm([(p1[:, 0:32], esel(T.z125, u), dp[:, u:512:16], u == 0, u == 15) for u in range(16)], dpr + ["z125"], R("p1"), 1024)
-            tt(B("coll")[:], p1[:, 0:32], T.constl[:], ALU.add, ["constl"], [R("coll")], 32, R("p1"))
-            c16 = B("col16"); nm = B("nm16")
-            cp(c16[:], B("coll")[:], [R("coll")], [R("col16")], 32)
-            offs = [c16[:, 24:32], c16[:, 8:16], c16[:, 0:8]]
-            cp(nm[:, 0:128], tb.indirect(offs[0]), tbr + [R("col16")], [R("nma")], 128 * RG)
-            cp(nm[:, 128:384], tb.indirect(c16[:, 0:16]), tbr + [R("col16")], [R("nmb")], 256 * RG)
-            if not last:
-                tt(B("cand")[:], st[:, 40 * t:40 * t + 40].indirect(T.coff[:]), T.tie[:], ALU.add,
-                   [stn, "stn%d_%d" % (s, t), "coff", R("st16"), "tie", "tie2"], [R("cand")], 128 * RG)
-                mm([(p1[:, 128 + 128 * h:256 + 128 * h], T.bo125[:], dp[:, 384:512], True, True) for h in range(2)], dpr + ["bo125"], R("p1"), 256)
-                tt(B("colh")[:], p1[:, 128:384], T.consth[:], ALU.add, ["consth"], [R("colh")], 256, R("p1"))
-            cw = T.cv[:, 0:4112]; cvr = ["cvl", "cvz"]
-            dcol = [512, 256, 640]
-            for ch, (l0, l1) in enumerate(CHUNKS):
-                sl = slice(16 * l0, 16 * l1); ne = 16 * (l1 - l0)
-                oa, oc, obb = [nm[:, 128 * k + l0:128 * k + l1] for k in range(3)]
-                ga, gb, gc = B("ga")[:, sl], B("gb")[:, sl], B("gcc")[:, sl]
-                ra, rb, rc = R("ga%d" % ch), R("gb%d" % ch), R("gc%d" % ch)
-                sg(ga, cw.indirect(oa), cvr + [R("nma")], [ra], ne)
-                sg(gb, cw.indirect(obb), cvr + [R("nmb")], [rb], ne)
-                if C_PLAIN[ch]:
-                    sg(gc, cw.indirect(oc), cvr + [R("nmb")], [rc], ne)
-                for q in range(3):
-                    pr = B("pr%d" % q); rp = R("pr%d_%d" % (q, ch))
-                    in1, r1 = (gb, rb) if q == 2 else (ga, ra)
-                    if (AB_PLAIN if q == 0 else C_PLAIN)[ch]:
-                        in0, r0 = (gb, rb) if q == 0 else (gc, rc)
-                        tt(pr[:, sl], in0, in1, ALU.mult, [r0, r1], [rp], ne * CP)
-                    else:
-                        tt(pr[:, sl], cw.indirect(obb if q == 0 else oc), in1, ALU.mult, cvr + [R("nmb"), r1], [rp], ne * RG)
-                    o = px[:, 128 * q + l0:128 * q + l1]
-                    lst = [(o, T.bo233[:], dp[:, dcol[q] + l0:dcol[q] + l1], True, False)]
-                    lst += [(o, esel(T.z233, p), pr[:, 16 * l0 + p:16 * l1:16], False, p == 15) for p in range(16)]
-                    mm(lst, [rp, "bo233", "z233"] + dpr, R("px"), 17 * max(64, l1 - l0))
-            fl = B("fl"); kt = B("kt"); first = B("first")
 
-            def act(out, in_, scale, bias, rd, wr, bank):
-                op("S", lambda: S.activation(out, in_, ACT.Relu, bias=bias, scale=scale), rd, wr, 0.07 + 128 * CY, bank)
-            ts(fl[:, 0:384], px[:, 0:384], MAGIC, MAGIC, ALU.add, ALU.is_equal, [], [R("fl")], 384, R("px"))
-            mm([(p2[:, 0:128], T.idb[:], fl[:, 128 * q:128 * q + 128], q == 0, q == 2) for q in range(3)], [R("fl"), "idb"], R("p2"), 384)
-            if EV_ON == "V":
-                ts(fl[:, 384:512], p2[:, 0:128], 3.0, 32.0, ALU.is_equal, ALU.mult, [], [R("ev")], 128, R("p2"))
-            else:
-                act(fl[:, 384:512], p2[:, 0:128], 32.0, -64.0, [], [R("ev")], R("p2"))
-            if last:
-                mm([(p2[:, 280:288], esel(T.z125, u), fl[:, 384 + u:512:16], u == 0, u == 15) for u in range(16)], [R("ev"), "z125"], R("p2"), 1024)
-            else:
-                mm([(p2[:, 256:288], esel(T.z125, u), fl[:, u:512:16], u == 0, u == 15) for u in range(16)], [R("fl"), R("ev"), "z125"], R("p2"), 1024)
-            mm([(p3[:, 128:256], T.tri[:], fl[:, 384:512], True, True)], [R("ev"), "tri"], R("p3"), 128)
-            k0 = 24 if last else 0
-            ts(kt[:, k0:32], p2[:, 256 + k0:288], 8.0 * 16384.0, None, ALU.mult, None, [], [R("kt")], 32, R("p2"))
-            if FIRST_ON == "V":
-                ts(first[:], p3[:, 128:256], 32.0, 4096.0, ALU.is_equal, ALU.mult, [], [R("first")], 128, R("p3"))
-            else:
-                act(first[:], p3[:, 128:256], 128.0, 0.0, [], [R("first")], R("p3"))
+            def both(x):
+                return [R(x + "0"), R(x + "1")]
+
+            def units(x, a, b):
+                return ["%s%d_%d" % (x, s, k) for k in range(a // 16, b // 16)]
+
+            def xin(a, b):
+                return B("xi")[:, XOFF[t] * NL + a:XOFF[t] * NL + b]
+            tb = B("tb")[:]
+            rx, rq = ["%s%d_%d" % (x, s, t) for x in ("x", "q")]; rh = "h%d" % t
+            rc = ["col%d%d_%d" % (s, a, t) for a in range(2)]
+            hq = T.hq[:, min(t, 2), NL * s:NL * s + NL]
+            nm, nmf, colf, f, y = B("nm16"), B("nmf"), B("colf"), B("f"), B("y")
+            wf = 3 - t
+            pd, bdd = psum(s, "d"); pso, bso = psum(s, "so"); py, by = psum(s, "y"); pxx, bxx = psum(s, "x")
+            cw = T.cv[:, 0:4112]; cvr = ["cvl", "cvz"]
+            for a in range(2):
+                n0 = 3 * HL * a
+                if a < SPLIT_NM:
+                    cp(nm[:, n0:n0 + HL], tb.indirect(B("coli")[:, t, a, 0:HC]), [R("tb"), rc[a]], [R("nma%d" % a)], HL * RG, gath=True)
+                    cp(nm[:, n0 + HL:n0 + 3 * HL], tb.indirect(B("coli")[:, t, a, HC:3 * HC]), [R("tb"), rc[a]], [R("nmb%d" % a)], 2 * HL * RG, gath=True)
+                else:
+                    cp(nm[:, n0:n0 + 3 * HL], tb.indirect(B("coli")[:, t, a, 0:3 * HC]), [R("tb"), rc[a]], [R("nma%d" % a), R("nmb%d" % a)], 3 * HL * RG, gath=True)
+            ts(nmf[:], nm[:], -2048.0, None, ALU.add, None, both("nma") + both("nmb"), [R("nmf")], 3 * NL // 2)
             if not last:
-                cpr, c2, c3 = B("cp"), B("c2"), B("c3")
-                ns = B("ns")[:, 32 * t:32 * t + 32]
-                tt(cpr[:], kt[:].indirect(T.mrep[:]), B("cand")[:], ALU.add, [R("kt"), R("cand"), "mrep"], [R("cp")], 128 * RG)
-                tt(c2[:], cpr[:, 0:64], cpr[:, 64:128], ALU.max, [R("cp")], [R("c2")], 128)
-                tt(c3[:], c2[:, 0:32], c2[:, 32:64], ALU.max, [R("c2")], [R("c3")], 64)
-                ts(ns, c3[:], 4095, None, ALU.bitwise_and, None, [R("c3")], [R("ns%d" % t)], 32)
-                rdma(st[:, 40 * (t + 1):40 * (t + 1) + 32], ns, "as%d_%d" % (t + 1, s), nxt, far, [R("ns%d" % t)], ["st%d_%d" % (s, t + 1)], LAT_R)
-                key, eq = B("key"), B("eq")
-                tt(key[:], kt[:, 24:32], B("coll")[:, 24:32], ALU.min, [R("kt"), R("coll")], [R("key")], 16)
-                tt(eq[:], key[:].indirect(T.krep[:]), B("colh")[:], ALU.is_equal, [R("key"), R("colh"), "krep"], [R("eq")], 256 * RG)
-                lst = [(p3[:, 0:8], T.idf[:], key[:], True, False)]
-                lst += [(p3[:, 0:8], esel(T.zneg, u), eq[:, 128 * h + u:128 * h + 128:16], False, h == 1 and u == 15) for h in range(2) for u in range(16)]
-                mm(lst, [R("eq"), R("key"), "idf", "zneg"], R("p3"), 2300)
-                tt(B("so")[:], p3[:, 0:8], T.jl[:], ALU.max, ["jl"], [R("so")], 8, R("p3"))
-                cp(B("so16")[:], B("so")[:], [R("so")], [R("so16")], 8)
-                tt(B("ncol")[:], tb.indirect(offs[0]), first[:], ALU.max, tbr + [R("col16"), R("first")], [R("ncol")], 128 * RG)
-            mk = B("mk")
-            for m in range(3):
-                tt(mk[:, 128 * m:128 * m + 128], tb.indirect(offs[m]), first[:], ALU.mult, tbr + [R("col16"), R("first")], [R("mk%d" % m)], 128 * RG)
+                ca = B("coli")[:, t, :, 0:HC]
+                ts(colf[:, 0:NC], ca, -2048.0, None, ALU.add, None, rc, [R("colf")], 8)
+                dlst = [(pd(0, 2 * NL), sq("idb"), T.mask[:], 2 * NL)]
+                if DUP:
+                    ts(colf[:, NC:2 * NC], ca, -2048.0, None, ALU.add, None, rc, [R("colg")], 8)
+                    dlst += [(pd(u, 2 * NL, 16), sq("id16"), colf[:, 0:2 * NC], 8) for u in range(16)]
+                else:
+                    dlst += [(pd(NL * h + u, NL * h + NL, 16), sq("id16"), colf[:, 0:NC], 8) for h in range(2) for u in range(16)]
+                dlst += [(pd(NL * h + HL * c, NL * h + HL * c + HL), sq("bda"), xin(HL * h, HL * h + HL), HL) for h in range(2) for c in range(2)]
+                for k in range(0, len(dlst), 10):
+                    mm([dlst[k:k + 10]], [R("colf"), R("colg"), "idb", "mask", "id16"] + ([rx, "bda"] if k + 10 > len(dlst) - 4 else []), bdd, k == 0, False)
+
+            for a in range(2):
+                px, bx = psum(s, "px%d" % a); pe, be = psum(s, "ev%d" % a); pf, bf = psum(s, "f%d" % a); pyd, byd = psum(s, "yd%d" % a)
+                l0 = HL * a; l1 = l0 + HL; lm = l1 - FUSE[t][2 * s + a]
+
+                def piece(x, m, p, q):
+                    return B(x)[:, 16 * (NL * m + p):16 * (NL * m + q)]
+
+                def names(m, p, q):
+                    return cw.indirect(nm[:, 2 * l0 + HL * m + p:2 * l0 + HL * m + q])
+                for m in range(3):
+                    z = lm if m == 2 else l1
+                    for p in range(l0, z, GP):
+                        q = min(z, p + GP)
+                        sg(piece("gv", m, p, q), names(m, p, q), cvr + [R("nm%s%d" % ("ab"[m > 0], a))], units("g%d" % m, p, q), 16 * (q - p))
+                for e, (m0, m1) in enumerate(((0, 1), (0, 2), (1, 2))):
+                    z = lm if e else l1
+                    for p in range(z, l1, PP):
+                        q = min(l1, p + PP)
+                        tt(piece("pr", e, p, q), names(2, p, q), piece("gv", m0, p, q), ALU.mult, cvr + [R("nmb%d" % a)] + units("g%d" % m0, p, q),
+                           units("pr%d" % e, p, q), 16 * (q - p) * RG, gath=True)
+                    for p in range(l0, z, PP):
+                        q = min(z, p + PP)
+                        tt(piece("pr", e, p, q), piece("gv", m0, p, q), piece("gv", m1, p, q), ALU.mult,
+                           units("g%d" % m0, p, q) + units("g%d" % m1, p, q), units("pr%d" % e, p, q), 16 * (q - p))
+                    o = px(HL * e, HL * e + HL)
+                    mm([[(o, esel("z233", p), B("pr")[:, 16 * (NL * e + l0) + p:16 * (NL * e + l1):16], HL) for p in range(16)]],
+                       units("pr%d" % e, l0, l1) + ["z233"], bx, e == 0, e == 2)
+                    if e == 1:
+                        mm([[(px(HL * k, HL * k + HL), sq("bdq%d" % k), xin(l0, l1), HL) for k in range(3)]], ["bdq0", "bdq1", "bdq2", rx], bx, False, False)
+                nf = B("nf"); n0 = 3 * l0; rn, rv, rf = R("nf%d" % a), R("v%d" % a), R("f%d" % a)
+                if ABS_ON == "S":
+                    act(B("ab")[:, n0:n0 + 3 * HL], px(0, 3 * HL), ACT.Abs, 0.0, 1.0, [], [R("ab%d" % a)], 3 * HL, bx)
+                    ts(nf[:, n0:n0 + 3 * HL], B("ab")[:, n0:n0 + 3 * HL], 140.4 * W, None, ALU.is_gt, None, [R("ab%d" % a)], [rn], 3 * HL // 2)
+                else:
+                    ts(nf[:, n0:n0 + 3 * HL], px(0, 3 * HL), MAGIC, MAGIC, ALU.add, ALU.not_equal, [], [rn], 3 * HL, bx)
+                nfq = [nf[:, n0 + HL * k:n0 + HL * k + HL] for k in range(3)]
+                lst = [[(pe(0, HL), sq("idn"), nfq[k], HL) for k in range(3)]]
+                if not last:
+                    lst.append([(pe(HL, 2 * HL), T.gw[:, 128 * k:128 * k + 128], nfq[k], HL) for k in range(3)])
+                mm(lst, [rn, "idn", "gw0_", "gw1_", "gw2_"], be)
+                nv = HL if last else 2 * HL
+                v = B("v")[:, 2 * l0:2 * l0 + nv]
+                if SIGN_ON == "S":
+                    act(v, pe(0, nv), ACT.Sign, 0.5, 1.0, [], [rv], nv, be)
+                else:
+                    ts(v, pe(0, nv), 0.0, 0.5, ALU.is_ge, ALU.subtract, [], [rv], nv, be)
+                mm([[(pf(0, HL), sq("tri"), B("v")[:, 2 * l0:2 * l0 + HL], HL)]], [rv, "tri"], bf)
+                if FIRST_ON == "S":
+                    act(f[:, l0:l1], pf(0, HL), ACT.Relu, cF, 1.0, ["cF"], [rf], HL, bf)
+                else:
+                    ts(f[:, l0:l1], pf(0, HL), cF, 0.0, ALU.add, ALU.max, ["cF"], [rf], HL, bf)
+                if not last:
+                    lst = []
+                    for b in range(3):
+                        o = pyd(HL * b, HL * b + HL)
+                        lst.append([(o, mat(MD + b), xin(l0, l1), HL), (o, sq("pg"), B("v")[:, 2 * l0 + HL:2 * l0 + 2 * HL], HL), (o, sq("pfm"), f[:, l0:l1], HL)])
+                    mm(lst, [rx, "md", rv, rf, "pg", "pfm"], byd)
+                    ts(y[:, n0:n0 + 3 * HL], pyd(0, 3 * HL), -8192.0, -2048.0, ALU.add, ALU.max, [], [R("yd%d" % a)], 3 * HL, byd)
+                    co = B("colo")[:, t, a, 0:3 * HC]
+                    columns(s, a, "zl", lambda u: y[:, n0 + u:n0 + 3 * HL:16], [R("yd%d" % a)], 1024.0, co, R("co%d%d" % (a, t)))
+                    rdma(B("coli")[:, t + 1, a, 0:3 * HC], co, "a%s%d_%d" % ("cd"[a], t + 1, s), [R("co%d%d" % (a, t))],
+                         ["col%d%d_%d" % (s, a, t + 1)], LAT_R)
+
+            mm([[(pxx(NL * m, NL * m + NL), sq("idb"), f[:], NL)]
+                + [(pxx(NL * m + HL * a, NL * m + HL * a + HL), sq("idb"), nmf[:, HL * (3 * a + m):HL * (3 * a + m + 1)], HL) for a in range(2)]
+                for m in range(3)], [R("nmf"), "idb"] + both("f"), bxx)
             if not last:
-                cp(tb.indirect(B("so16")[:]), B("ncol")[:], [R("so16"), R("ncol"), R("tbl"), R("tbd")], [R("tb")], 128 * 3.8)
-            for k in range(4):
-                mm([(p3[:, 32:56], esel(T.z32, u), mk[:, u:384:16], u == 0, u == 15) for u in range(4 * k, 4 * k + 4)],
-                   [R("mk0"), R("mk1"), R("mk2"), "z32"], R("p3"), 1024)
-            ts(B("fm1")[:], kt[:, 24:32].indirect(T.mrep[:, 0:2]), 1.0, -1.0, ALU.min, ALU.add, [R("kt"), "mrep"], [R("fm1")], 64)
-            tt(T.ybuf[:, 48 * t + s:48 * t + 48:2], p3[:, 32:56], B("fm1")[:, 0:24], ALU.add, [R("fm1")], ["y%d_%d" % (t, s)], 24, R("p3"))
+                eq = B("eq"); so = B("so")
+                mm([[(pd(NL * h + HL * c, NL * h + HL * c + HL), sq("bdf"), f[:, HL * h:HL * h + HL], HL) for h in range(2) for c in range(2)]],
+                   both("f") + ["bdf"], bdd, False, True)
+                if EQ_ON == "V":
+                    ts(eq[:], pd(0, 2 * NL), M27 + 36864.0, M27, ALU.add, ALU.is_equal, [], [R("eq")], 2 * NL, bdd)
+                else:
+                    act(B("ae")[:], pd(0, 2 * NL), ACT.Abs, 36864.0, 1.0, [], [R("ae")], 2 * NL, bdd)
+                    if EQ_ON == "S":
+                        act(eq[:], B("ae")[:], ACT.Relu, 8.0, -1.0, [R("ae")], [R("eq")], 2 * NL)
+                    else:
+                        ts(eq[:], B("ae")[:], 8.0, None, ALU.is_lt, None, [R("ae")], [R("eq")], NL)
+                if DUP_SO:
+                    o = pso(0, 2 * NC)
+                    mm([[(o, sq("idk"), eq[:, u:2 * NL:16], 8) for u in range(16)]
+                        + [(pso(NC * h, NC * h + NC), sq("idb"), colf[:, 0:NC], 8) for h in range(2)]], [R("eq"), R("colf"), "idb", "idk"], bso)
+                    tt(so[:, 16:16 + 2 * NC], o, T.jl[:, 0:2 * NC], ALU.min, ["jl"], [R("sp")], 8, bso)
+                    tt(so[:, 0:NC], so[:, 16:16 + NC], so[:, 16 + NC:16 + 2 * NC], ALU.max, [R("sp")], [R("so")], 8)
+                else:
+                    o = pso(0, NC)
+                    mm([[(o, sq("idb"), colf[:, 0:NC], 8)] + [(o, sq("idk"), eq[:, NL * h + u:NL * h + NL:16], 8) for h in range(2) for u in range(16)]],
+                       [R("eq"), R("colf"), "idb", "idk"], bso)
+                    tt(so[:, 0:NC], o, T.jl[:, 0:NC], ALU.min, ["jl"], [R("so")], 8, bso)
+                ts(B("so16")[:, 0:NC], so[:, 0:NC], 2048.0, None, ALU.add, None, [R("so")], [R("so16")], 8)
+                ts(B("ncol")[:], pxx(0, NL), 2048.0, 4096.0, ALU.add, ALU.min, [], [R("ncol")], NL, bxx)
+                cp(tb.indirect(B("so16")[:, 0:NC]), B("ncol")[:], [R("so16"), R("ncol")], [R("tb")], NL * RS, gath=True)
+                pyf, byf = psum(s, "yf"); pxo, bxo = psum(s, "xo"); x1 = XOFF[t + 1] * NL; x2 = XOFF[t + 2] * NL
+                if wf:
+                    lst = []
+                    for j in range(wf):
+                        b, r0 = STAR[j + 1]; o = pyf(NL * j, NL * j + NL)
+                        lst.append([(o, mat(MS + (r0 - 2) // 4), xin(NL * b, NL * b + NL), NL), (o, mat(MH + LATER.index((t + 4, t + 5 + j))), hq, NL),
+                                    (o, sq("pfm"), f[:], NL)]
+                                   + [(pyf(NL * j + HL * a, NL * j + HL * a + HL), sq("pg"), B("v")[:, NL * a + HL:NL * a + NL], HL) for a in range(2)])
+                    mm(lst, [rx, rq, rh, "ms", "pg", "pfm"] + both("v") + both("f"), byf)
+                    if YF_ON == "S":
+                        act(B("yf")[:, 0:wf * NL], pyf(0, NL * wf), ACT.Relu, -6144.0, 1.0, [], [R("yf")], NL * wf, byf)
+                    else:
+                        ts(B("yf")[:, 0:wf * NL], pyf(0, NL * wf), -8192.0, -2048.0, ALU.add, ALU.max, [], [R("yf")], NL * wf, byf)
+                lst = [[], [], []]
+                for j in range(wf):
+                    b = STAR[j][0]; k = (STAR[j][1] - 6) // 4
+                    lst[2 * b].append((pxo(NL * b, NL * b + NL), T.rf[:, 128 * k:128 * k + 128], B("yf")[:, NL * j:NL * (j + 1)], (4 if YF_ON == "S" else 1) * NL))
+                for a in range(2):
+                    lst[0 if wf else a] += [(pxo(HL * a, HL * a + HL), mat(RD + b), y[:, HL * (3 * a + b):HL * (3 * a + b + 1)], HL) for b in range(3)]
+                mm([x for x in lst if x], both("yd") + [R("yf"), "mr", "rf"], bxo)
+                ts(B("xo")[:, x1:x2], pxo(0, x2 - x1), cX, None, ALU.add, None, ["cX"], [R("xo%d" % t)], x2 - x1, bxo)
+                rdma(B("xi")[:, x1:x2], B("xo")[:, x1:x2], "ay%d_%d" % (t + 1, s), [R("xo%d" % t)],
+                     ["x%d_%d" % (s, t + 1), "q%d_%d" % (s, t + 1)], LAT_R + 0.5)
+            ons = OUT_ON == "S" and not last
+            if ons:
+                act(T.mkf[:, :, s, :], pxx(0, 3 * NL), ACT.Relu, -6143.0, 1.0, [], [R("mk")], 3 * NL, bxx)
+            else:
+                ts(T.mk[:, :, s, :], pxx(0, 3 * NL), -8192.0, -4096.0, ALU.add, ALU.max, [], [R("mk")], 3 * NL, bxx)
+            if s == NS - 1:
+                o = py(0, 48); out = T.ybuf[:, 48 * t:48 * t + 48]
+                if ons:
+                    for k in range(4):
+                        mm([[(o, T.zf[:, 15 - u:143 - u], T.mkf[:, :, :, u], 256) for u in range(4 * k, 4 * k + 4)]], ["mk0", "mk1", "zf"], by, k == 0, k == 3)
+                    act(out, o, ACT.Identity, -1.0, 1.0, [], ["y%d" % t], 48, by)
+                else:
+                    mm([[(o, esel("z1", u), T.mk[:, :, :, u], 48) for u in range(16)]], ["mk0", "mk1", "z1"], by)
+                    ts(out, o, 63488.0, -1.0, ALU.add, ALU.max, [], ["y%d" % t], 48, by)
         for m in range(3):
             k = 3 * t + m
-            dma("S" if last and m == 1 else "Y", [(T.yn[:, 256 * k:256 * k + 256], T.ybuf[:, 16 * k:16 * k + 16])],
-                ["y%d_0" % t, "y%d_1" % t], [], "out%d" % k, 2.5)
+            dma("S" if last and m == 1 else "Y", [(T.yn[:, 256 * k:256 * k + 256], T.ybuf[:, 16 * k:16 * k + 16])], ["y%d" % t], [], "out%d" % k, 2.5)
     return ops
 
 
@@ -341,6 +525,8 @@ def find_deps(ops):
             if o["bank"] in bank:
                 d.setdefault(bank[o["bank"]], False)
             bank[o["bank"]] = i
+        for j in o.get("after", []):
+            d.setdefault(j, False)
         d.pop(i, None)
         deps.append(d)
         for r in o["rd"]:
@@ -355,47 +541,32 @@ def order_queues(variants, deps):
     eng = ["VSPGY".index(o["eng"]) for o in ops]
     tabs = []
     for v, c in zip(variants, COSTS):
-        pre = [[(j, v[j]["lat"] + c[4] if (eng[j] != eng[i] or v[j]["sem"]) else (c[5] if h and eng[i] != 2 else 0.0))
+        pre = [[(j, v[j]["lat"] + c[4] if (eng[j] != eng[i] or (h and v[j]["sem"])) else (c[5] if h and eng[i] != 2 else 0.0))
                 for j, h in deps[i].items()] for i in range(n)]
-        tabs.append(([o["dur"] for o in v], [o["lat"] for o in v], pre))
-    dur, lat, pre = tabs[0]
-    succ = [[] for _ in range(n)]
-    for i in range(n):
-        for j, gp in pre[i]:
-            succ[j].append((i, gp))
-    base = [0.0] * n
-    for i in range(n - 1, -1, -1):
-        base[i] = dur[i] + max([gp + base[k] for k, gp in succ[i]] + [lat[i]])
-
-    def schedule(prio, look):
-        left = [len(d) for d in deps]
-        ready = [0.0] * n; cand = [[] for _ in range(5)]; free = [0.0] * 5; order = []
+        suc = [[] for _ in range(n)]
         for i in range(n):
-            if not left[i]:
-                cand[eng[i]].append(i)
-        for _ in range(n):
-            bt, be = 1e30, 0
-            for e in range(5):
-                if cand[e]:
-                    t0 = max(free[e], min([ready[i] for i in cand[e]]))
-                    if t0 < bt:
-                        bt, be = t0, e
-            lim = bt + look; bi, bp = -1, -1e30
-            for i in cand[be]:
-                if ready[i] <= lim and prio[i] > bp:
-                    bi, bp = i, prio[i]
-            f = max(free[be], ready[bi]) + dur[bi]; free[be] = f
-            cand[be].remove(bi); order.append(bi)
-            for k, gp in succ[bi]:
-                if f + gp > ready[k]:
-                    ready[k] = f + gp
-                left[k] -= 1
-                if not left[k]:
-                    cand[eng[k]].append(k)
-        return order
+            for j, gp in pre[i]:
+                suc[j].append((i, gp))
+        tabs.append(([o["dur"] for o in v], [o["lat"] for o in v], pre, suc))
+
+    def place(seq, dur, edges, head):
+        fin = [0.0] * n; busy = [([], []) for _ in range(5)]
+        for i in seq:
+            t0 = head[i]
+            for j, gp in edges[i]:
+                if fin[j] + gp > t0:
+                    t0 = fin[j] + gp
+            st, en = busy[eng[i]]; d = dur[i]
+            k = len(st)
+            while k > 0 and en[k - 1] > t0:
+                k -= 1
+            while k < len(st) and t0 + d > st[k] + 1e-9:
+                t0 = max(t0, en[k]); k += 1
+            st.insert(k, t0); en.insert(k, t0 + d); fin[i] = t0 + d
+        return fin
 
     def replay(order, tab):
-        d, lt, pr = tab
+        d, lt, pr, _ = tab
         fin = [0.0] * n; free = [0.0] * 5
         for i in order:
             t0 = free[eng[i]]
@@ -405,41 +576,84 @@ def order_queues(variants, deps):
             fin[i] = free[eng[i]] = t0 + d[i]
         return fin, max(fin[i] + lt[i] for i in range(n))
 
-    kinds = sorted(set(o["typ"] for o in ops if o["typ"][0] is not None)); kid = {k: x for x, k in enumerate(kinds)}
-    of = [kid.get(o["typ"], -1) for o in ops]
+    def legal(key, edges, ahead):
+        key = list(key)
+        for i in (range(n) if ahead else range(n - 1, -1, -1)):
+            for j, _ in edges[i]:
+                if key[j] >= key[i]:
+                    key[i] = key[j] + 1e-6
+        return sorted(range(n), key=lambda i: key[i])
     rng = np.random.default_rng(SEED)
-
-    def score(shift, look):
-        order = schedule([base[i] + (shift[of[i]] if of[i] >= 0 else 0.0) for i in range(n)], look)
-        return sum(replay(order, tab)[1] for tab in tabs), order
+    scale = [w / c[0] / (1.0 + c[2]) for w, c in zip(WEIGHT, COSTS)]
+    zero = [0.0] * n
+    dur, lat, pre, suc = tabs[0]
     best = None
-    for lagv in (6.0, 9.0, 12.0, 15.0):
-        for look in (0.05, 0.15, 0.3):
-            shift = [-lagv * k[0][0] for k in kinds]
-            sc, order = score(shift, look)
-            if best is None or sc < best[0]:
-                best = (sc, order, shift, look)
-    cur = best
     for it in range(SEARCH):
-        shift = list(cur[2]); look = cur[3]
-        for x in rng.integers(0, len(kinds), int(rng.integers(1, 6))):
-            shift[int(x)] += float(rng.normal()) * 4.0
-        if rng.random() < 0.05:
-            look = float(rng.choice([0.05, 0.1, 0.15, 0.2, 0.3]))
-        sc, order = score(shift, look)
-        if sc < cur[0] + 1.5 * (1.0 - it / SEARCH) * rng.random():
-            cur = (sc, order, shift, look)
-            if sc < best[0]:
-                best = cur
-    return best[1], [replay(best[1], tab) for tab in tabs]
+        if it < 12:
+            key = [0.0 if o["typ"][0] is None else (6.0 + it) * (o["typ"][0][1] + o["typ"][0][0] / NS) + 0.01 * o["typ"][1] for o in ops]
+        else:
+            size = float(rng.choice([0.1, 0.4, 1.5]))
+            noise = rng.normal(size=n) * size * (rng.random(n) < float(rng.choice([0.02, 0.1, 0.5])))
+            key = [float(x) for x in np.array(best[2]) + noise]
+        fin = place(legal(key, pre, True), dur, pre, zero)
+        for _ in range(2):
+            back = place(legal([-x for x in fin], suc, False), dur, suc, lat)
+            fin = place(legal([-x for x in back], pre, True), dur, pre, zero)
+        start = [fin[i] - dur[i] for i in range(n)]
+        order = legal(start, pre, True)
+        sc = sum(replay(order, tab)[1] * w for tab, w in zip(tabs, scale))
+        if best is None or sc <= best[0]:
+            best = (sc, order, start)
+
+    def critical(order, tab, fin):
+        d, lt, pr, _ = tab
+        prev = {}; lastq = [-1] * 5
+        for i in order:
+            prev[i] = lastq[eng[i]]; lastq[eng[i]] = i
+        i = max(range(n), key=lambda x: fin[x] + lt[x]); arcs = []
+        while True:
+            t0 = fin[i] - d[i]; p = prev[i]
+            nx = [j for j, gp in pr[i] if abs(fin[j] + gp - t0) < 1e-9]
+            if p >= 0 and abs(fin[p] - t0) < 1e-9 and p not in deps[i] and (not nx or rng.random() < 0.5):
+                arcs.append((p, i)); i = p
+            elif nx:
+                i = nx[0]
+            elif p >= 0 and abs(fin[p] - t0) < 1e-9:
+                i = p
+            else:
+                return arcs
+
+    def swap(order, u, v):
+        pu, pv = order.index(u), order.index(v)
+        tied = {u}; tq = set(); ahead = []; behind = []
+        for x in order[pu + 1:pv]:
+            if eng[x] in tq or any(j in tied for j in deps[x]):
+                tied.add(x); tq.add(eng[x]); behind.append(x)
+            else:
+                ahead.append(x)
+        if any(j in tied for j in deps[v]):
+            return None
+        return order[:pu] + ahead + [v, u] + behind + order[pv + 1:]
+    cur = best[1]; res = [replay(cur, tab) for tab in tabs]; csc = best[0]; top = (csc, cur)
+    for it in range(SWAPS):
+        k = int(rng.integers(len(tabs)))
+        arcs = critical(cur, tabs[k], res[k][0])
+        if not arcs:
+            continue
+        new = swap(cur, *arcs[int(rng.integers(len(arcs)))])
+        if new is None:
+            continue
+        nres = [replay(new, tab) for tab in tabs]
+        sc = sum(r[1] * w for r, w in zip(nres, scale))
+        if sc <= csc + HEAT * (1.0 - it / SWAPS) * float(rng.exponential()) * scale[0]:
+            cur, res, csc = new, nres, sc
+            if sc < top[0]:
+                top = (sc, cur)
+    return top[1], [replay(top[1], tab) for tab in tabs]
 
 
 def rank_program(g, core, T, topo):
-    rank = T.rank_of(core)
-    if rank is None:
-        for c in T.cores:
-            if helper_of(c, T, topo) == core:
-                helper_program(g, core, c, T, topo)
+    if T.rank_of(core) is None:
         return
     variants = [build_ops(g, core, T, topo, c) for c in COSTS]
     ops = variants[0]
@@ -468,9 +682,7 @@ def rank_program(g, core, T, topo):
     done = set(); total = {}; waited = {}
     for i in order:
         o = ops[i]; e = o["eng"]; q = queue[e]
-        sems = [ops[j]["sem"] for j in deps[i] if ops[j]["sem"] and ops[j]["sem"][0] != "sent"]
-        if o["ext"]:
-            sems.append(o["ext"])
+        sems = [ops[j]["sem"] for j, hard in deps[i].items() if hard and ops[j]["sem"] and ops[j]["sem"][0] != "sent"] + o["ext"]
         for (nm, v) in sems:
             if (e, nm) not in done:
                 done.add((e, nm)); q.wait_ge(T.sem[nm], v); waited[nm] = v

@@ -15,25 +15,24 @@ XOFF = [0, 2, 4, 5, 6, 7]
 
 NS, NH, NC, NL = 2, 4, 8, 128
 HL, HC = 64, 4
-GP = 64
-PP = 64
 SPLIT_NM = 0
-FUSE = [[0, 0, 0, 0]] * 5
-ABS_ON = "V"
-SIGN_ON = "S"
-FIRST_ON = "V"
+SQUARED = []
+PLAIN = ([("S", 0, 64), ("S", 64, 128), ("S", 128, 192)], [(0, 64)])
+PLAN = {(4, 3): ([("S", 0, 64), ("S", 64, 128), ("V", 128, 160), ("S", 160, 192)], [(0, 32), (32, 64)])}
+ON_S = {"abs": [], "first": [], "eq": [], "out": [], "yf": []}
+SIGN_ON = "SS"
 DUP = True
 DUP_SO = True
-EQ_ON = "V"
-OUT_ON = "V"
-YF_ON = "V"
-FIRST_CALL = 10.0
-COSTS = [(0.00090, 0.00050, 1.35, 3.8, 0.2, 0.12, 4.5), (0.00087, 0.00044, 1.56, 3.8, 0.1, 0.06, 3.0), (0.00085, 0.00045, 1.1, 2.0, 0.15, 0.1, 3.5), (0.0011, 0.00055, 1.95, 5.0, 0.1, 0.06, 3.0)]
-WEIGHT = [1.0, 1.0, 1.5, 0.7]
-SEARCH = 1500
+FIRST_CALL = 6.0
+FIRST_HOLD = 7.0
+SPREAD = 1
+COSTS = [(0.00088, 0.00047, 1.55, 3.8, 0.2, 0.12, 4.5), (0.00087, 0.00044, 1.56, 3.8, 0.1, 0.06, 3.0), (0.00085, 0.00045, 1.1, 2.0, 0.15, 0.1, 3.5), (0.0011, 0.00055, 1.95, 5.0, 0.1, 0.06, 3.0)]
+WEIGHT = [1, 1, 2.5, 0.8]
+SEARCH = 1800
 SEED = 1
-SWAPS = 12000
-HEAT = 0.1
+SWAPS = 25000
+HEAT = 0.3
+STEPS = [0, 0, 1, 2, 3, 5]
 ORDER = {}
 
 
@@ -50,9 +49,9 @@ SCRATCH = {
     "ybuf": ("sbuf", [128, 48 * RO], "float32"), "tg": ("sbuf", [128, 8], "float32"), "pe": ("sbuf", [128, 8], "float32"),
     "pidx": ("sbuf", [128, 8], "int32"), "pand": ("sbuf", [128, 8], "int32"), "pc": ("sbuf", [128, 32], "float32"),
     "xr": ("sbuf", [128, 144], "float32"), "gr": ("sbuf", [128, 128], "float32"),
-    "zs": ("sbuf", [128, 4 * 144], "bfloat16"), "sq": ("sbuf", [128, 20 * 128], "bfloat16"),
+    "ovs": ("sbuf", [128, 2, 1024], "bfloat16"), "zs": ("sbuf", [128, 6 * 144], "bfloat16"), "sq": ("sbuf", [128, 21 * 128], "bfloat16"),
     "gw0": ("sbuf", [128, 3, 8, 16], "bfloat16"), "gw1": ("sbuf", [128, 8, 16], "bfloat16"),
-    "gw": ("sbuf", [128, 384], "bfloat16"), "rf": ("sbuf", [128, 256], "float32" if YF_ON == "S" else "bfloat16"),
+    "gw": ("sbuf", [128, 384], "bfloat16"), "rf": ("sbuf", [128, 256], "bfloat16"), "rff": ("sbuf", [128, 256], "float32"),
     "zf": ("sbuf", [128, 144], "float32"), "mkf": ("sbuf", [128, 24, 2, 16], "float32"), "mk": ("sbuf", [128, 24, 2, 16], "float16"),
     "hq": ("sbuf", [128, 3, 256], "float16"), "codes": ("sbuf", [128, NM, 8, 16], "bfloat16"), "mats": ("sbuf", [128, 128 * NM], "bfloat16"),
     "ci": ("sbuf", [128, 256], "bfloat16"), "hb": ("sbuf", [128, 256], "bfloat16"), "mask": ("sbuf", [128, 256], "bfloat16"),
@@ -60,14 +59,14 @@ SCRATCH = {
     "jl0": ("sbuf", [128, 16], "float32"), "jl": ("sbuf", [128, 16], "float32"),
     "il0": ("sbuf", [128, 128], "float32"), "il": ("sbuf", [128, 128], "uint16"),
 }
-ZS = ["z1", "z125", "z233", "zl"]
-SQ = ["one", "idb", "idn", "idk", "id16", "bd", "bd233", "bdq0", "bdq1", "bdq2", "bda", "bdf", "bdk", "tr", "tri", "pfm", "cpg", "pg", "zero"]
+ZS = ["z1", "z125", "z233", "zl", "zp", "zn"]
+SQ = ["one", "idb", "idn", "idk", "id16", "bd", "bd233", "bdq0", "bdq1", "bdq2", "bda", "bdf", "bdk", "tr", "tri", "pfm", "cpg", "pg", "pg2", "tri2"]
 for _s in range(NS):
     for _n, _w, _d in (("tb", [NH * TW], "int32"),
                        ("xi", [XOFF[RO] * NL], "float16"), ("xo", [XOFF[RO] * NL], "float16"),
-                       ("y", [3 * NL], "float16"), ("yf", [3 * NL], "float32" if YF_ON == "S" else "float16"),
+                       ("y", [3 * NL], "float16"), ("yf", [3 * NL], "float16"), ("yff", [3 * NL], "float32"),
                        ("coli", [RO, 2, 16], "uint16"), ("colo", [RO, 2, 16], "uint16"), ("colf", [16], "float16"),
-                       ("nm16", [3 * NL], "uint16"), ("nmf", [3 * NL], "float16"),
+                       ("nm16", [3 * NL], "uint16"), ("nmf", [2, 3, HL], "float16"),
                        ("gv", [48 * NL], "bfloat16"), ("pr", [48 * NL], "bfloat16"),
                        ("ab", [3 * NL], "bfloat16"), ("nf", [3 * NL], "bfloat16"), ("v", [2 * NL], "bfloat16"), ("f", [NL], "bfloat16"),
                        ("ae", [2 * NL], "bfloat16"), ("eq", [2 * NL], "bfloat16"), ("so", [32], "float32"), ("so16", [8], "uint16"),
@@ -90,14 +89,13 @@ def build_ops(g, core, T, topo, cost):
     V, S, P = g.vector, g.scalar, g.tensor
     n = len(T.cores); rank = T.rank_of(core)
     nxt = T.cores[(rank + 1) % n]; prv = T.cores[(rank - 1) % n]
-    nin = len(topo.engines(prv, core))
 
     def op(eng, fn, rd, wr, dur, bank=None, sem=None, lat=0.0):
         ops.append({"eng": eng, "fn": fn, "rd": rd, "wr": wr, "dur": dur, "bank": bank, "sem": sem, "lat": lat,
                     "ext": [ext[r] for r in rd if r in ext], "typ": (tag[0], len(ops) - tag[1])})
 
     def vd(x, gath=False):
-        return (0.05 if gath else 0.03) + max(64, x) * CY
+        return (0.05 if gath else 0.015) + max(64, x) * CY
 
     def ts(out, in0, s1, s2, o0, o1, rd, wr, x, bank=None):
         if o1 is None:
@@ -146,14 +144,15 @@ def build_ops(g, core, T, topo, cost):
                 q.dma_start(o, i).then_inc(T.sem[sem], 16)
         op(eng, fn, rd, wr, 0.06 * len(pairs), bank="queue" + eng, sem=(sem, 16 * len(pairs)), lat=lat)
 
-    def rdma(out, in_, sem, rd, wr, lat):
+    def rdma(out, in_, sem, rd, wr, lat, cnt=None):
         rid, pid, _ = topo.addr(nxt)
-        op("G", lambda: g.remote_dma(out, in_, T.sem[sem], T.sem.sent, pid, rid, topo.mask(core, nxt)), rd, wr, 0.3,
-           sem=("sent", len(topo.engines(core, nxt))), lat=lat)
+        use = topo.engines(core, nxt)[::SPREAD][0:cnt]
+        op("G", lambda: g.remote_dma(out, in_, T.sem[sem], T.sem.sent, pid, rid, sum(1 << e for e in use)), rd, wr,
+           0.3, sem=("sent", len(use)), lat=lat)
         ops[-1]["after"] = first[0:1]
         first.append(len(ops) - 1)
         for w in wr:
-            ext[w] = (sem, nin)
+            ext[w] = (sem, len(topo.engines(prv, core)[::SPREAD][0:cnt]))
 
     def zz(name):
         k = ZS.index(name)
@@ -177,11 +176,11 @@ def build_ops(g, core, T, topo, cost):
     def tload(eng, s, rd, lat):
         dma(eng, [(T["tb_%d" % s][:, TW * k:TW * k + NB], T.tsee[:, NB * (NS * k + s):NB * (NS * k + s + 1)]) for k in range(NH)],
             rd, ["tb%d" % s], "lt%d" % s, lat)
-    dma("Y", [(T.ob[:, 0:1024], T.obs[:, 0:1024])], [], ["ob0"], "lob0", 2.8)
-    dma("Y", [(T.ob[:, 1024:2048], T.obs[:, 1024:2048])], [], ["ob1"], "lob1", 3.8)
-    tload("S", 0, [], 8.0)
-    dma("Y", [(T.cv[:, 0:4096], T.cvec[:])], [], ["cvl"], "lcv", 9.0)
-    tload("Y", 1, ["cvl"], 4.5)
+    dma("Y", [(T.ob[:, 0:1024], T.obs[:, 0:1024])], [], ["ob0"], "lob0", 2.0)
+    dma("Y", [(T.ob[:, 1024:2048], T.obs[:, 1024:2048])], [], ["ob1"], "lob1", 2.6)
+    tload("Y", 0, [], 4.6)
+    dma("Y", [(T.cv[:, 0:4096], T.cvec[:])], [], ["cvl"], "lcv", 6.8)
+    tload("Y", 1, [], 8.8)
 
     pc = T.pc
     U, K4, G16, ODD = [pc[:, k:k + 1] for k in range(4)]
@@ -197,41 +196,49 @@ def build_ops(g, core, T, topo, cost):
     cp(pc[:, 0:4], T.pand[:, 0:4], ["pand%d" % k for k in range(4)], ["pc"], 4)
 
     def scol(name, in_, scale, bias, rd):
-        return pcol(name, in_, scale, bias, ALU.mult, ALU.add, rd)
+        col[name] = pc[:, 4 + len(col):5 + len(col)]
+        act(col[name], in_, ACT.Identity, bias, scale, ["pc"] + rd, [name], 1)
+        return col[name]
     U16 = pcol("u16", U, 16.0, None, ALU.mult, None, [])
     io("il0", T.il0[:], [[1, NS], [256, 8], [NS, NC]], 0, 0, 128)
     ts(T.il[:], T.il0[:], U16, None, ALU.add, None, ["il0", "u16"], ["il"], 128)
     io("xr", T.xr[:], [[1, 144]], -15, 0, 144)
     io("cb", T.cb[:, 0:3 * HC], [[0, 3], [TW, NH]], 0, 0, 12)
-    io("one", sq("one"), [[0, 128]], 1, 0, 128)
+    kq = T.tg[:, 4:5]
+    io("kq", kq, [[0, 1]], 0, 1, 1)
     ms(T.cf[:, 0:3 * HC], -0.4375, ["cf"])
     ms(T.cv[:, 4096:4112], 0.0, ["cvz"])
-    diag("idb", "one", ALU.is_equal, 0.0)
+    ts(sq("idb"), T.xr[:, 15:143], kq, None, ALU.is_equal, None, ["xr", "kq"], ["idb"], 128)
     io("gr", T.gr[:], [[16, 8], [0, 16]], 0, 0, 128)
     ts(zz("z1"), T.xr[:], G16, None, ALU.is_equal, None, ["xr", "pc"], ["z1"], 144)
     ts(sq("bd"), T.gr[:], G16, None, ALU.is_equal, None, ["gr", "pc"], ["bd"], 128)
-    k0 = pcol("k0", K4, 0.0, 0.125, ALU.is_equal, ALU.mult, [])
+    k2 = pcol("k2", K4, 2.0, 0.4375 / 8192, ALU.is_equal, ALU.mult, [])
+    k1 = pcol("k1", K4, 0.0, None, ALU.is_equal, None, [])
+    k0 = scol("k0", k1, 0.125, k2, ["k1", "k2"])
     e15 = pcol("e15", U, 15.0, None, ALU.is_equal, None, [])
     io("tg", T.tg[:, 0:3], [[1, 3]], 3, 0, 3)
     ts(T.pe[:, 0:3], T.tg[:, 0:3], U, e15, ALU.is_equal, ALU.subtract, ["tg", "pc", "e15"], ["wq0", "wq1", "wq2"], 3)
     wq = [T.pe[:, q:q + 1] for q in range(3)]
     wa1 = pcol("wa1", U, 0.0, -2.0, ALU.is_equal, ALU.mult, [])
     wa = scol("wa", e15, -7.0 / 2048, wa1, ["e15", "wa1"])
-    if YF_ON == "S":
+    cX = scol("cX", e15, -8192.0, 6144.0, ["e15"])
+    if ON_S["yf"]:
         cx0 = pcol("cx0", U, 6.0, 8192.0, ALU.is_lt, ALU.mult, [])
-        cX = scol("cX", cx0, 1.0, -2048.0, ["cx0"])
-    else:
-        cX = scol("cX", e15, -8192.0, 6144.0, ["e15"])
+        cXs = scol("cXs", cx0, 1.0, -2048.0, ["cx0"])
     for nm, w, rd in (("z125", 0.125, []), ("z233", W, []), ("zl", k0, ["k0"])):
         act(zz(nm), zz("z1"), ACT.Identity, 0.0, w, ["z1"] + rd, [nm], 144)
-    sv = 1.0 if SIGN_ON == "S" else 2.0
+    sv = 1.0
     for nm, src, w, rd in ([("bd233", "bd", -W, []), ("idn", "idb", -1.0, []), ("idk", "idb", 4096.0, []), ("id16", "idb", 16.0, []),
-                            ("bda", "bd", wa, ["wa"]), ("bdf", "bd", -1.0, []), ("bdk", "bd", -4096.0 * sv, [])]
+                            ("bda", "bd", wa, ["wa"]), ("bdf", "bd", -1.0, [])]
                            + [("bdq%d" % q, "bd233", wq[q], ["wq%d" % q]) for q in range(3)]):
         act(sq(nm), sq(src), ACT.Identity, 0.0, w, [src] + rd, [nm], 128)
-    diag("tr", "bdk", ALU.is_gt, 0.0)
-    diag("tri", "tr", ALU.not_equal, 4096.0 * sv)
-    cF = scol("cF", U, -4096.0, 4096.0, [])
+    ts(sq("bdk"), T.xr[:, 15:143], kq, -4096.0, ALU.is_gt, ALU.mult, ["xr", "kq"], ["bdk"], 128)
+    tt(sq("tr"), sq("bdk"), sq("bd"), ALU.mult, ["bdk", "bd"], ["tr"], 128)
+    tt(sq("tri"), sq("tr"), sq("idk"), ALU.add, ["tr", "idk"], ["tri"], 128)
+    act(sq("tri2"), sq("tri"), ACT.Identity, 0.0, 2.0, ["tri"], ["tri2"], 128)
+    cF = pcol("cF", U, -4096.0, None, ALU.mult, None, [])
+    cy0 = pcol("cy0", U, 4.0, 131072.0, ALU.is_lt, ALU.mult, [])
+    cY = scol("cY", cy0, 1.0, -73728.0, ["cy0"])
     ms(T.gw0[:], 0.0, ["gw0"], 192)
     for k, (q, rows, w) in enumerate(((0, slice(1, 3), 1), (0, slice(4, 6), 1), (1, slice(0, 4, 3), 1), (1, slice(2, 6, 3), -1),
                                       (2, slice(0, 2), -1), (2, slice(3, 5), -1))):
@@ -247,9 +254,10 @@ def build_ops(g, core, T, topo, cost):
     sg0 = scol("sg0", ODD, -8192.0 * sv, 4096.0 * sv, [])
     sgn = pcol("sgn", U, 6.0, sg0, ALU.is_lt, ALU.mult, ["sg0"])
     ts(sq("pg"), sq("cpg"), kp2, sgn, ALU.is_equal, ALU.mult, ["cpg", "kp2", "sgn"], ["pg"], 64)
+    pgs = ["pg2" if x == "V" else "pg" for x in SIGN_ON]
+    if "pg2" in pgs:
+        act(sq("pg2"), sq("pg"), ACT.Identity, 0.0, 2.0, ["pg"], ["pg2"], 128)
     kp = scol("kp", K4, 1.0, G16, [])
-    kq = T.tg[:, 4:5]
-    io("kq", kq, [[0, 1]], 0, 1, 1)
 
     cd = T.codes; made = {"d": [], "s": [], "r": []}
 
@@ -264,18 +272,20 @@ def build_ops(g, core, T, topo, cost):
             src = [source(case, PAIRS[3 * k + b]) for k in range(2)]
             code("d", cd[:, MD + b, :, 4 * case:4 * case + 4], [[16, 8], [src[1] - src[0], 4]], src[0], 32)
         code("s", cd[:, MS:MH, :, 4 * case:4 * case + 4], [[4, 3], [16, 8], [1, 4]], 2 + NEXT[case][0], 96)
-    code("s", cd[:, MH:RD], [[0, 768]], -1, 768)
+    made["s"].append("cs4"); ms(cd[:, MH:RF], -1.0, ["cs4"], 576)
+    code("d", cd[:, MD:MS, :, 2:16:4], [[0, 3], [16, 8], [0, 4]], 15, 96, made["d"][0:12])
     for x in pairs:
         code("s", cd[:, MS:MH, :, x], [[0, 48]], -1, 48, made["s"][0:4])
         code("s", cd[:, MH:RD, :, x], [[1, 6], [16, 8], [0, 2]], 0, 96, made["s"][4:5])
-    code("r", cd[:, RD:RF], [[0, 384]], -1, 384)
     for b in range(3):
-        code("r", cd[:, RD + b, :, b:6:3], [[16, 8], [1, 2]], 0, 16, made["r"][0:1])
+        code("r", cd[:, RD + b, :, b:6:3], [[16, 8], [1, 2]], 0, 16, ["cs4"])
     io("cf2", cd[:, RF:NM], [[-4, 2], [16, 8], [1, 16]], -6, 0, 256)
     for name, m0, m1, key, kn in (("d", MD, MS, kq, "kq"), ("s", MS, RD, kq, "kq"), ("r", RD, RF, kp, "kp")):
         ts(T.mats[:, 128 * m0:128 * m1], cd[:, m0:m1], key, None, ALU.is_equal, None, made[name] + [kn], ["m" + name], 64 * (m1 - m0))
-    ts(T.rf[:], cd[:, RF:NM], kp, None, ALU.is_equal, None, ["cf2", "kp"], ["rf"], 256 if YF_ON == "S" else 128)
-    if OUT_ON == "S":
+    ts(T.rf[:], cd[:, RF:NM], kp, None, ALU.is_equal, None, ["cf2", "kp"], ["rf"], 128)
+    if ON_S["yf"]:
+        act(T.rff[:], T.rf[:], ACT.Identity, 0.0, 1.0, ["rf"], ["rff"], 256)
+    if ON_S["out"]:
         act(T.zf[:], zz("z1"), ACT.Identity, 0.0, 1.0, ["z1"], ["zf"], 144)
     U2 = scol("u2", U, 2.0, 0.0, [])
     for h in range(2):
@@ -289,7 +299,7 @@ def build_ops(g, core, T, topo, cost):
 
     def columns(s, a, z, src, rd, add, out, wr):
         ps, bank = psum(s, "col%d" % a); o = ps(0, 3 * HC)
-        mm([[(o, sq("idb"), T.cb[:, 0:3 * HC], 12), (o, sq("idb"), T.cf[:, 0:3 * HC], 12)]
+        mm([[(o, sq("idb"), T.cb[:, 0:3 * HC], 12)] + ([] if add else [(o, sq("idb"), T.cf[:, 0:3 * HC], 12)])
             + [(o, esel(z, u), src(u), 12) for u in range(16)]], rd + [z, "idb", "cb", "cf"], bank)
         ts(out, o, M23 + add, M23, ALU.add, ALU.subtract, [], [wr], 12, bank)
 
@@ -299,19 +309,36 @@ def build_ops(g, core, T, topo, cost):
             sg(T.ovf[:, 512 * h:512 * h + 512] if s == 0 else T.ovg[:, 512 * h:512 * h + 512],
                T.ob[:, 0:1024 * (h + 1)].indirect(T.il[:, 64 * s + 32 * h:64 * s + 32 * h + 32]), ["il", "ob0", "ob%d" % h], ["ov%d%d" % (s, h)], 512)
     at = {}
-    for j0, d, cnt, x in [(0, 1, 3, 0), (0, 2, 2, 4), (0, 3, 1, 8), (3, 1, 4, 9), (2, 2, 4, 13), (1, 3, 4, 17), (0, 4, 4, 21), (0, 5, 3, 25), (0, 6, 2, 6), (0, 7, 1, 3)]:
+    for j0, d, cnt, x in [(0, 1, 3, 0), (0, 2, 2, 4), (0, 3, 1, 8), (4, 1, 3, 10), (4, 2, 2, 15), (4, 3, 1, 20), (3, 1, 1, 9), (2, 2, 2, 13), (1, 3, 3, 17), (0, 4, 4, 21), (0, 5, 3, 25), (0, 6, 2, 6), (0, 7, 1, 3)]:
         for s, ov in enumerate((T.ovf, T.ovg)):
-            tt(dp[:, x:x + cnt, NL * s:NL * s + NL], ov[:, NL * j0:NL * (j0 + cnt)], ov[:, NL * (j0 + d):NL * (j0 + d + cnt)], ALU.mult,
-               ["ov%d0" % s] + (["ov%d1" % s] if j0 + d + cnt > 4 else []), ["dp%d_%d" % (x, s)], NL * cnt)
+            out = dp[:, x:x + cnt, NL * s:NL * s + NL]; in0 = ov[:, NL * j0:NL * (j0 + cnt)]; in1 = ov[:, NL * (j0 + d):NL * (j0 + d + cnt)]
+            rd = (["ov%d0" % s] if j0 < 4 else []) + (["ov%d1" % s] if j0 + d + cnt > 4 else [])
+            if d in SQUARED:
+                ps, bank = psum(s, "px1"); o = ps(0, NL * cnt)
+                mm([[(o, sq("idb"), in0, NL * cnt), (o, sq("idn"), in1, NL * cnt)]], rd + ["idb", "idn"], bank)
+                act(out, o, ACT.Square, 0.0, 1.0, [], ["dp%d_%d" % (x, s)], NL * cnt, bank)
+            else:
+                tt(out, in0, in1, ALU.mult, rd, ["dp%d_%d" % (x, s)], NL * cnt)
         for k in range(cnt):
             at[(j0 + k, j0 + k + d)] = (x + k, "dp%d_" % x)
+    if SQUARED:
+        for s, ov in enumerate((T.ovf, T.ovg)):
+            act(T.ovs[:, s], ov[:], ACT.Square, 0.0, 1.0, ["ov%d0" % s, "ov%d1" % s], ["ovs%d" % s], 1024)
+        for nm, w in (("zp", 0.5), ("zn", -0.5)):
+            act(zz(nm), zz("z1"), ACT.Identity, 0.0, w, ["z1"], [nm], 144)
+
+    def terms(o, r, pair, s):
+        src = dp[:, at[pair][0], NL * s:NL * s + NL]
+        if pair[1] - pair[0] not in SQUARED:
+            return [(o, esel("z1", r), src, NL)]
+        return [(o, esel("zn", r), src, NL)] + [(o, esel("zp", r), T.ovs[:, s, NL * j:NL * j + NL], NL) for j in pair]
     ps, bank = psum(1, "px0")
     mm([[(ps(0, 256), esel("z1", r), dp[:, at[pair][0], :], 256) for r, pair in enumerate(LATER)]],
        ["z1"] + [at[pair][1] + str(s) for pair in LATER[0:3] for s in range(NS)], bank)
     ts(T.hq[:, 0], ps(0, 256), -2048.0, None, ALU.add, None, [], ["h0"], 256, bank)
     for t in range(2):
-        rdma(T.hq[:, t + 1], T.hq[:, t], "ah%d" % (t + 1), ["h%d" % t], ["h%d" % (t + 1)], LAT_R + 1.0)
-        ops[-1]["dur"] += FIRST_CALL * (1 - t)
+        rdma(T.hq[:, t + 1], T.hq[:, t], "ah%d" % (t + 1), ["h%d" % t], ["h%d" % (t + 1)], LAT_R + 3.0)
+        ops[-1]["dur"] += FIRST_HOLD * (1 - t)
     rows = [list(enumerate(PAIRS)), []]
     for j, (b, r0) in enumerate(STAR):
         rows[b] += [(r0 + k, (k, 4 + j)) for k in range(4)]
@@ -321,8 +348,11 @@ def build_ops(g, core, T, topo, cost):
             columns(s, a, "z125", lambda u: dp[:, 0:9:4, l0 + u:l0 + HL:16], ["dp%d_%d" % (x, s) for x in (0, 4, 8)], 0.0,
                     T["coli_%d" % s][:, 0, a, 0:3 * HC], "col%d%d_0" % (s, a))
         ps, bank = psum(s, "x0")
-        mm([[(ps(NL * b, NL * b + NL), esel("z1", r), dp[:, at[pair][0], NL * s:NL * s + NL], NL) for r, pair in rows[b]] for b in range(2)],
-           ["z1"] + sorted(set(x[1] + str(s) for x in at.values())), bank)
+        for b in range(2):
+            for k in range(0, len(rows[b]), 4):
+                part = rows[b][k:k + 4]
+                mm([[x for r, pair in part for x in terms(ps(NL * b, NL * b + NL), r, pair, s)]],
+                   ["z1", "zp", "zn", "ovs%d" % s] + sorted(set(at[pair][1] + str(s) for _, pair in part)), bank, k == 0, k + 4 >= len(rows[b]))
         ts(T["xi_%d" % s][:, 0:2 * NL], ps(0, 2 * NL), -2048.0, None, ALU.add, None, [], ["x%d_0" % s, "q%d_0" % s], 2 * NL, bank)
 
     for t in range(RO):
@@ -375,35 +405,32 @@ def build_ops(g, core, T, topo, cost):
 
             for a in range(2):
                 px, bx = psum(s, "px%d" % a); pe, be = psum(s, "ev%d" % a); pf, bf = psum(s, "f%d" % a); pyd, byd = psum(s, "yd%d" % a)
-                l0 = HL * a; l1 = l0 + HL; lm = l1 - FUSE[t][2 * s + a]
+                l0 = HL * a; l1 = l0 + HL
 
-                def piece(x, m, p, q):
-                    return B(x)[:, 16 * (NL * m + p):16 * (NL * m + q)]
+                def piece(x, p, q):
+                    return B(x)[:, 16 * (3 * l0 + p):16 * (3 * l0 + q)]
 
-                def names(m, p, q):
-                    return cw.indirect(nm[:, 2 * l0 + HL * m + p:2 * l0 + HL * m + q])
-                for m in range(3):
-                    z = lm if m == 2 else l1
-                    for p in range(l0, z, GP):
-                        q = min(z, p + GP)
-                        sg(piece("gv", m, p, q), names(m, p, q), cvr + [R("nm%s%d" % ("ab"[m > 0], a))], units("g%d" % m, p, q), 16 * (q - p))
+                def names(p, q):
+                    return cw.indirect(nm[:, 3 * l0 + p:3 * l0 + q])
+                plan = PLAN.get((t, 2 * s + a), PLAIN)
+                nmr = cvr + [R("nma%d" % a), R("nmb%d" % a)]
+                for eng, p, q in plan[0]:
+                    wr = ["g%d%d_%d" % (s, a, k) for k in range(p // 16, q // 16)]
+                    if eng == "S":
+                        sg(piece("gv", p, q), names(p, q), nmr, wr, 16 * (q - p))
+                    else:
+                        cp(piece("gv", p, q), names(p, q), nmr, wr, 16 * (q - p) * RG, gath=True)
                 for e, (m0, m1) in enumerate(((0, 1), (0, 2), (1, 2))):
-                    z = lm if e else l1
-                    for p in range(z, l1, PP):
-                        q = min(l1, p + PP)
-                        tt(piece("pr", e, p, q), names(2, p, q), piece("gv", m0, p, q), ALU.mult, cvr + [R("nmb%d" % a)] + units("g%d" % m0, p, q),
-                           units("pr%d" % e, p, q), 16 * (q - p) * RG, gath=True)
-                    for p in range(l0, z, PP):
-                        q = min(z, p + PP)
-                        tt(piece("pr", e, p, q), piece("gv", m0, p, q), piece("gv", m1, p, q), ALU.mult,
-                           units("g%d" % m0, p, q) + units("g%d" % m1, p, q), units("pr%d" % e, p, q), 16 * (q - p))
-                    o = px(HL * e, HL * e + HL)
-                    mm([[(o, esel("z233", p), B("pr")[:, 16 * (NL * e + l0) + p:16 * (NL * e + l1):16], HL) for p in range(16)]],
+                    for p, q in plan[1]:
+                        tt(piece("pr", HL * e + p, HL * e + q), piece("gv", HL * m0 + p, HL * m0 + q), piece("gv", HL * m1 + p, HL * m1 + q), ALU.mult,
+                           ["g%d%d_%d" % (s, a, 4 * m + k) for m in (m0, m1) for k in range(p // 16, q // 16)], units("pr%d" % e, l0 + p, l0 + q), 16 * (q - p))
+                    o = px(HL * e, HL * e + HL); c0 = 16 * HL * (3 * a + e)
+                    mm([[(o, esel("z233", p), B("pr")[:, c0 + p:c0 + 16 * HL:16], HL) for p in range(16)]],
                        units("pr%d" % e, l0, l1) + ["z233"], bx, e == 0, e == 2)
                     if e == 1:
                         mm([[(px(HL * k, HL * k + HL), sq("bdq%d" % k), xin(l0, l1), HL) for k in range(3)]], ["bdq0", "bdq1", "bdq2", rx], bx, False, False)
                 nf = B("nf"); n0 = 3 * l0; rn, rv, rf = R("nf%d" % a), R("v%d" % a), R("f%d" % a)
-                if ABS_ON == "S":
+                if t in ON_S["abs"]:
                     act(B("ab")[:, n0:n0 + 3 * HL], px(0, 3 * HL), ACT.Abs, 0.0, 1.0, [], [R("ab%d" % a)], 3 * HL, bx)
                     ts(nf[:, n0:n0 + 3 * HL], B("ab")[:, n0:n0 + 3 * HL], 140.4 * W, None, ALU.is_gt, None, [R("ab%d" % a)], [rn], 3 * HL // 2)
                 else:
@@ -415,42 +442,32 @@ def build_ops(g, core, T, topo, cost):
                 mm(lst, [rn, "idn", "gw0_", "gw1_", "gw2_"], be)
                 nv = HL if last else 2 * HL
                 v = B("v")[:, 2 * l0:2 * l0 + nv]
-                if SIGN_ON == "S":
+                tri = "tri"
+                if pgs[a] == "pg" and not last:
                     act(v, pe(0, nv), ACT.Sign, 0.5, 1.0, [], [rv], nv, be)
                 else:
                     ts(v, pe(0, nv), 0.0, 0.5, ALU.is_ge, ALU.subtract, [], [rv], nv, be)
-                mm([[(pf(0, HL), sq("tri"), B("v")[:, 2 * l0:2 * l0 + HL], HL)]], [rv, "tri"], bf)
-                if FIRST_ON == "S":
-                    act(f[:, l0:l1], pf(0, HL), ACT.Relu, cF, 1.0, ["cF"], [rf], HL, bf)
-                else:
-                    ts(f[:, l0:l1], pf(0, HL), cF, 0.0, ALU.add, ALU.max, ["cF"], [rf], HL, bf)
+                    tri = "tri2"
+                mm([[(pf(0, HL), sq(tri), B("v")[:, 2 * l0:2 * l0 + HL], HL)]], [rv, tri], bf)
+                ts(f[:, l0:l1], pf(0, HL), cF, -4096.0, ALU.add, ALU.max, ["cF"], [rf], HL, bf)
                 if not last:
                     lst = []
                     for b in range(3):
                         o = pyd(HL * b, HL * b + HL)
-                        lst.append([(o, mat(MD + b), xin(l0, l1), HL), (o, sq("pg"), B("v")[:, 2 * l0 + HL:2 * l0 + 2 * HL], HL), (o, sq("pfm"), f[:, l0:l1], HL)])
-                    mm(lst, [rx, "md", rv, rf, "pg", "pfm"], byd)
-                    ts(y[:, n0:n0 + 3 * HL], pyd(0, 3 * HL), -8192.0, -2048.0, ALU.add, ALU.max, [], [R("yd%d" % a)], 3 * HL, byd)
+                        lst.append([(o, mat(MD + b), xin(l0, l1), HL), (o, sq(pgs[a]), B("v")[:, 2 * l0 + HL:2 * l0 + 2 * HL], HL), (o, sq("pfm"), f[:, l0:l1], HL)])
+                    mm(lst, [rx, "md", rv, rf, pgs[a], "pfm"], byd)
+                    ts(y[:, n0:n0 + 3 * HL], pyd(0, 3 * HL), cY, -2048.0, ALU.add, ALU.max, ["cY"], [R("yd%d" % a)], 3 * HL, byd)
                     co = B("colo")[:, t, a, 0:3 * HC]
                     columns(s, a, "zl", lambda u: y[:, n0 + u:n0 + 3 * HL:16], [R("yd%d" % a)], 1024.0, co, R("co%d%d" % (a, t)))
                     rdma(B("coli")[:, t + 1, a, 0:3 * HC], co, "a%s%d_%d" % ("cd"[a], t + 1, s), [R("co%d%d" % (a, t))],
                          ["col%d%d_%d" % (s, a, t + 1)], LAT_R)
 
-            mm([[(pxx(NL * m, NL * m + NL), sq("idb"), f[:], NL)]
-                + [(pxx(NL * m + HL * a, NL * m + HL * a + HL), sq("idb"), nmf[:, HL * (3 * a + m):HL * (3 * a + m + 1)], HL) for a in range(2)]
-                for m in range(3)], [R("nmf"), "idb"] + both("f"), bxx)
             if not last:
+                mm([[(pxx(0, NL), sq("idb"), f[:], NL), (pxx(0, NL), sq("idb"), nmf[:, :, 0, :], NL)]], [R("nmf"), "idb"] + both("f"), bxx)
                 eq = B("eq"); so = B("so")
                 mm([[(pd(NL * h + HL * c, NL * h + HL * c + HL), sq("bdf"), f[:, HL * h:HL * h + HL], HL) for h in range(2) for c in range(2)]],
                    both("f") + ["bdf"], bdd, False, True)
-                if EQ_ON == "V":
-                    ts(eq[:], pd(0, 2 * NL), M27 + 36864.0, M27, ALU.add, ALU.is_equal, [], [R("eq")], 2 * NL, bdd)
-                else:
-                    act(B("ae")[:], pd(0, 2 * NL), ACT.Abs, 36864.0, 1.0, [], [R("ae")], 2 * NL, bdd)
-                    if EQ_ON == "S":
-                        act(eq[:], B("ae")[:], ACT.Relu, 8.0, -1.0, [R("ae")], [R("eq")], 2 * NL)
-                    else:
-                        ts(eq[:], B("ae")[:], 8.0, None, ALU.is_lt, None, [R("ae")], [R("eq")], NL)
+                ts(eq[:], pd(0, 2 * NL), M27 - 28672.0, M27, ALU.add, ALU.is_equal, [], [R("eq")], 2 * NL, bdd)
                 if DUP_SO:
                     o = pso(0, 2 * NC)
                     mm([[(o, sq("idk"), eq[:, u:2 * NL:16], 8) for u in range(16)]
@@ -463,7 +480,7 @@ def build_ops(g, core, T, topo, cost):
                        [R("eq"), R("colf"), "idb", "idk"], bso)
                     tt(so[:, 0:NC], o, T.jl[:, 0:NC], ALU.min, ["jl"], [R("so")], 8, bso)
                 ts(B("so16")[:, 0:NC], so[:, 0:NC], 2048.0, None, ALU.add, None, [R("so")], [R("so16")], 8)
-                ts(B("ncol")[:], pxx(0, NL), 2048.0, 4096.0, ALU.add, ALU.min, [], [R("ncol")], NL, bxx)
+                ts(B("ncol")[:], pxx(0, NL), 6144.0, 4096.0, ALU.add, ALU.min, [], [R("ncol")], NL, bxx)
                 cp(tb.indirect(B("so16")[:, 0:NC]), B("ncol")[:], [R("so16"), R("ncol")], [R("tb")], NL * RS, gath=True)
                 pyf, byf = psum(s, "yf"); pxo, bxo = psum(s, "xo"); x1 = XOFF[t + 1] * NL; x2 = XOFF[t + 2] * NL
                 if wf:
@@ -472,39 +489,34 @@ def build_ops(g, core, T, topo, cost):
                         b, r0 = STAR[j + 1]; o = pyf(NL * j, NL * j + NL)
                         lst.append([(o, mat(MS + (r0 - 2) // 4), xin(NL * b, NL * b + NL), NL), (o, mat(MH + LATER.index((t + 4, t + 5 + j))), hq, NL),
                                     (o, sq("pfm"), f[:], NL)]
-                                   + [(pyf(NL * j + HL * a, NL * j + HL * a + HL), sq("pg"), B("v")[:, NL * a + HL:NL * a + NL], HL) for a in range(2)])
-                    mm(lst, [rx, rq, rh, "ms", "pg", "pfm"] + both("v") + both("f"), byf)
-                    if YF_ON == "S":
-                        act(B("yf")[:, 0:wf * NL], pyf(0, NL * wf), ACT.Relu, -6144.0, 1.0, [], [R("yf")], NL * wf, byf)
-                    else:
-                        ts(B("yf")[:, 0:wf * NL], pyf(0, NL * wf), -8192.0, -2048.0, ALU.add, ALU.max, [], [R("yf")], NL * wf, byf)
+                                   + [(pyf(NL * j + HL * a, NL * j + HL * a + HL), sq(pgs[a]), B("v")[:, NL * a + HL:NL * a + NL], HL) for a in range(2)])
+                    mm(lst, [rx, rq, rh, "ms", "pfm"] + pgs + both("v") + both("f"), byf)
+                    ts(B("yf")[:, 0:wf * NL], pyf(0, NL * wf), cY, -2048.0, ALU.add, ALU.max, ["cY"], [R("yf")], NL * wf, byf)
                 lst = [[], [], []]
                 for j in range(wf):
                     b = STAR[j][0]; k = (STAR[j][1] - 6) // 4
-                    lst[2 * b].append((pxo(NL * b, NL * b + NL), T.rf[:, 128 * k:128 * k + 128], B("yf")[:, NL * j:NL * (j + 1)], (4 if YF_ON == "S" else 1) * NL))
+                    lst[2 * b].append((pxo(NL * b, NL * b + NL), T.rf[:, 128 * k:128 * k + 128], B("yf")[:, NL * j:NL * (j + 1)], NL))
                 for a in range(2):
                     lst[0 if wf else a] += [(pxo(HL * a, HL * a + HL), mat(RD + b), y[:, HL * (3 * a + b):HL * (3 * a + b + 1)], HL) for b in range(3)]
                 mm([x for x in lst if x], both("yd") + [R("yf"), "mr", "rf"], bxo)
                 ts(B("xo")[:, x1:x2], pxo(0, x2 - x1), cX, None, ALU.add, None, ["cX"], [R("xo%d" % t)], x2 - x1, bxo)
                 rdma(B("xi")[:, x1:x2], B("xo")[:, x1:x2], "ay%d_%d" % (t + 1, s), [R("xo%d" % t)],
                      ["x%d_%d" % (s, t + 1), "q%d_%d" % (s, t + 1)], LAT_R + 0.5)
-            ons = OUT_ON == "S" and not last
-            if ons:
-                act(T.mkf[:, :, s, :], pxx(0, 3 * NL), ACT.Relu, -6143.0, 1.0, [], [R("mk")], 3 * NL, bxx)
-            else:
-                ts(T.mk[:, :, s, :], pxx(0, 3 * NL), -8192.0, -4096.0, ALU.add, ALU.max, [], [R("mk")], 3 * NL, bxx)
-            if s == NS - 1:
-                o = py(0, 48); out = T.ybuf[:, 48 * t:48 * t + 48]
-                if ons:
-                    for k in range(4):
-                        mm([[(o, T.zf[:, 15 - u:143 - u], T.mkf[:, :, :, u], 256) for u in range(4 * k, 4 * k + 4)]], ["mk0", "mk1", "zf"], by, k == 0, k == 3)
-                    act(out, o, ACT.Identity, -1.0, 1.0, [], ["y%d" % t], 48, by)
+            for m in range(3):
+                if last and s == NS - 1:
+                    for a in range(2):
+                        tt(T.mk[:, 8 * m + 4 * a:8 * m + 4 * a + 4, s, :], nmf[:, a, m, :], f[:, HL * a:HL * a + HL], ALU.min,
+                           [R("nmf"), R("f%d" % a)], ["mk%d%d%d" % (s, m, a)], HL)
                 else:
-                    mm([[(o, esel("z1", u), T.mk[:, :, :, u], 48) for u in range(16)]], ["mk0", "mk1", "z1"], by)
-                    ts(out, o, 63488.0, -1.0, ALU.add, ALU.max, [], ["y%d" % t], 48, by)
+                    tt(T.mk[:, 8 * m:8 * m + 8, s, :], nmf[:, :, m, :], f[:], ALU.min, [R("nmf")] + both("f"), ["mk%d%d%d" % (s, m, a) for a in range(2)], NL)
+            if s == NS - 1:
+                o = py(0, 48)
+                mm([[(o, esel("z1", u), T.mk[:, :, :, u], 48) for u in range(16)]],
+                   ["mk%d%d%d" % (x, m, a) for x in range(NS) for m in range(3) for a in range(2)] + ["z1"], by)
+                ts(T.ybuf[:, 48 * t:48 * t + 48], o, 63488.0, -1.0, ALU.add, ALU.max, [], ["y%d" % t], 48, by)
         for m in range(3):
             k = 3 * t + m
-            dma("S" if last and m == 1 else "Y", [(T.yn[:, 256 * k:256 * k + 256], T.ybuf[:, 16 * k:16 * k + 16])], ["y%d" % t], [], "out%d" % k, 2.5)
+            dma("S" if last and m == 1 else "Y", [(T.yn[:, 256 * k:256 * k + 256], T.ybuf[:, 16 * k:16 * k + 16])], ["y%d" % t], [], "out%d" % k, 2.0)
     return ops
 
 
@@ -541,7 +553,7 @@ def order_queues(variants, deps):
     eng = ["VSPGY".index(o["eng"]) for o in ops]
     tabs = []
     for v, c in zip(variants, COSTS):
-        pre = [[(j, v[j]["lat"] + c[4] if (eng[j] != eng[i] or (h and v[j]["sem"])) else (c[5] if h and eng[i] != 2 else 0.0))
+        pre = [[(j, FIRST_CALL if j in v[i].get("after", []) and not h else v[j]["lat"] + c[4] if (eng[j] != eng[i] or (h and v[j]["sem"])) else (c[5] if h and eng[i] != 2 else 0.0))
                 for j, h in deps[i].items()] for i in range(n)]
         suc = [[] for _ in range(n)]
         for i in range(n):
@@ -565,16 +577,21 @@ def order_queues(variants, deps):
             st.insert(k, t0); en.insert(k, t0 + d); fin[i] = t0 + d
         return fin
 
-    def replay(order, tab):
+    ends = [i for i in range(n) if not tabs[0][3][i]]
+
+    def replay(order, tab, old=None, p0=0):
         d, lt, pr, _ = tab
-        fin = [0.0] * n; free = [0.0] * 5
-        for i in order:
+        fin = list(old) if p0 else [0.0] * n
+        free = [0.0] * 5
+        for i in order[:p0]:
+            free[eng[i]] = fin[i]
+        for i in order[p0:]:
             t0 = free[eng[i]]
             for j, gp in pr[i]:
                 if fin[j] + gp > t0:
                     t0 = fin[j] + gp
             fin[i] = free[eng[i]] = t0 + d[i]
-        return fin, max(fin[i] + lt[i] for i in range(n))
+        return fin, max([fin[i] + lt[i] for i in ends])
 
     def legal(key, edges, ahead):
         key = list(key)
@@ -640,10 +657,29 @@ def order_queues(variants, deps):
         arcs = critical(cur, tabs[k], res[k][0])
         if not arcs:
             continue
-        new = swap(cur, *arcs[int(rng.integers(len(arcs)))])
+        u, v = arcs[int(rng.integers(len(arcs)))]
+        new = swap(cur, u, v)
         if new is None:
             continue
-        nres = [replay(new, tab) for tab in tabs]
+        early = rng.random() < 0.5
+        for _ in range(int(rng.choice(STEPS))):
+            if early:
+                p = new.index(v) - 1
+                while p >= 0 and eng[new[p]] != eng[v]:
+                    p -= 1
+                more = swap(new, new[p], v) if p >= 0 and new[p] not in deps[v] else None
+            else:
+                p = new.index(u) + 1
+                while p < n and eng[new[p]] != eng[u]:
+                    p += 1
+                more = swap(new, u, new[p]) if p < n and u not in deps[new[p]] else None
+            if more is None:
+                break
+            new = more
+        p0 = 0
+        while new[p0] == cur[p0]:
+            p0 += 1
+        nres = [replay(new, tab, r[0], p0) for tab, r in zip(tabs, res)]
         sc = sum(r[1] * w for r, w in zip(nres, scale))
         if sc <= csc + HEAT * (1.0 - it / SWAPS) * float(rng.exponential()) * scale[0]:
             cur, res, csc = new, nres, sc

@@ -3,563 +3,642 @@ from concourse.mybir import AluOpType, ActivationFunctionType
 
 ALU = AluOpType
 ACT = ActivationFunctionType
-RO, NB, TW = 5, 451, 512
-W = 233.0
+RO, NB = 5, 451
+W, W2 = 233.0, 233.25
 MAGIC = 1.5 * 2.0 ** 39
-M23, M27 = 1.5 * 2.0 ** 23, 1.5 * 2.0 ** 27
+M23, M26 = 1.5 * 2.0 ** 23, 1.5 * 2.0 ** 26
+BIG = 8192.0
+C0, CS = 64, 456
 NEXT = [[1, 2, 3, 4], [0, 4, 2, 3], [0, 1, 2, 4], [0, 1, 4, 3]]
 PAIRS = [(0, 1), (0, 2), (0, 3), (1, 2), (1, 3), (2, 3)]
-STAR = [(0, 6), (0, 10), (1, 6), (1, 2)]
 LATER = [(4, 5), (4, 6), (4, 7), (5, 6), (5, 7), (6, 7)]
-XOFF = [0, 2, 4, 5, 6, 7]
+TWINS = [(0, 1, -1), (0, 2, 7), (0, 3, 6), (1, 2, 6), (1, 3, 7), (2, 3, 6), (4, 0, 5), (4, 1, 6), (4, 2, 7), (3, 4, 6),
+         (5, 0, 6), (5, 1, 7), (2, 5, 7), (3, 5, 7), (6, -1, 7)]
+QROW = {(min(x, z), max(x, z)): k for k, (x, y, z) in enumerate(TWINS) if z >= 0}
+XW = [264, 520, 264, 264, 264]
+XOFF = [0, 264, 784, 1048, 1312, 1576]
+SG = 35
 
-NS, NH, NC, NL = 2, 4, 8, 128
-HL, HC = 64, 4
-SPLIT_NM = 0
-SQUARED = []
-PLAIN = ([("S", 0, 64), ("S", 64, 128), ("S", 128, 192)], [(0, 64)])
-PLAN = {(4, 3): ([("S", 0, 64), ("S", 64, 128), ("V", 128, 160), ("S", 160, 192)], [(0, 32), (32, 64)])}
-ON_S = {"abs": [], "first": [], "eq": [], "out": [], "yf": []}
-SIGN_ON = "SS"
-DUP = True
-DUP_SO = True
-FIRST_CALL = 6.0
-FIRST_HOLD = 7.0
-SPREAD = 1
-COSTS = [(0.00088, 0.00047, 1.55, 3.8, 0.2, 0.12, 4.5), (0.00087, 0.00044, 1.56, 3.8, 0.1, 0.06, 3.0), (0.00085, 0.00045, 1.1, 2.0, 0.15, 0.1, 3.5), (0.0011, 0.00055, 1.95, 5.0, 0.1, 0.06, 3.0)]
-WEIGHT = [1, 1, 2.5, 0.8]
-SEARCH = 1800
+KIND = [x.split() for x in ("P00a P00a P00a P00a", "P00a P01a P00a P00a", "P00a P01a P00a P00a", "P00a P01a P00a P00a", "P01b P01b P01d P01d")]
+SIGN_ON = "VVVVV"
+E_ON = "V"
+SCALE_V = ["mq", "wb", "hc", "ri", "pi", "k15", "k3", "k0"]
+P_PART = 1400
+C_CUT = [(0, 48), (48, 64)]
+LOADS = [2.0, 2.6, 3.6, 5.8]
+D_AT = [0, 2, 2, 2, 2]
+ZERO_S = ["dpf", "yb", "vb", "xo0", "xo1", "mats13", "mats17"]
+SPLIT_POST = ["11", "11", "11", "11", "11"]
+FIRST_CALL = 1.0
+FIRST_HOLD = 6.0
+COSTS = [(0.00087, 0.00047, 1.45, 3.4, 0.25, 0.14, 4.8, 0.8, 2.5), (0.00087, 0.00045, 1.5, 3.8, 0.13, 0.08, 3.5, 0.8, 2.5),
+         (0.00083, 0.00044, 1.1, 2.0, 0.17, 0.1, 4.0, 0.8, 2.5), (0.0011, 0.00055, 1.95, 5.0, 0.1, 0.06, 3.0, 0.8, 2.5)]
+WEIGHT = [0.3, 1.2, 2.0, 0.7]
+SEARCH = 8000
 SEED = 1
-SWAPS = 25000
-HEAT = 0.3
+SWAPS = 12000
+HEAT = 0.05
+PASSES = [1]
+NOISE = [0.4, 1.5]
+WINDOW = 5
+PLACE = [0]
 STEPS = [0, 0, 1, 2, 3, 5]
 ORDER = {}
+
+MATS = ["gab", "gac", "gbc", "c35", "rdo", "rdd", "ri", "pg", "mdo", "mdd", "mf", "ms6", "ms10", "mh0", "mh1", "mh2", "mh3", "mh4", "mh5", "mq6", "mq7",
+        "id4k", "cq",
+        "idb", "idn", "id2k", "bd", "pn", "hc", "k0", "k3", "pi", "gbn", "rf6", "rf10", "bdx", "bdy", "pm", "pmn", "id64", "i64"]
+NZ = 21
+
+SCRATCH = {
+    "cv": ("sbuf", [128, 4112], "bfloat16"), "ob": ("sbuf", [128, 8, 64, 4], "bfloat16"),
+    "dpf": ("sbuf", [128, 64, 16, 4], "float32"), "dpo": ("sbuf", [128, 3, 64, 4], "bfloat16"), "lo": ("sbuf", [128, 2, 128], "float32"),
+    "gab": ("sbuf", [128, 4, 2048], "bfloat16"), "gcc": ("sbuf", [128, 4, 1024], "bfloat16"),
+    "xx": ("sbuf", [128, 4, 1024], "float32"), "yy": ("sbuf", [128, 4, 1024], "float32"), "pab": ("sbuf", [128, 4, 1024], "bfloat16"),
+    "coli": ("sbuf", [128, RO, 4, 16], "uint16"), "colo": ("sbuf", [128, RO, 4, 16], "uint16"), "nm": ("sbuf", [128, 768], "uint16"),
+    "nf": ("sbuf", [128, 4, 192], "bfloat16"), "rr": ("sbuf", [128, 4, 128], "float16"),
+    "vb": ("sbuf", [128, 1040], "bfloat16"), "yb": ("sbuf", [128, 1040], "float16"),
+    "hq": ("sbuf", [128, 3, 256], "float16"), "ee": ("sbuf", [128, 2, 2, 2, 2, 2, 16], "float16"),
+    "fs": ("sbuf", [128, 2, 4, 2, 16], "bfloat16"), "nmf": ("sbuf", [128, 2, 3, 4, 2, 16], "float16"), "mk": ("sbuf", [128, 3, 4, 4, 16], "float16"),
+    "wab": ("sbuf", [128, 2, 2 * 4 * SG], "float16"), "scn": ("sbuf", [128, 2, 2 * 4 * SG], "float16"),
+    "so16": ("sbuf", [128, 2, 8], "uint16"), "ncol": ("sbuf", [128, 2, 128], "int32"), "yf": ("sbuf", [128, 2, 384], "float16"),
+    "ybuf": ("sbuf", [128, 48 * RO], "float32"),
+    "mats": ("sbuf", [128, len(MATS), 8, 16], "bfloat16"), "mq": ("sbuf", [128, 6, 8, 16], "float16"),
+    "wt": ("sbuf", [128, 4, 3, 8], "bfloat16"), "wb": ("sbuf", [128, 8, SG], "bfloat16"),
+    "pu": ("sbuf", [128, 4, 2, 1024], "bfloat16"), "yl": ("sbuf", [128, 192, 4], "float32"), "w8": ("sbuf", [128, 4, 8], "bfloat16"), "wy": ("sbuf", [128, 3, 8], "float32"),
+    "pidx": ("sbuf", [128, 8], "int32"), "pand": ("sbuf", [128, 8], "int32"), "pc": ("sbuf", [128, 64], "float32"),
+    "xr": ("sbuf", [128, 144], "float32"), "xc": ("sbuf", [128, 8, 16], "bfloat16"), "gr": ("sbuf", [128, 8, 16], "bfloat16"), "z1": ("sbuf", [128, 144], "bfloat16"),
+    "g8": ("sbuf", [128, 3, 8], "float32"), "c38": ("sbuf", [128, 3, 8], "float32"), "gm8": ("sbuf", [128, 3, 8], "float32"),
+    "m16": ("sbuf", [128, 2, 2, 64], "bfloat16"), "pw": ("sbuf", [128, 2, 16], "float32"), "uge": ("sbuf", [128, 4], "float32"),
+    "ci": ("sbuf", [128, 2, 2, 32], "bfloat16"), "cpd": ("sbuf", [128, 2, 2, SG], "float16"), "d1": ("sbuf", [128, 8 * SG], "float16"),
+    "zz": ("sbuf", [128, 520], "bfloat16"), "me": ("sbuf", [128, 2, 64], "bfloat16"), "t4": ("sbuf", [128, 12], "float32"), "z8": ("sbuf", [128, 144], "bfloat16"), "cb": ("sbuf", [128, 2, 48], "bfloat16"),
+}
+for _s in range(2):
+    SCRATCH["tb%d" % _s] = ("sbuf", [128, 2048], "int32")
+    SCRATCH["xi%d" % _s] = ("sbuf", [128, XOFF[RO]], "float16")
+    SCRATCH["xo%d" % _s] = ("sbuf", [128, 520], "float16")
+for _b in range(8):
+    SCRATCH["ps%d" % _b] = ("psum", [128, 512], "float32")
+
+SEMAPHORES = (["cV", "cS", "cP", "cG", "lob0", "lob1", "lcv", "sent", "sx0", "sx1", "ah10", "ah11", "ah20", "ah21"] + ["lt%d" % p for p in range(4)]
+              + ["ac%d_%d" % (t, p) for t in range(1, RO) for p in range(4)] + ["ay%d_%d" % (t, s) for t in range(1, RO) for s in range(2)]
+              + ["out%d" % k for k in range(3 * RO - 2)])
+
+SL = np.s_
+MASKS = {}
 
 
 def source(case, pair):
     x, y = sorted((NEXT[case][pair[0]], NEXT[case][pair[1]]))
-    return STAR[0][1] + x if y == 4 else PAIRS.index((x, y))
+    return 6 + x if y == 4 else PAIRS.index((x, y))
 
 
-MD, MS, MH, RD, RF, NM = 0, 3, 6, 12, 15, 17
-
-SCRATCH = {
-    "cv": ("sbuf", [128, 4112], "bfloat16"), "ob": ("sbuf", [128, 2048], "bfloat16"),
-    "ovf": ("sbuf", [128, 1024], "bfloat16"), "ovg": ("sbuf", [128, 1024], "bfloat16"), "dp": ("sbuf", [128, 28, 256], "bfloat16"),
-    "ybuf": ("sbuf", [128, 48 * RO], "float32"), "tg": ("sbuf", [128, 8], "float32"), "pe": ("sbuf", [128, 8], "float32"),
-    "pidx": ("sbuf", [128, 8], "int32"), "pand": ("sbuf", [128, 8], "int32"), "pc": ("sbuf", [128, 32], "float32"),
-    "xr": ("sbuf", [128, 144], "float32"), "gr": ("sbuf", [128, 128], "float32"),
-    "ovs": ("sbuf", [128, 2, 1024], "bfloat16"), "zs": ("sbuf", [128, 6 * 144], "bfloat16"), "sq": ("sbuf", [128, 21 * 128], "bfloat16"),
-    "gw0": ("sbuf", [128, 3, 8, 16], "bfloat16"), "gw1": ("sbuf", [128, 8, 16], "bfloat16"),
-    "gw": ("sbuf", [128, 384], "bfloat16"), "rf": ("sbuf", [128, 256], "bfloat16"), "rff": ("sbuf", [128, 256], "float32"),
-    "zf": ("sbuf", [128, 144], "float32"), "mkf": ("sbuf", [128, 24, 2, 16], "float32"), "mk": ("sbuf", [128, 24, 2, 16], "float16"),
-    "hq": ("sbuf", [128, 3, 256], "float16"), "codes": ("sbuf", [128, NM, 8, 16], "bfloat16"), "mats": ("sbuf", [128, 128 * NM], "bfloat16"),
-    "ci": ("sbuf", [128, 256], "bfloat16"), "hb": ("sbuf", [128, 256], "bfloat16"), "mask": ("sbuf", [128, 256], "bfloat16"),
-    "cb": ("sbuf", [128, 32], "bfloat16"), "cf": ("sbuf", [128, 32], "bfloat16"),
-    "jl0": ("sbuf", [128, 16], "float32"), "jl": ("sbuf", [128, 16], "float32"),
-    "il0": ("sbuf", [128, 128], "float32"), "il": ("sbuf", [128, 128], "uint16"),
-}
-ZS = ["z1", "z125", "z233", "zl", "zp", "zn"]
-SQ = ["one", "idb", "idn", "idk", "id16", "bd", "bd233", "bdq0", "bdq1", "bdq2", "bda", "bdf", "bdk", "tr", "tri", "pfm", "cpg", "pg", "pg2", "tri2"]
-for _s in range(NS):
-    for _n, _w, _d in (("tb", [NH * TW], "int32"),
-                       ("xi", [XOFF[RO] * NL], "float16"), ("xo", [XOFF[RO] * NL], "float16"),
-                       ("y", [3 * NL], "float16"), ("yf", [3 * NL], "float16"), ("yff", [3 * NL], "float32"),
-                       ("coli", [RO, 2, 16], "uint16"), ("colo", [RO, 2, 16], "uint16"), ("colf", [16], "float16"),
-                       ("nm16", [3 * NL], "uint16"), ("nmf", [2, 3, HL], "float16"),
-                       ("gv", [48 * NL], "bfloat16"), ("pr", [48 * NL], "bfloat16"),
-                       ("ab", [3 * NL], "bfloat16"), ("nf", [3 * NL], "bfloat16"), ("v", [2 * NL], "bfloat16"), ("f", [NL], "bfloat16"),
-                       ("ae", [2 * NL], "bfloat16"), ("eq", [2 * NL], "bfloat16"), ("so", [32], "float32"), ("so16", [8], "uint16"),
-                       ("ncol", [NL], "int32")):
-        SCRATCH["%s_%d" % (_n, _s)] = ("sbuf", [128] + _w, _d)
-for _b in range(8):
-    SCRATCH["ps%d" % _b] = ("psum", [128, 512], "float32")
-PSUM = {"px0": (0, 0), "yd0": (0, 192), "x": (0, 0), "px1": (1, 0), "yd1": (1, 192), "yf": (1, 0), "xo": (1, 0),
-        "ev0": (2, 0), "f0": (2, 128), "col0": (2, 192), "ev1": (2, 208), "f1": (2, 336), "col1": (2, 400), "y": (2, 416),
-        "d": (3, 0), "so": (3, 256), "x0": (3, 0)}
-
-SEMAPHORES = (["cV", "cS", "cP", "cG", "lob0", "lob1", "lcv", "sent"] + ["lt%d" % s for s in range(NS)]
-              + ["a%s%d_%d" % (k, t, s) for k in "cdy" for t in range(1, RO) for s in range(NS)] + ["ah1", "ah2"]
-              + ["out%d" % k for k in range(3 * RO)])
+def cover(ap):
+    key = (ap[0], str(ap[1]))
+    if key not in MASKS:
+        shape = SCRATCH[ap[0]][1][1:]
+        hit = np.zeros(shape, bool); hit[ap[1][1:]] = True
+        MASKS[key] = int.from_bytes(np.packbits(hit.ravel(), bitorder="little").tobytes(), "little")
+    return MASKS[key]
 
 
-def build_ops(g, core, T, topo, cost):
-    ops = []; tag = [None, 0]; ext = {}; first = []
-    CY, PCY, RG, RS, _, _, LAT_R = cost
+def size(ap):
+    return bin(cover(ap)).count("1")
+
+
+def lines(entries):
+    out = []; left = sorted(entries, key=lambda e: (e[2], e[1]))
+    while left:
+        r, c, w = left[0]; best = [left[0]]
+        for r2, c2, w2 in left[1:]:
+            if w2 == w and c2 > c:
+                run = [left[0]]
+                while (r + (r2 - r) * len(run), c + (c2 - c) * len(run), w) in left:
+                    run.append((r + (r2 - r) * len(run), c + (c2 - c) * len(run), w))
+                if len(run) > len(best):
+                    best = run
+        out.append(best); left = [e for e in left if e not in best]
+    return out
+
+
+def build_ops(g, core, T, topo):
+    ops = []; tag = [None, 0]; first = []; sent = {}
     V, S, P = g.vector, g.scalar, g.tensor
     n = len(T.cores); rank = T.rank_of(core)
     nxt = T.cores[(rank + 1) % n]; prv = T.cores[(rank - 1) % n]
 
-    def op(eng, fn, rd, wr, dur, bank=None, sem=None, lat=0.0):
-        ops.append({"eng": eng, "fn": fn, "rd": rd, "wr": wr, "dur": dur, "bank": bank, "sem": sem, "lat": lat,
-                    "ext": [ext[r] for r in rd if r in ext], "typ": (tag[0], len(ops) - tag[1])})
+    def A(name, idx=()):
+        return (name, (slice(None),) + (idx if isinstance(idx, tuple) else (idx,)))
 
-    def vd(x, gath=False):
-        return (0.05 if gath else 0.015) + max(64, x) * CY
+    def top8(ap):
+        return (ap[0], (slice(0, 8),) + ap[1][1:])
 
-    def ts(out, in0, s1, s2, o0, o1, rd, wr, x, bank=None):
+    def R(x):
+        if not isinstance(x, tuple):
+            return x
+        if x[0] == "ind":
+            return R(x[1]).indirect(R(x[2]))
+        return T[x[0]][x[1]]
+
+    def parts(lst):
+        out = []
+        for x in lst:
+            if isinstance(x, tuple):
+                out += [x[1], x[2]] if x[0] == "ind" else [x]
+        return out
+
+    def op(eng, fn, rd, wr, kind, x, sem=None, lat=0.0):
+        rd = parts(rd); wi = [w for w in wr if w[0] == "ind"]
+        rd += [w[2] for w in wi]; wr = [w[1] if w[0] == "ind" else w for w in wr]
+        bank = [a[0] for a in rd + wr if a[0] in SCRATCH and SCRATCH[a[0]][0] == "psum"]
+        ops.append({"eng": eng, "fn": fn, "rd": [a for a in rd if a[0] in SCRATCH and a[0] not in bank], "wr": [a for a in wr if a[0] in SCRATCH and a[0] not in bank],
+                    "kind": kind, "x": x, "bank": bank[0] if bank else None, "sem": sem, "lat": lat, "arr": None, "more": 0.0,
+                    "typ": (tag[0], len(ops) - tag[1])})
+
+    def two(*aps):
+        return all(SCRATCH[a[0]][2] in ("bfloat16", "float16", "uint16") for a in aps)
+
+    def ts(out, in0, s1, s2, o0, o1=None):
+        x = size(out) / (2 if two(out, in0) else 1)
         if o1 is None:
-            op("V", lambda: V.tensor_scalar(out, in0, s1, None, o0), rd, wr, vd(x), bank)
+            op("V", lambda: V.tensor_scalar(R(out), R(in0), R(s1), None, o0), [in0, s1], [out], "v", x)
         else:
-            op("V", lambda: V.tensor_scalar(out, in0, s1, s2, o0, o1), rd, wr, vd(x), bank)
+            op("V", lambda: V.tensor_scalar(R(out), R(in0), R(s1), R(s2), o0, o1), [in0, s1, s2], [out], "v", x)
 
-    def tt(out, in0, in1, o, rd, wr, x, bank=None, gath=False):
-        op("V", lambda: V.tensor_tensor(out, in0, in1, o), rd, wr, vd(x, gath), bank)
-
-    def cp(out, in_, rd, wr, x, bank=None, gath=False):
-        op("V", lambda: V.tensor_copy(out, in_), rd, wr, vd(x, gath), bank)
-
-    def ms(ap, c, wr, x=64):
-        op("V", lambda: V.memset(ap, c), [], wr, vd(x))
-
-    def sg(out, in_, rd, wr, x):
-        op("S", lambda: S.activation(out, in_, ACT.Copy), rd, wr, 0.065 + x * RG * CY)
-
-    def act(out, in_, func, bias, scale, rd, wr, x, bank=None):
-        op("S", lambda: S.activation(out, in_, func, bias=bias, scale=scale), rd, wr, 0.1 + max(64, x) * CY, bank)
-
-    def io(name, out, pat, base, cm, x, flt=True):
-        if flt:
-            op("G", lambda: g.iota(out, pat, base, cm, allow_small_or_imprecise_dtypes=True), [], [name], 0.13 + 2 * x * CY)
+    def tt(out, in0, in1, o):
+        if in0[0] == "ind":
+            kind, x = "vg", size(out)
         else:
-            op("G", lambda: g.iota(out, pat, base, cm), [], [name], 0.13 + 2 * x * CY)
+            kind, x = "v", size(out) * (1 if two(out, in0, in1) or in0[0][0:2] == "ps" or in1[0][0:2] == "ps" else 2)
+        op("V", lambda: V.tensor_tensor(R(out), R(in0), R(in1), o), [in0, in1], [out], kind, x)
 
-    def diag(name, src, cmp, fill):
-        op("G", lambda: g.affine_select(sq(name), sq(src), [[1, 128]], cmp, fill, 0, -1), [src], [name], 0.17 + 256 * CY)
+    def cp(out, in_):
+        kind, x = ("vs", size(in_)) if out[0] == "ind" else ("vg", size(out)) if in_[0] == "ind" else ("v", size(out))
+        op("V", lambda: V.tensor_copy(R(out), R(in_)), [in_], [out], kind, x)
 
-    def mm(lst, rd, bank, first=True, last=True):
+    def ms(ap, c):
+        if ap[0] in ZERO_S or (ap[0] == "mats" and "mats%d" % ap[1][1].start in ZERO_S):
+            return act(ap, A("zz", SL[0:size(ap)]), ACT.Copy)
+        op("V", lambda: V.memset(R(ap), c), [], [ap], "v", size(ap) / (2 if two(ap) else 1))
+
+    def scan(out, d0, d1, ini, o0, o1):
+        op("V", lambda: V.tensor_tensor_scan(R(out), R(d0), R(d1), ini, o0, o1), [d0, d1], [out], "v", size(out) / (2 if two(out, d0, d1) else 1))
+
+    def act(out, in_, func, bias=0.0, scale=1.0):
+        if out[0] in SCALE_V or (out[0] == "mats" and MATS[out[1][1]] in SCALE_V):
+            return ts(out, in_, scale, None, ALU.mult)
+        op("S", lambda: S.activation(R(out), R(in_), func, bias=R(bias), scale=R(scale)), [in_, bias, scale], [out],
+           "sg" if in_[0] == "ind" else "s", size(out))
+
+    def io(out, pat, base, cm=0):
+        if SCRATCH[out[0]][2] == "int32":
+            op("G", lambda: g.iota(R(out), pat, base, cm), [], [out], "g", size(out))
+        else:
+            op("G", lambda: g.iota(R(out), pat, base, cm, allow_small_or_imprecise_dtypes=True), [], [out], "g", size(out))
+
+    def put(ap, pat, base, w):
+        op("G", lambda: g.affine_select(R(ap), R(ap), pat, ALU.not_equal, float(w), base, 1), [ap], [ap], "g", size(ap))
+        ops[-1]["more"] = 0.04
+
+    def mm(lst, start=True, stop=True):
+        cyc = [max(min(64, size(l)), size(o)) * (4 if SCRATCH[l[0]][2] == "float32" else 1) for o, l, r in lst]
+        if sum(cyc) > P_PART and len(lst) > 1:
+            k = min(range(1, len(lst)), key=lambda x: abs(2 * sum(cyc[0:x]) - sum(cyc)))
+            mm(lst[0:k], start, False); mm(lst[k:], False, stop)
+            return
+
         def fn():
             ins = None
-            for grp in lst:
-                for k, (o, l, r, _) in enumerate(grp):
-                    ins = P.matmul(o, l, r, first and k == 0, last and k == len(grp) - 1)
+            for k, (o, l, r) in enumerate(lst):
+                ins = P.matmul(R(o), R(l), R(r), start and k == 0, stop and k == len(lst) - 1)
             return ins
-        op("P", fn, rd, [], 0.03 + sum(max(64, x[3]) for grp in lst for x in grp) * PCY, bank)
+        op("P", fn, [x[1] for x in lst] + [x[2] for x in lst], [lst[0][0]], "p",
+           sum(max(min(64, size(l)), size(o)) * (4 if SCRATCH[l[0]][2] == "float32" else 1) for o, l, r in lst))
 
-    def dma(eng, pairs, rd, wr, sem, lat):
+    def dma(eng, pairs, sem, lat):
         q = {"Y": g.sync, "S": g.scalar}[eng]
 
         def fn():
             for (o, i) in pairs:
-                q.dma_start(o, i).then_inc(T.sem[sem], 16)
-        op(eng, fn, rd, wr, 0.06 * len(pairs), bank="queue" + eng, sem=(sem, 16 * len(pairs)), lat=lat)
+                q.dma_start(R(o), R(i)).then_inc(T.sem[sem], 16)
+        op(eng, fn, [x[1] for x in pairs], [x[0] for x in pairs], "fix", 0.06 * len(pairs), sem=(sem, 16 * len(pairs)), lat=lat)
+        ops[-1]["bank"] = "queue" + eng
 
-    def rdma(out, in_, sem, rd, wr, lat, cnt=None):
+    def gdma(out, in_, sem, add):
+        if add:
+            op("G", lambda: g.dma_start(R(out), R(in_), accum_op=ALU.add).then_inc(T.sem[sem], 16), [in_, out], [out], "gd", 0, sem=(sem, 16))
+        else:
+            op("G", lambda: g.dma_start(R(out), R(in_)).then_inc(T.sem[sem], 16), [in_], [out], "gd", 0, sem=(sem, 16))
+
+    def rdma(out, in_, sem, local, more):
         rid, pid, _ = topo.addr(nxt)
-        use = topo.engines(core, nxt)[::SPREAD][0:cnt]
-        op("G", lambda: g.remote_dma(out, in_, T.sem[sem], T.sem.sent, pid, rid, sum(1 << e for e in use)), rd, wr,
-           0.3, sem=("sent", len(use)), lat=lat)
+        use = topo.engines(core, nxt)
+        sent[local] = sent.get(local, 0) + len(use)
+        op("G", lambda: g.remote_dma(R(out), R(in_), T.sem[sem], T.sem[local], pid, rid, sum(1 << e for e in use)), [in_], [out],
+           "rd", more, sem=(local, sent[local]))
+        ops[-1]["arr"] = (sem, len(topo.engines(prv, core)))
         ops[-1]["after"] = first[0:1]
         first.append(len(ops) - 1)
-        for w in wr:
-            ext[w] = (sem, len(topo.engines(prv, core)[::SPREAD][0:cnt]))
 
-    def zz(name):
-        k = ZS.index(name)
-        return T.zs[:, 144 * k:144 * k + 144]
+    def mat(name, idx=()):
+        return A("mats", (MATS.index(name),) + (idx if isinstance(idx, tuple) else (idx,)))
 
-    def esel(name, u):
-        k = ZS.index(name)
-        return T.zs[:, 144 * k + 15 - u:144 * k + 143 - u]
+    def ps(b, a, z, step=1):
+        return A("ps%d" % b, SL[a:z:step])
 
-    def sq(name, a=0, b=128, step=1):
-        k = SQ.index(name)
-        return T.sq[:, 128 * k + a:128 * k + b:step]
+    def tload(p, lat):
+        dma("Y", [(A("tb%d" % (p // 2), SL[1024 * (p % 2) + C0 + CS * s:1024 * (p % 2) + C0 + CS * s + NB]), A("tsee", SL[NB * (4 * s + p):NB * (4 * s + p + 1)]))
+                  for s in range(2)], "lt%d" % p, lat)
+    dma("Y", [(A("ob", SL[0:4]), A("obs", SL[0:1024]))], "lob0", 2.0)
+    dma("Y", [(A("ob", SL[4:8]), A("obs", SL[1024:2048]))], "lob1", 2.6)
+    tload(0, 3.6)
+    dma("Y", [(A("cv", SL[0:4096]), A("cvec"))], "lcv", 5.8)
+    for p in range(1, 4):
+        tload(p, 5.8 + p)
 
-    def mat(k):
-        return T.mats[:, 128 * k:128 * k + 128]
+    ncol = [6]
 
-    def psum(s, place):
-        b, c0 = PSUM[place]; b += 4 * s
-        return (lambda a, z, step=1: T["ps%d" % b][:, c0 + a:c0 + z:step]), "ps%d" % b
+    def pcol(in0, s1, s2, o0, o1=None):
+        c = A("pc", SL[ncol[0]:ncol[0] + 1]); ncol[0] += 1
+        ts(c, in0, s1, s2, o0, o1)
+        return c
+    U, K4, G16, KQ = [A("pc", SL[k:k + 1]) for k in range(4)]
+    io(A("pidx", SL[0:1]), [[0, 1]], 0, 1)
+    for k, a in enumerate((15, 3, 112, 127)):
+        ts(A("pand", SL[k:k + 1]), A("pidx", SL[0:1]), a, None, ALU.bitwise_and)
+    ts(A("pand", SL[4:5]), A("pidx", SL[0:1]), 64, None, ALU.bitwise_and)
+    ts(A("pand", SL[5:6]), A("pidx", SL[0:1]), 2, 15, ALU.arith_shift_right, ALU.bitwise_and)
+    cp(A("pc", SL[0:6]), A("pand", SL[0:6]))
+    ky = pcol(K4, 16.0, A("pc", SL[4:5]), ALU.mult, ALU.add)
+    io(mat("bdx"), [[64, 2], [0, 16], [16, 4]], 0)
+    io(A("g8"), [[0, 3], [16, 8]], 0)
+    io(A("gr"), [[16, 8], [0, 16]], 0)
+    io(A("xc"), [[1, 128]], 0)
+    io(A("m16"), [[0, 16], [1, 16]], 0)
+    io(A("xr"), [[1, 144]], -15)
+    io(A("c38"), [[1, 3], [16, 8]], 0)
+    ms(A("zz"), 0.0)
+    ms(A("dpf", SL[:, 15]), 0.0)
+    ms(A("cv", SL[4096:4112]), 0.0)
+    for a, b in ((7, 10), (0, 4), (4, 7), (10, 13), (13, 17), (17, NZ)):
+        ms(A("mats", SL[a:b]), 0.0)
+    ms(A("wt", 1), 0.0); ms(A("wb"), 0.0); ms(A("d1"), 0.0)
+    for s in range(2):
+        ms(A("xi%d" % s, SL[0:257:2]), 0.0); ms(A("xo%d" % s, SL[0:513:2]), 0.0)
+    ms(A("vb", SL[0:1040:2]), 0.0); ms(A("yb", SL[0:1040:2]), 0.0)
+    ts(A("w8", 0), A("g8", 0), G16, None, ALU.is_equal)
+    ts(A("w8", 1), A("g8", 0), G16, W / 4096, ALU.is_equal, ALU.mult)
+    ts(A("w8", 2), A("g8", 0), G16, 4096.0, ALU.is_equal, ALU.mult)
+    ts(A("wy", 0), A("g8", 0), G16, W2 / 4096, ALU.is_equal, ALU.mult)
+    ts(A("wy", SL[1:3]), A("g8", SL[1:3]), G16, 1.0 / 4096, ALU.is_equal, ALU.mult)
+    if any(x[0] == "U" for y in KIND for x in y):
+        act(A("w8", 3), A("w8", 1), ACT.Identity, 0.0, 64.0)
+    ts(A("gm8"), A("g8"), G16, 0.125, ALU.is_equal, ALU.mult)
+    ts(mat("bd"), A("gr"), G16, None, ALU.is_equal)
+    ts(mat("idb"), A("xc"), KQ, None, ALU.is_equal)
+    ts(mat("bdx"), mat("bdx"), G16, None, ALU.is_equal)
+    ts(mat("bdy"), A("gr"), ky, None, ALU.is_equal)
+    ts(mat("pm"), A("xc"), A("pc", SL[5:6]), ky, ALU.subtract, ALU.is_equal)
+    ts(A("m16"), A("m16"), U, None, ALU.is_equal)
 
-    def tload(eng, s, rd, lat):
-        dma(eng, [(T["tb_%d" % s][:, TW * k:TW * k + NB], T.tsee[:, NB * (NS * k + s):NB * (NS * k + s + 1)]) for k in range(NH)],
-            rd, ["tb%d" % s], "lt%d" % s, lat)
-    dma("Y", [(T.ob[:, 0:1024], T.obs[:, 0:1024])], [], ["ob0"], "lob0", 2.0)
-    dma("Y", [(T.ob[:, 1024:2048], T.obs[:, 1024:2048])], [], ["ob1"], "lob1", 2.6)
-    tload("Y", 0, [], 4.6)
-    dma("Y", [(T.cv[:, 0:4096], T.cvec[:])], [], ["cvl"], "lcv", 6.8)
-    tload("Y", 1, [], 8.8)
+    def e(k):
+        return A("m16", SL[0, 0, k:k + 1])
+    s2 = pcol(e(0), M26, None, ALU.mult)
+    si = pcol(e(14), 2049.0, pcol(s2, -256.0, None, ALU.add), ALU.mult, ALU.add)
+    ts(A("uge", SL[0:3]), A("xr", SL[19:28:4]), U, None, ALU.is_le)
+    sr = pcol(U, 6.0, -2048.0, ALU.is_lt, ALU.mult)
+    sr = pcol(sr, 6144.0, s2, ALU.add, ALU.add)
+    sr = pcol(e(15), -8192.0, pcol(e(14), -6143.0, sr, ALU.mult, ALU.add), ALU.mult, ALU.add)
+    wq = [pcol(e(15), e(3), W, ALU.subtract, ALU.mult),
+          pcol(e(14), -102.5, pcol(e(15), e(4), W2, ALU.subtract, ALU.mult), ALU.mult, ALU.add)]
+    w5 = pcol(e(5), -1.0 / 4096, None, ALU.mult)
+    for c, d in ((1800, -140.5), (1801, 140.5)):
+        wq.append(pcol(e(14), d / 4096, pcol(e(15), c / 2048.0, w5, ALU.mult, ALU.add), ALU.mult, ALU.add))
+    if any(x[0] == "U" for y in KIND for x in y):
+        wq += [pcol(e(15), e(k), W, ALU.subtract, ALU.mult) for k in (4, 5)]
+    for q in range(len(wq)):
+        act(A("mq", q), mat("bdx"), ACT.Identity, 0.0, wq[q])
+    k3 = pcol(K4, 3.0, None, ALU.is_equal)
+    cb = pcol(A("uge", SL[0:1]), -2 * BIG, None, ALU.mult)
+    cb = pcol(A("uge", SL[1:2]), 2 * BIG, cb, ALU.mult, ALU.add)
+    cb = pcol(A("uge", SL[2:3]), -BIG, cb, ALU.mult, ALU.add)
+    cY = pcol(k3, 2048.0, cb, ALU.mult, ALU.add)
+    ts(A("pw", 0), A("xr", SL[15:31]), U, 0.25, ALU.is_ge, ALU.max)
+    scan(A("pw", 1), A("pw", 0), A("xr", SL[0:16]), 2.0 ** 15, ALU.mult, ALU.max)
+    hcol = A("pw", SL[1, 15:16])
+    h1 = pcol(hcol, M23, None, ALU.mult); h2 = pcol(hcol, M23 + 1.0, None, ALU.mult)
+    e0 = pcol(e(0), 1.0, None, ALU.mult)
+    for nm, src, w in (("id64", "idb", 64.0), ("i64", "idb", 1.0 / 64), ("idn", "idb", -1.0), ("id2k", "idb", 2048.0), ("pn", "bd", -BIG), ("hc", "bd", hcol), ("k0", "bd", e0), ("k3", "bd", k3)):
+        act(mat(nm), mat(src), ACT.Identity, 0.0, w)
+    for nm, src, cols, w in (("c35", "bd", SL[:, 0:1], -3.5 / 4096), ("gab", "bdy", SL[:, 1:5], 1.0), ("gac", "bdy", SL[:, 0:6:5], 1.0), ("gac", "bdy", SL[:, 3:5], -1.0),
+                             ("gbc", "bdy", SL[:, 0:3], -1.0), ("gbc", "bdy", SL[:, 5:6], -1.0), ("pmn", "pm", SL[:, :], -1.0), ("gbn", "gbc", SL[:, :], -1.0),
+                             ("ri", "k3", SL[:, 0:6], -0.5)):
+        act(mat(nm, cols), mat(src, cols), ACT.Identity, 0.0, w)
+    for a, b, w in ((1, 2, 1.0 / 2048), (2, 18, -1.0), (18, 34, -1.0)):
+        act(A("wb", SL[:, a:b]), mat("k0", SL[:, 0:b - a]), ACT.Identity, 0.0, w)
+    kp = pcol(K4, G16, None, ALU.add)
+    ts(mat("rdo", SL[:, 0:3]), A("xc", SL[:, 0:3]), kp, None, ALU.is_equal)
+    tt(mat("rdo", SL[:, 0:6]), mat("rdo", SL[:, 0:6]), mat("ri", SL[:, 0:6]), ALU.add)
+    io(mat("pi"), [[16, 8], [4, 4], [0, 4]], 3)
+    for cols, w in ((SL[:, 0:4], -2.0), (SL[:, 4:16], 2.0)):
+        ts(mat("pi", cols), mat("pi", cols), KQ, w, ALU.is_equal, ALU.mult)
+    for nm, c, cols in (("rdd", 3.0, SL[:, 3:6]), ("rf6", 6.0, SL[:, :]), ("rf10", 10.0, SL[:, :])):
+        ts(mat(nm, cols), A("xc", cols), c, kp, ALU.subtract, ALU.is_equal)
+    ts(A("c38"), A("c38"), kp, pcol(k3, 0.5, None, ALU.mult), ALU.is_equal, ALU.subtract)
+    tt(A("wt", 0), A("c38"), A("gm8"), ALU.mult)
+    ts(A("wt", 3), A("gm8"), k3, -4.0, ALU.mult, ALU.mult)
+    ts(A("z8"), A("xr"), G16, 0.125, ALU.is_equal, ALU.mult)
+    act(A("z1"), A("z8"), ACT.Identity, 0.0, 8.0)
+    io(A("cb", 0), [[0, 6], [CS, 2], [0, 4]], 0)
+    ms(A("cb", 1), -0.4375)
+    put(A("wt", 1), [[0, 3], [-16, 8]], -14, -0.4375)
+    put(A("wt", SL[1, :, 1:8:2]), [[0, 3], [-32, 4]], -31, -CS / 2048.0)
+    for run in lines([(source(0, PAIRS[k]), k, 0.125) for k in range(3)]):
+        put(A("wt", SL[1, run[0][1]:run[-1][1] + 1]), [[run[0][0] - run[-1][0] if len(run) > 1 else 0, len(run)], [-16, 8]], -run[0][0], 0.125)
 
-    pc = T.pc
-    U, K4, G16, ODD = [pc[:, k:k + 1] for k in range(4)]
-    col = {}
+    def sparse(name, cnt, step, entries):
+        k = MATS.index(name)
+        for run in lines(entries):
+            (r, c, w), m = run[0], len(run)
+            dr, dc = (run[1][0] - r, run[1][1] - c) if m > 1 else (0, 1)
+            put(A("mats", SL[k:k + cnt, :, c:c + dc * (m - 1) + 1:dc]), [[-step, cnt], [-16, 8], [-dr, m]], -r, w)
+    sparse("pg", 1, 0, [(r, 4 * c + k, w * BIG) for r, c, w in ((0, 1, 1), (1, 1, 1), (2, 2, -1), (3, 2, -1), (4, 3, 1), (5, 3, -1)) for k in range(4)])
+    for nm, b in (("mdo", 0), ("mdd", 3)):
+        sparse(nm, 1, 0, [(source(c, PAIRS[b + k]), 4 * c + k, 1 if c else -1) for c in range(4) for k in range(3)])
+    sparse("mf", 1, 0, [(source(0, PAIRS[k]), k, 1) for k in range(6)] + [(14, 0, -3.5)])
+    sparse("ms6", 2, 4, [(6 + NEXT[c][k], 4 * c + k, 1) for c in range(4) for k in range(4) if NEXT[c][k] < 4])
+    for x, cnt in ((0, 3), (3, 2), (5, 1)):
+        sparse("mh%d" % x, cnt, 1, [(QROW[LATER[x]], 4 * c + NEXT[c].index(4), 1) for c in range(4)])
+    for j in (6, 7):
+        sparse("mq%d" % j, 1, 0, [(QROW[(NEXT[c][k], j)], 4 * c + k, 1) for c in range(4) for k in range(4) if NEXT[c][k] < 4])
+    ts(mat("id4k"), A("xc"), KQ, 4096.0, ALU.is_equal, ALU.mult)
+    act(mat("cq"), mat("bd"), ACT.Identity, 0.0, -0.4375)
+    sh0 = pcol(e(0), 2048.0, -2048.0, ALU.mult, ALU.add)
+    sh1 = pcol(sh0, M23, None, ALU.add)
+    for b in range(2):
+        io(A("ci", b), [[0, 2], [1, 2], [2, 16]], -b)
+    ts(A("ci"), A("ci"), pcol(U, 2.0, None, ALU.mult), -1.0, ALU.subtract, ALU.max)
+    if E_ON == "S":
+        ts(A("ci"), A("ci"), 1.0, 1.25, ALU.min, ALU.add)
+        ts(A("cpd", SL[:, :, 2:34]), A("ci"), -BIG, None, ALU.mult)
+        for q in range(2):
+            act(A("me", q), A("m16", SL[0, 0]), ACT.Identity, -65536.0, 65536.0 + 10240 * q)
+    else:
+        ts(A("cpd", SL[:, :, 2:34]), A("ci"), 1.0, -BIG, ALU.min, ALU.mult)
+    ms(A("cpd", SL[:, :, 0:1]), 0.0); ms(A("cpd", SL[:, :, 34:35]), 16.0); ms(A("d1", SL[0:8 * SG:SG]), 16.0)
+    io(A("t4", SL[0:4]), [[-32, 2], [CS - 16, 2]], 256 + C0)
+    io(A("t4", SL[4:12]), [[1024, 2], [16, 4]], 0)
+    ts(A("cpd", SL[:, :, 1:2]), A("t4", SL[0:4]), U, 1.0 / 256, ALU.subtract, ALU.mult)
+    ts(A("d1", SL[34:8 * SG:SG]), A("t4", SL[4:12]), U, 1.0 / 256, ALU.add, ALU.mult)
 
-    def pcol(name, in0, s1, s2, o0, o1, rd):
-        col[name] = pc[:, 4 + len(col):5 + len(col)]
-        ts(col[name], in0, s1, s2, o0, o1, ["pc"] + rd, [name], 1)
-        return col[name]
-    io("pidx", T.pidx[:, 0:1], [[0, 1]], 0, 1, 1, False)
-    for k, a in enumerate((15, 3, 112, 1)):
-        ts(T.pand[:, k:k + 1], T.pidx[:, 0:1], a, None, ALU.bitwise_and, None, ["pidx"], ["pand%d" % k], 1)
-    cp(pc[:, 0:4], T.pand[:, 0:4], ["pand%d" % k for k in range(4)], ["pc"], 4)
+    def win(name, base, e):
+        return A(name, SL[base + 1 - e:base + 129 - e])
 
-    def scol(name, in_, scale, bias, rd):
-        col[name] = pc[:, 4 + len(col):5 + len(col)]
-        act(col[name], in_, ACT.Identity, bias, scale, ["pc"] + rd, [name], 1)
-        return col[name]
-    U16 = pcol("u16", U, 16.0, None, ALU.mult, None, [])
-    io("il0", T.il0[:], [[1, NS], [256, 8], [NS, NC]], 0, 0, 128)
-    ts(T.il[:], T.il0[:], U16, None, ALU.add, None, ["il0", "u16"], ["il"], 128)
-    io("xr", T.xr[:], [[1, 144]], -15, 0, 144)
-    io("cb", T.cb[:, 0:3 * HC], [[0, 3], [TW, NH]], 0, 0, 12)
-    kq = T.tg[:, 4:5]
-    io("kq", kq, [[0, 1]], 0, 1, 1)
-    ms(T.cf[:, 0:3 * HC], -0.4375, ["cf"])
-    ms(T.cv[:, 4096:4112], 0.0, ["cvz"])
-    ts(sq("idb"), T.xr[:, 15:143], kq, None, ALU.is_equal, None, ["xr", "kq"], ["idb"], 128)
-    io("gr", T.gr[:], [[16, 8], [0, 16]], 0, 0, 128)
-    ts(zz("z1"), T.xr[:], G16, None, ALU.is_equal, None, ["xr", "pc"], ["z1"], 144)
-    ts(sq("bd"), T.gr[:], G16, None, ALU.is_equal, None, ["gr", "pc"], ["bd"], 128)
-    k2 = pcol("k2", K4, 2.0, 0.4375 / 8192, ALU.is_equal, ALU.mult, [])
-    k1 = pcol("k1", K4, 0.0, None, ALU.is_equal, None, [])
-    k0 = scol("k0", k1, 0.125, k2, ["k1", "k2"])
-    e15 = pcol("e15", U, 15.0, None, ALU.is_equal, None, [])
-    io("tg", T.tg[:, 0:3], [[1, 3]], 3, 0, 3)
-    ts(T.pe[:, 0:3], T.tg[:, 0:3], U, e15, ALU.is_equal, ALU.subtract, ["tg", "pc", "e15"], ["wq0", "wq1", "wq2"], 3)
-    wq = [T.pe[:, q:q + 1] for q in range(3)]
-    wa1 = pcol("wa1", U, 0.0, -2.0, ALU.is_equal, ALU.mult, [])
-    wa = scol("wa", e15, -7.0 / 2048, wa1, ["e15", "wa1"])
-    cX = scol("cX", e15, -8192.0, 6144.0, ["e15"])
-    if ON_S["yf"]:
-        cx0 = pcol("cx0", U, 6.0, 8192.0, ALU.is_lt, ALU.mult, [])
-        cXs = scol("cXs", cx0, 1.0, -2048.0, ["cx0"])
-    for nm, w, rd in (("z125", 0.125, []), ("z233", W, []), ("zl", k0, ["k0"])):
-        act(zz(nm), zz("z1"), ACT.Identity, 0.0, w, ["z1"] + rd, [nm], 144)
-    sv = 1.0
-    for nm, src, w, rd in ([("bd233", "bd", -W, []), ("idn", "idb", -1.0, []), ("idk", "idb", 4096.0, []), ("id16", "idb", 16.0, []),
-                            ("bda", "bd", wa, ["wa"]), ("bdf", "bd", -1.0, [])]
-                           + [("bdq%d" % q, "bd233", wq[q], ["wq%d" % q]) for q in range(3)]):
-        act(sq(nm), sq(src), ACT.Identity, 0.0, w, [src] + rd, [nm], 128)
-    ts(sq("bdk"), T.xr[:, 15:143], kq, -4096.0, ALU.is_gt, ALU.mult, ["xr", "kq"], ["bdk"], 128)
-    tt(sq("tr"), sq("bdk"), sq("bd"), ALU.mult, ["bdk", "bd"], ["tr"], 128)
-    tt(sq("tri"), sq("tr"), sq("idk"), ALU.add, ["tr", "idk"], ["tri"], 128)
-    act(sq("tri2"), sq("tri"), ACT.Identity, 0.0, 2.0, ["tri"], ["tri2"], 128)
-    cF = pcol("cF", U, -4096.0, None, ALU.mult, None, [])
-    cy0 = pcol("cy0", U, 4.0, 131072.0, ALU.is_lt, ALU.mult, [])
-    cY = scol("cY", cy0, 1.0, -73728.0, ["cy0"])
-    ms(T.gw0[:], 0.0, ["gw0"], 192)
-    for k, (q, rows, w) in enumerate(((0, slice(1, 3), 1), (0, slice(4, 6), 1), (1, slice(0, 4, 3), 1), (1, slice(2, 6, 3), -1),
-                                      (2, slice(0, 2), -1), (2, slice(3, 5), -1))):
-        io("gw0%d" % k, T.gw0[:, q, :, rows], [[0, 16]], w, 0, 16)
-        ops[-1]["rd"].append("gw0")
-    io("gw1", T.gw1[:], [[0, 8], [-2, 2], [0, 8]], 1, 0, 128)
-    io("gw1", T.gw1[:, :, 4:8], [[0, 32]], -1, 0, 32)
-    for q in range(3):
-        tt(T.gw[:, 128 * q:128 * q + 128], T.gw0[:, q], sq("bd"), ALU.mult, ["gw0%d" % (2 * q), "gw0%d" % (2 * q + 1), "bd"], ["gw%d_" % q], 128)
-    tt(sq("pfm"), T.gw1[:], sq("bd"), ALU.mult, ["gw1", "bd"], ["pfm"], 128)
-    io("cpg", sq("cpg"), [[16, 8], [1, 4], [0, 4]], -1, 0, 128)
-    kp2 = pcol("kp2", K4, 2.0, G16, ALU.min, ALU.add, [])
-    sg0 = scol("sg0", ODD, -8192.0 * sv, 4096.0 * sv, [])
-    sgn = pcol("sgn", U, 6.0, sg0, ALU.is_lt, ALU.mult, ["sg0"])
-    ts(sq("pg"), sq("cpg"), kp2, sgn, ALU.is_equal, ALU.mult, ["cpg", "kp2", "sgn"], ["pg"], 64)
-    pgs = ["pg2" if x == "V" else "pg" for x in SIGN_ON]
-    if "pg2" in pgs:
-        act(sq("pg2"), sq("pg"), ACT.Identity, 0.0, 2.0, ["pg"], ["pg2"], 128)
-    kp = scol("kp", K4, 1.0, G16, [])
+    def odd(name, base, cnt):
+        return A(name, SL[base + 1:base + 2 * cnt:2])
 
-    cd = T.codes; made = {"d": [], "s": [], "r": []}
-
-    def code(kind, out, pat, base, x, over=()):
-        made[kind].append("c%s%d" % (kind, len(made[kind])))
-        io(made[kind][-1], out, pat, base, 0, x)
-        ops[-1]["rd"] += list(over)
-    new = [4 * case + NEXT[case].index(4) for case in range(4)]
-    pairs = [slice(new[0], new[2] + 1, new[2] - new[0]), slice(new[1], new[3] + 1, new[3] - new[1])]
-    for case in range(4):
-        for b in range(3):
-            src = [source(case, PAIRS[3 * k + b]) for k in range(2)]
-            code("d", cd[:, MD + b, :, 4 * case:4 * case + 4], [[16, 8], [src[1] - src[0], 4]], src[0], 32)
-        code("s", cd[:, MS:MH, :, 4 * case:4 * case + 4], [[4, 3], [16, 8], [1, 4]], 2 + NEXT[case][0], 96)
-    made["s"].append("cs4"); ms(cd[:, MH:RF], -1.0, ["cs4"], 576)
-    code("d", cd[:, MD:MS, :, 2:16:4], [[0, 3], [16, 8], [0, 4]], 15, 96, made["d"][0:12])
-    for x in pairs:
-        code("s", cd[:, MS:MH, :, x], [[0, 48]], -1, 48, made["s"][0:4])
-        code("s", cd[:, MH:RD, :, x], [[1, 6], [16, 8], [0, 2]], 0, 96, made["s"][4:5])
-    for b in range(3):
-        code("r", cd[:, RD + b, :, b:6:3], [[16, 8], [1, 2]], 0, 16, ["cs4"])
-    io("cf2", cd[:, RF:NM], [[-4, 2], [16, 8], [1, 16]], -6, 0, 256)
-    for name, m0, m1, key, kn in (("d", MD, MS, kq, "kq"), ("s", MS, RD, kq, "kq"), ("r", RD, RF, kp, "kp")):
-        ts(T.mats[:, 128 * m0:128 * m1], cd[:, m0:m1], key, None, ALU.is_equal, None, made[name] + [kn], ["m" + name], 64 * (m1 - m0))
-    ts(T.rf[:], cd[:, RF:NM], kp, None, ALU.is_equal, None, ["cf2", "kp"], ["rf"], 128)
-    if ON_S["yf"]:
-        act(T.rff[:], T.rf[:], ACT.Identity, 0.0, 1.0, ["rf"], ["rff"], 256)
-    if ON_S["out"]:
-        act(T.zf[:], zz("z1"), ACT.Identity, 0.0, 1.0, ["z1"], ["zf"], 144)
-    U2 = scol("u2", U, 2.0, 0.0, [])
-    for h in range(2):
-        io("ci%d" % h, T.ci[:, NL * h:NL * h + NL], [[-1, 2], [0, NH], [2, 16]], h, 0, NL)
-    io("hb", T.hb[:], [[0, 4], [-8192, NH], [0, 16]], -8192, 0, 2 * NL)
-    ts(T.ci[:], T.ci[:], U2, -1.0, ALU.subtract, ALU.max, ["ci0", "ci1", "u2"], ["ci0", "ci1"], NL)
-    ts(T.ci[:], T.ci[:], 1.0, -8192.0, ALU.min, ALU.mult, ["ci0", "ci1"], ["ci0", "ci1"], NL)
-    tt(T.mask[:], T.ci[:], T.hb[:], ALU.add, ["ci0", "ci1", "hb"], ["mask"], 2 * NL)
-    io("jl0", T.jl0[:], [[0, 2], [16, 2], [TW, NH]], 464 - 2048, 0, 16)
-    act(T.jl[:], T.jl0[:], ACT.Identity, U, 1.0, ["jl0", "pc"], ["jl"], 16)
-
-    def columns(s, a, z, src, rd, add, out, wr):
-        ps, bank = psum(s, "col%d" % a); o = ps(0, 3 * HC)
-        mm([[(o, sq("idb"), T.cb[:, 0:3 * HC], 12)] + ([] if add else [(o, sq("idb"), T.cf[:, 0:3 * HC], 12)])
-            + [(o, esel(z, u), src(u), 12) for u in range(16)]], rd + [z, "idb", "cb", "cf"], bank)
-        ts(out, o, M23 + add, M23, ALU.add, ALU.subtract, [], [wr], 12, bank)
-
-    dp = T.dp
-    for s in range(NS):
-        for h in range(2):
-            sg(T.ovf[:, 512 * h:512 * h + 512] if s == 0 else T.ovg[:, 512 * h:512 * h + 512],
-               T.ob[:, 0:1024 * (h + 1)].indirect(T.il[:, 64 * s + 32 * h:64 * s + 32 * h + 32]), ["il", "ob0", "ob%d" % h], ["ov%d%d" % (s, h)], 512)
-    at = {}
-    for j0, d, cnt, x in [(0, 1, 3, 0), (0, 2, 2, 4), (0, 3, 1, 8), (4, 1, 3, 10), (4, 2, 2, 15), (4, 3, 1, 20), (3, 1, 1, 9), (2, 2, 2, 13), (1, 3, 3, 17), (0, 4, 4, 21), (0, 5, 3, 25), (0, 6, 2, 6), (0, 7, 1, 3)]:
-        for s, ov in enumerate((T.ovf, T.ovg)):
-            out = dp[:, x:x + cnt, NL * s:NL * s + NL]; in0 = ov[:, NL * j0:NL * (j0 + cnt)]; in1 = ov[:, NL * (j0 + d):NL * (j0 + d + cnt)]
-            rd = (["ov%d0" % s] if j0 < 4 else []) + (["ov%d1" % s] if j0 + d + cnt > 4 else [])
-            if d in SQUARED:
-                ps, bank = psum(s, "px1"); o = ps(0, NL * cnt)
-                mm([[(o, sq("idb"), in0, NL * cnt), (o, sq("idn"), in1, NL * cnt)]], rd + ["idb", "idn"], bank)
-                act(out, o, ACT.Square, 0.0, 1.0, [], ["dp%d_%d" % (x, s)], NL * cnt, bank)
-            else:
-                tt(out, in0, in1, ALU.mult, rd, ["dp%d_%d" % (x, s)], NL * cnt)
-        for k in range(cnt):
-            at[(j0 + k, j0 + k + d)] = (x + k, "dp%d_" % x)
-    if SQUARED:
-        for s, ov in enumerate((T.ovf, T.ovg)):
-            act(T.ovs[:, s], ov[:], ACT.Square, 0.0, 1.0, ["ov%d0" % s, "ov%d1" % s], ["ovs%d" % s], 1024)
-        for nm, w in (("zp", 0.5), ("zn", -0.5)):
-            act(zz(nm), zz("z1"), ACT.Identity, 0.0, w, ["z1"], [nm], 144)
-
-    def terms(o, r, pair, s):
-        src = dp[:, at[pair][0], NL * s:NL * s + NL]
-        if pair[1] - pair[0] not in SQUARED:
-            return [(o, esel("z1", r), src, NL)]
-        return [(o, esel("zn", r), src, NL)] + [(o, esel("zp", r), T.ovs[:, s, NL * j:NL * j + NL], NL) for j in pair]
-    ps, bank = psum(1, "px0")
-    mm([[(ps(0, 256), esel("z1", r), dp[:, at[pair][0], :], 256) for r, pair in enumerate(LATER)]],
-       ["z1"] + [at[pair][1] + str(s) for pair in LATER[0:3] for s in range(NS)], bank)
-    ts(T.hq[:, 0], ps(0, 256), -2048.0, None, ALU.add, None, [], ["h0"], 256, bank)
+    def star(j):
+        return A("ob", j)
+    for k in range(3):
+        tt(A("dpo", k), star(0), star(k + 1), ALU.mult)
+    mm([(ps(3, 0, 48), mat("idb"), A("cb", x)) for x in range(2)]
+       + [(ps(3, 0, 48), A("z8", SL[15 - v:143 - v]), A("dpo", SL[:, 4 * v:4 * v + 4])) for v in range(16)])
+    for p in range(4):
+        ts(A("coli", SL[0, p, 0:12]), ps(3, p, 48, 4), M23 + C0, M23, ALU.add, ALU.subtract)
+    packs = sorted(set(x[1:] for x in TWINS), key=lambda x: [v[1:] for v in TWINS].index(x))
+    for s in range(2):
+        for k0 in range(0, len(packs), 2):
+            b = ((0, 1, 2, 0, 1, 2), (4, 6, 3, 4, 6, 3))[s][k0 // 2]; c = 256 * (k0 // 6)
+            mm([(ps(b, c + 128 * k, c + 128 * k + 128), mat(m), A("ob", SL[j, :, 2 * s:2 * s + 2]))
+                for k in range(2) for m, j in zip(("idb", "id4k"), packs[k0 + k]) if j >= 0])
+            for r, x in enumerate(TWINS):
+                if x[1:] in packs[k0:k0 + 2]:
+                    k = packs.index(x[1:]) - k0
+                    tt(A("dpf", SL[:, r, 2 * s:2 * s + 2]), A("ob", SL[x[0], :, 2 * s:2 * s + 2]), ps(b, c + 128 * k, c + 128 * k + 128), ALU.mult)
+        o = ps(5 + 2 * s, 0, 128); hp = A("hq", SL[0, 128 * s:128 * s + 128])
+        mm([(o, mat(m), A("m16", 0)) for m in ("cq", "c35")]
+           + [(ps(5 + 2 * s, 64 * a + u, 64 * a + 64, 8), A("dpf", SL[8 * u:8 * u + 8, :, 2 * s + a]), A("wy", 1)) for a in range(2) for u in range(8)])
+        ts(hp, o, sh1, M23, ALU.add, ALU.subtract)
+        tt(A("lo", s), o, hp, ALU.subtract)
+        ts(A("lo", s), A("lo", s), sh0, 4096.0, ALU.add, ALU.mult)
+        ts(odd("xi%d" % s, 0, 128), A("lo", s), si, s2, ALU.add, ALU.subtract)
     for t in range(2):
-        rdma(T.hq[:, t + 1], T.hq[:, t], "ah%d" % (t + 1), ["h%d" % t], ["h%d" % (t + 1)], LAT_R + 3.0)
-        ops[-1]["dur"] += FIRST_HOLD * (1 - t)
-    rows = [list(enumerate(PAIRS)), []]
-    for j, (b, r0) in enumerate(STAR):
-        rows[b] += [(r0 + k, (k, 4 + j)) for k in range(4)]
-    for s in range(NS):
-        for a in range(2):
-            l0 = NL * s + HL * a
-            columns(s, a, "z125", lambda u: dp[:, 0:9:4, l0 + u:l0 + HL:16], ["dp%d_%d" % (x, s) for x in (0, 4, 8)], 0.0,
-                    T["coli_%d" % s][:, 0, a, 0:3 * HC], "col%d%d_0" % (s, a))
-        ps, bank = psum(s, "x0")
-        for b in range(2):
-            for k in range(0, len(rows[b]), 4):
-                part = rows[b][k:k + 4]
-                mm([[x for r, pair in part for x in terms(ps(NL * b, NL * b + NL), r, pair, s)]],
-                   ["z1", "zp", "zn", "ovs%d" % s] + sorted(set(at[pair][1] + str(s) for _, pair in part)), bank, k == 0, k + 4 >= len(rows[b]))
-        ts(T["xi_%d" % s][:, 0:2 * NL], ps(0, 2 * NL), -2048.0, None, ALU.add, None, [], ["x%d_0" % s, "q%d_0" % s], 2 * NL, bank)
+        for s in range(2):
+            rdma(A("hq", SL[t + 1, 128 * s:128 * s + 128]), A("hq", SL[t, 128 * s:128 * s + 128]), "ah%d%d" % (t + 1, s), "sent", 2.0)
+            ops[-1]["more"] = FIRST_HOLD * (t + s == 0)
 
+    cw = A("cv", SL[0:4112])
     for t in range(RO):
         last = t == RO - 1
-        for s in range(NS):
+        for s in range(2):
             tag[0], tag[1] = (s, t), len(ops)
-
-            def B(x):
-                return T["%s_%d" % (x, s)]
-
-            def R(x):
-                return "%s%d" % (x, s)
-
-            def both(x):
-                return [R(x + "0"), R(x + "1")]
-
-            def units(x, a, b):
-                return ["%s%d_%d" % (x, s, k) for k in range(a // 16, b // 16)]
-
-            def xin(a, b):
-                return B("xi")[:, XOFF[t] * NL + a:XOFF[t] * NL + b]
-            tb = B("tb")[:]
-            rx, rq = ["%s%d_%d" % (x, s, t) for x in ("x", "q")]; rh = "h%d" % t
-            rc = ["col%d%d_%d" % (s, a, t) for a in range(2)]
-            hq = T.hq[:, min(t, 2), NL * s:NL * s + NL]
-            nm, nmf, colf, f, y = B("nm16"), B("nmf"), B("colf"), B("f"), B("y")
-            wf = 3 - t
-            pd, bdd = psum(s, "d"); pso, bso = psum(s, "so"); py, by = psum(s, "y"); pxx, bxx = psum(s, "x")
-            cw = T.cv[:, 0:4112]; cvr = ["cvl", "cvz"]
+            xi, xo, tb, x0 = "xi%d" % s, "xo%d" % s, "tb%d" % s, XOFF[t]
+            bA, bB = 4 + 2 * s, 5 + 2 * s
             for a in range(2):
-                n0 = 3 * HL * a
-                if a < SPLIT_NM:
-                    cp(nm[:, n0:n0 + HL], tb.indirect(B("coli")[:, t, a, 0:HC]), [R("tb"), rc[a]], [R("nma%d" % a)], HL * RG, gath=True)
-                    cp(nm[:, n0 + HL:n0 + 3 * HL], tb.indirect(B("coli")[:, t, a, HC:3 * HC]), [R("tb"), rc[a]], [R("nmb%d" % a)], 2 * HL * RG, gath=True)
-                else:
-                    cp(nm[:, n0:n0 + 3 * HL], tb.indirect(B("coli")[:, t, a, 0:3 * HC]), [R("tb"), rc[a]], [R("nma%d" % a), R("nmb%d" % a)], 3 * HL * RG, gath=True)
-            ts(nmf[:], nm[:], -2048.0, None, ALU.add, None, both("nma") + both("nmb"), [R("nmf")], 3 * NL // 2)
-            if not last:
-                ca = B("coli")[:, t, :, 0:HC]
-                ts(colf[:, 0:NC], ca, -2048.0, None, ALU.add, None, rc, [R("colf")], 8)
-                dlst = [(pd(0, 2 * NL), sq("idb"), T.mask[:], 2 * NL)]
-                if DUP:
-                    ts(colf[:, NC:2 * NC], ca, -2048.0, None, ALU.add, None, rc, [R("colg")], 8)
-                    dlst += [(pd(u, 2 * NL, 16), sq("id16"), colf[:, 0:2 * NC], 8) for u in range(16)]
-                else:
-                    dlst += [(pd(NL * h + u, NL * h + NL, 16), sq("id16"), colf[:, 0:NC], 8) for h in range(2) for u in range(16)]
-                dlst += [(pd(NL * h + HL * c, NL * h + HL * c + HL), sq("bda"), xin(HL * h, HL * h + HL), HL) for h in range(2) for c in range(2)]
-                for k in range(0, len(dlst), 10):
-                    mm([dlst[k:k + 10]], [R("colf"), R("colg"), "idb", "mask", "id16"] + ([rx, "bda"] if k + 10 > len(dlst) - 4 else []), bdd, k == 0, False)
+                p = 2 * s + a; kind = KIND[t][p]; bk = 2 + a; n0 = 192 * p; y0 = 256 * p
 
-            for a in range(2):
-                px, bx = psum(s, "px%d" % a); pe, be = psum(s, "ev%d" % a); pf, bf = psum(s, "f%d" % a); pyd, byd = psum(s, "yd%d" % a)
-                l0 = HL * a; l1 = l0 + HL
+                def names(k, a0=0, z0=64):
+                    return ("ind", cw, A("nm", SL[n0 + 64 * k + a0:n0 + 64 * k + z0]))
+                cp(A("nm", SL[n0:n0 + 192]), ("ind", A(tb, SL[1024 * a:1024 * a + 1024]), A("coli", SL[t, p, 0:12])))
+                ops[-1]["at"] = t + p / 4
+                kind, nw, nt, cut = kind[0], int(kind[1]), int(kind[2]), kind[3]; npl = 4 - nt
 
-                def piece(x, p, q):
-                    return B(x)[:, 16 * (3 * l0 + p):16 * (3 * l0 + q)]
-
-                def names(p, q):
-                    return cw.indirect(nm[:, 3 * l0 + p:3 * l0 + q])
-                plan = PLAN.get((t, 2 * s + a), PLAIN)
-                nmr = cvr + [R("nma%d" % a), R("nmb%d" % a)]
-                for eng, p, q in plan[0]:
-                    wr = ["g%d%d_%d" % (s, a, k) for k in range(p // 16, q // 16)]
-                    if eng == "S":
-                        sg(piece("gv", p, q), names(p, q), nmr, wr, 16 * (q - p))
-                    else:
-                        cp(piece("gv", p, q), names(p, q), nmr, wr, 16 * (q - p) * RG, gath=True)
-                for e, (m0, m1) in enumerate(((0, 1), (0, 2), (1, 2))):
-                    for p, q in plan[1]:
-                        tt(piece("pr", HL * e + p, HL * e + q), piece("gv", HL * m0 + p, HL * m0 + q), piece("gv", HL * m1 + p, HL * m1 + q), ALU.mult,
-                           ["g%d%d_%d" % (s, a, 4 * m + k) for m in (m0, m1) for k in range(p // 16, q // 16)], units("pr%d" % e, l0 + p, l0 + q), 16 * (q - p))
-                    o = px(HL * e, HL * e + HL); c0 = 16 * HL * (3 * a + e)
-                    mm([[(o, esel("z233", p), B("pr")[:, c0 + p:c0 + 16 * HL:16], HL) for p in range(16)]],
-                       units("pr%d" % e, l0, l1) + ["z233"], bx, e == 0, e == 2)
-                    if e == 1:
-                        mm([[(px(HL * k, HL * k + HL), sq("bdq%d" % k), xin(l0, l1), HL) for k in range(3)]], ["bdq0", "bdq1", "bdq2", rx], bx, False, False)
-                nf = B("nf"); n0 = 3 * l0; rn, rv, rf = R("nf%d" % a), R("v%d" % a), R("f%d" % a)
-                if t in ON_S["abs"]:
-                    act(B("ab")[:, n0:n0 + 3 * HL], px(0, 3 * HL), ACT.Abs, 0.0, 1.0, [], [R("ab%d" % a)], 3 * HL, bx)
-                    ts(nf[:, n0:n0 + 3 * HL], B("ab")[:, n0:n0 + 3 * HL], 140.4 * W, None, ALU.is_gt, None, [R("ab%d" % a)], [rn], 3 * HL // 2)
+                def ab(k, r0, r1):
+                    return A("gab", SL[p, 1024 * k + 256 * r0:1024 * k + 256 * r1])
+                if nt == 0 and cut in "ab":
+                    act(A("gab", p), names(0, 0, 128), ACT.Copy, 0.0, 64.0)
+                elif npl:
+                    for k in range(2):
+                        act(ab(k, 0, npl), names(k, 0, 16 * npl), ACT.Copy, 0.0, 64.0)
+                if nt:
+                    act(ab(0, npl, 4), names(0, 16 * npl, 64), ACT.Copy, 0.0, 4096.0)
+                if nw:
+                    cp(A("gcc", SL[p, 0:256 * nw]), names(2, 0, 16 * nw))
+                for c0, c1 in ([(nw, npl)] if cut in "ac" or npl - nw < 2 else [(nw, npl - 1), (npl - 1, npl)]):
+                    if c1 > c0:
+                        act(A("gcc", SL[p, 256 * c0:256 * c1]), names(2, 16 * c0, 16 * c1), ACT.Copy)
+                ts(A("nmf", SL[s, :, :, a]), A("nm", SL[n0:n0 + 192]), -2048.0, None, ALU.add)
+                for r in range(4):
+                    tt(A("pab", SL[p, r:1024:4]), ab(1, r, r + 1) if r < npl else names(1, 16 * r, 16 * r + 16), ab(0, r, r + 1), ALU.mult)
+                mm([(ps(bk, u, 64, 8), A("pab", SL[p, 128 * u:128 * u + 128]), A("w8", 1)) for u in range(8)], True, False)
+                for h in range(2):
+                    r1 = min(2 * h + 2, npl)
+                    if kind == "P" and r1 > 2 * h:
+                        o = ps(h, 0, 256 * (r1 - 2 * h))
+                        mm([(o, mat("id64"), ab(0, 2 * h, r1)), (o, mat("i64"), ab(1, 2 * h, r1))])
+                    for r in range(2 * h, 2 * h + 2):
+                        o = A("yy", SL[p, r:1024:4]); q = SL[p, 256 * r:256 * r + 256]
+                        if kind == "U":
+                            for x in range(2):
+                                tt(A("pu", SL[p, x, r:1024:4]), A("gcc", q), ab(x, r, r + 1), ALU.mult)
+                        elif r < npl:
+                            tt(o, A("gcc", q), ps(h, 256 * (r % 2), 256 * (r % 2) + 256), ALU.mult)
+                        else:
+                            tt(A("xx", q), names(1, 16 * r, 16 * r + 16), ab(0, r, r + 1), ALU.add)
+                            tt(o, names(2, 16 * r, 16 * r + 16), A("xx", q), ALU.mult)
+                xp = odd(xi, x0 + 128 * a, 64)
+                if kind == "U":
+                    mm([(ps(bk, 64 * (h + 1) + u, 64 * (h + 2), 8), A("pu", SL[p, h, 128 * u:128 * u + 128]), A("w8", 3)) for h in range(2) for u in range(8)]
+                       + [(ps(bk, 64 * q, 64 * q + 64), A("mq", (0, 4, 5)[q]), xp) for q in range(3)], False, True)
+                    ts(A("nf", p), ps(bk, 0, 192), MAGIC, MAGIC, ALU.add, ALU.not_equal)
+                    fl = [A("nf", SL[p, 64 * q:64 * q + 64]) for q in range(3)]
                 else:
-                    ts(nf[:, n0:n0 + 3 * HL], px(0, 3 * HL), MAGIC, MAGIC, ALU.add, ALU.not_equal, [], [rn], 3 * HL, bx)
-                nfq = [nf[:, n0 + HL * k:n0 + HL * k + HL] for k in range(3)]
-                lst = [[(pe(0, HL), sq("idn"), nfq[k], HL) for k in range(3)]]
+                    mm([(ps(bk, 64 + u, 256, 8), A("yy", SL[p, 128 * u:128 * u + 128]), A("wy")) for u in range(8)]
+                       + [(ps(bk, 64 * q, 64 * q + 64), A("mq", q), xp) for q in range(4)], False, True)
+                    ts(A("nf", SL[p, 0:128]), ps(bk, 0, 128), MAGIC, MAGIC, ALU.add, ALU.not_equal)
+                    ts(A("rr", p), ps(bk, 128, 256), M23, M23, ALU.add, ALU.subtract)
+                    fl = [A("nf", SL[p, 0:64]), A("nf", SL[p, 64:128]), A("rr", SL[p, 0:64]), A("rr", SL[p, 64:128])]
+                mm([(ps(bk, 256, 320), mat(m), x) for m, x in zip(("pmn", "pmn", "pmn", "pm"), fl)]
+                   + ([] if last else [(ps(bk, 320, 384), mat(m), x) for m, x in zip(("gab", "gac", "gbc", "gbn"), fl)]))
+                nv = 64 if last else 128
+                if SIGN_ON[t] == "V":
+                    ts(odd("vb", y0, nv), ps(bk, 256, 256 + nv), 0.0, None, ALU.is_ge)
+                else:
+                    act(odd("vb", y0, nv), ps(bk, 256, 256 + nv), ACT.Sigmoid, 100.0, 200.0)
+                vh, vd = odd("vb", y0, 64), odd("vb", y0 + 128, 64)
                 if not last:
-                    lst.append([(pe(HL, 2 * HL), T.gw[:, 128 * k:128 * k + 128], nfq[k], HL) for k in range(3)])
-                mm(lst, [rn, "idn", "gw0_", "gw1_", "gw2_"], be)
-                nv = HL if last else 2 * HL
-                v = B("v")[:, 2 * l0:2 * l0 + nv]
-                tri = "tri"
-                if pgs[a] == "pg" and not last:
-                    act(v, pe(0, nv), ACT.Sign, 0.5, 1.0, [], [rv], nv, be)
-                else:
-                    ts(v, pe(0, nv), 0.0, 0.5, ALU.is_ge, ALU.subtract, [], [rv], nv, be)
-                    tri = "tri2"
-                mm([[(pf(0, HL), sq(tri), B("v")[:, 2 * l0:2 * l0 + HL], HL)]], [rv, tri], bf)
-                ts(f[:, l0:l1], pf(0, HL), cF, -4096.0, ALU.add, ALU.max, ["cF"], [rf], HL, bf)
-                if not last:
-                    lst = []
-                    for b in range(3):
-                        o = pyd(HL * b, HL * b + HL)
-                        lst.append([(o, mat(MD + b), xin(l0, l1), HL), (o, sq(pgs[a]), B("v")[:, 2 * l0 + HL:2 * l0 + 2 * HL], HL), (o, sq("pfm"), f[:, l0:l1], HL)])
-                    mm(lst, [rx, "md", rv, rf, pgs[a], "pfm"], byd)
-                    ts(y[:, n0:n0 + 3 * HL], pyd(0, 3 * HL), cY, -2048.0, ALU.add, ALU.max, ["cY"], [R("yd%d" % a)], 3 * HL, byd)
-                    co = B("colo")[:, t, a, 0:3 * HC]
-                    columns(s, a, "zl", lambda u: y[:, n0 + u:n0 + 3 * HL:16], [R("yd%d" % a)], 1024.0, co, R("co%d%d" % (a, t)))
-                    rdma(B("coli")[:, t + 1, a, 0:3 * HC], co, "a%s%d_%d" % ("cd"[a], t + 1, s), [R("co%d%d" % (a, t))],
-                         ["col%d%d_%d" % (s, a, t + 1)], LAT_R)
+                    mm([(ps(bk, 64 * b, 64 * b + 64), mat(m), x) for b in range(2) for m, x in ((("mdo", "mdd")[b], xp), ("pg", vd), ("pn", vh))])
+                    ts(odd("yb", y0, 128), ps(bk, 0, 128), cY, -2048.0, ALU.add, ALU.max)
+                    mm([(ps(bk, 384, 396), win(b, b0, x), A("wt", SL[k, :, 4 * x:4 * x + 4])) for k, b, b0 in ((1, xi, x0 + 128 * a), (0, "yb", y0)) for x in range(2)])
+                    co = A("colo", SL[t, p, 0:12])
+                    ts(co, ps(bk, 384, 396), M23 + 768 + C0, M23, ALU.add, ALU.subtract)
+                    rdma(A("coli", SL[t + 1, p, 0:12]), co, "ac%d_%d" % (t + 1, p), "sent", 0.0)
 
-            if not last:
-                mm([[(pxx(0, NL), sq("idb"), f[:], NL), (pxx(0, NL), sq("idb"), nmf[:, :, 0, :], NL)]], [R("nmf"), "idb"] + both("f"), bxx)
-                eq = B("eq"); so = B("so")
-                mm([[(pd(NL * h + HL * c, NL * h + HL * c + HL), sq("bdf"), f[:, HL * h:HL * h + HL], HL) for h in range(2) for c in range(2)]],
-                   both("f") + ["bdf"], bdd, False, True)
-                ts(eq[:], pd(0, 2 * NL), M27 - 28672.0, M27, ALU.add, ALU.is_equal, [], [R("eq")], 2 * NL, bdd)
-                if DUP_SO:
-                    o = pso(0, 2 * NC)
-                    mm([[(o, sq("idk"), eq[:, u:2 * NL:16], 8) for u in range(16)]
-                        + [(pso(NC * h, NC * h + NC), sq("idb"), colf[:, 0:NC], 8) for h in range(2)]], [R("eq"), R("colf"), "idb", "idk"], bso)
-                    tt(so[:, 16:16 + 2 * NC], o, T.jl[:, 0:2 * NC], ALU.min, ["jl"], [R("sp")], 8, bso)
-                    tt(so[:, 0:NC], so[:, 16:16 + NC], so[:, 16 + NC:16 + 2 * NC], ALU.max, [R("sp")], [R("so")], 8)
-                else:
-                    o = pso(0, NC)
-                    mm([[(o, sq("idb"), colf[:, 0:NC], 8)] + [(o, sq("idk"), eq[:, NL * h + u:NL * h + NL:16], 8) for h in range(2) for u in range(16)]],
-                       [R("eq"), R("colf"), "idb", "idk"], bso)
-                    tt(so[:, 0:NC], o, T.jl[:, 0:NC], ALU.min, ["jl"], [R("so")], 8, bso)
-                ts(B("so16")[:, 0:NC], so[:, 0:NC], 2048.0, None, ALU.add, None, [R("so")], [R("so16")], 8)
-                ts(B("ncol")[:], pxx(0, NL), 6144.0, 4096.0, ALU.add, ALU.min, [], [R("ncol")], NL, bxx)
-                cp(tb.indirect(B("so16")[:, 0:NC]), B("ncol")[:], [R("so16"), R("ncol")], [R("tb")], NL * RS, gath=True)
-                pyf, byf = psum(s, "yf"); pxo, bxo = psum(s, "xo"); x1 = XOFF[t + 1] * NL; x2 = XOFF[t + 2] * NL
-                if wf:
-                    lst = []
-                    for j in range(wf):
-                        b, r0 = STAR[j + 1]; o = pyf(NL * j, NL * j + NL)
-                        lst.append([(o, mat(MS + (r0 - 2) // 4), xin(NL * b, NL * b + NL), NL), (o, mat(MH + LATER.index((t + 4, t + 5 + j))), hq, NL),
-                                    (o, sq("pfm"), f[:], NL)]
-                                   + [(pyf(NL * j + HL * a, NL * j + HL * a + HL), sq(pgs[a]), B("v")[:, NL * a + HL:NL * a + NL], HL) for a in range(2)])
-                    mm(lst, [rx, rq, rh, "ms", "pfm"] + pgs + both("v") + both("f"), byf)
-                    ts(B("yf")[:, 0:wf * NL], pyf(0, NL * wf), cY, -2048.0, ALU.add, ALU.max, ["cY"], [R("yf")], NL * wf, byf)
-                lst = [[], [], []]
+            def state():
+                wf = 3 - t; hq = A("hq", SL[min(t, 2), 128 * s:128 * s + 128])
+                yo = [odd("yb", 256 * (2 * s + a), 64) for a in range(2)]
+                src = [("ms10", odd(xi, x0, 128)), ("ms6", odd(xi, x0 + 256, 128)) if t else ("mq6", hq), ("mq7", hq)]
+                lst = []
                 for j in range(wf):
-                    b = STAR[j][0]; k = (STAR[j][1] - 6) // 4
-                    lst[2 * b].append((pxo(NL * b, NL * b + NL), T.rf[:, 128 * k:128 * k + 128], B("yf")[:, NL * j:NL * (j + 1)], NL))
-                for a in range(2):
-                    lst[0 if wf else a] += [(pxo(HL * a, HL * a + HL), mat(RD + b), y[:, HL * (3 * a + b):HL * (3 * a + b + 1)], HL) for b in range(3)]
-                mm([x for x in lst if x], both("yd") + [R("yf"), "mr", "rf"], bxo)
-                ts(B("xo")[:, x1:x2], pxo(0, x2 - x1), cX, None, ALU.add, None, ["cX"], [R("xo%d" % t)], x2 - x1, bxo)
-                rdma(B("xi")[:, x1:x2], B("xo")[:, x1:x2], "ay%d_%d" % (t + 1, s), [R("xo%d" % t)],
-                     ["x%d_%d" % (s, t + 1), "q%d_%d" % (s, t + 1)], LAT_R + 0.5)
-            for m in range(3):
-                if last and s == NS - 1:
-                    for a in range(2):
-                        tt(T.mk[:, 8 * m + 4 * a:8 * m + 4 * a + 4, s, :], nmf[:, a, m, :], f[:, HL * a:HL * a + HL], ALU.min,
-                           [R("nmf"), R("f%d" % a)], ["mk%d%d%d" % (s, m, a)], HL)
+                    o = ps(bB, 128 * j, 128 * j + 128)
+                    lst += ([(o, mat(src[j][0]), src[j][1]), (o, mat("mh%d" % LATER.index((t + 4, t + 5 + j))), hq)]
+                            + [(ps(bB, 128 * j + 64 * a, 128 * j + 64 * a + 64), mat("pi"), yo[a]) for a in range(2)])
+                if wf:
+                    mm(lst)
+                    ts(A("yf", SL[s, 0:128 * wf]), ps(bB, 0, 128 * wf), -4096.0, -2048.0, ALU.add, ALU.max)
+                mm([(ps(bB, 0, 128), mat("mf"), odd(xi, x0, 128))]
+                   + [(ps(bB, 64 * a, 64 * a + 64), mat(m), x) for a in range(2)
+                      for m, x in (("rdo", yo[a]), ("rdd", odd("yb", 256 * (2 * s + a) + 128, 64)))]
+                   + [(ps(bB, 128 * (j // 2), 128 * (j // 2) + 128), mat(("rf6", "rf10")[j % 2]), A("yf", SL[s, 128 * j:128 * j + 128])) for j in range(wf)])
+                nx = 256 if t == 0 else 128
+                ts(odd(xo, 0, nx), ps(bB, 0, nx), sr, s2, ALU.add, ALU.subtract)
+                rdma(A(xi, SL[XOFF[t + 1]:XOFF[t + 1] + 2 * nx + 1]), A(xo, SL[0:2 * nx + 1]), "ay%d_%d" % (t + 1, s), "sx%d" % s, 0.5)
+
+            for grp in ([[0], [1]] if SPLIT_POST[t][s] == "1" else [[0, 1]]):
+                a0, a1 = grp[0], grp[-1] + 1
+                bH = 2 + a0 if len(grp) == 1 else bB; c1 = 448 - 64 * a1
+                lst = []
+                for a in grp:
+                    y0 = 256 * (2 * s + a)
+                    c0 = (64 if last else 128) * a
+                    lst += [(ps(bA, c0, c0 + 64), win("vb", y0, x), mat("hc", SL[4 * x:4 * x + 4])) for x in range(2)]
+                    if not last:
+                        lst += [(ps(bA, c0 + 64, c0 + 128), win(b, b0, x), mat(m, SL[4 * x:4 * x + 4]))
+                                for m, b, b0 in (("k0", xi, x0 + 128 * a), ("k3", "yb", y0)) for x in range(2)]
+                        if E_ON == "S":
+                            lst.append((ps(bA, c0, c0 + 128), mat("idb"), A("me")))
+                mm(lst)
+                if last:
+                    tt(A("ee", SL[s, a0:a1, 0]), ps(bA, 64 * a0, 64 * a1), A("m16", SL[0, a0:a1]), ALU.mult)
+                elif E_ON == "S":
+                    act(A("ee", SL[s, a0:a1]), ps(bA, 128 * a0, 128 * a1), ACT.Relu)
                 else:
-                    tt(T.mk[:, 8 * m:8 * m + 8, s, :], nmf[:, :, m, :], f[:], ALU.min, [R("nmf")] + both("f"), ["mk%d%d%d" % (s, m, a) for a in range(2)], NL)
-            if s == NS - 1:
-                o = py(0, 48)
-                mm([[(o, esel("z1", u), T.mk[:, :, :, u], 48) for u in range(16)]],
-                   ["mk%d%d%d" % (x, m, a) for x in range(NS) for m in range(3) for a in range(2)] + ["z1"], by)
-                ts(T.ybuf[:, 48 * t:48 * t + 48], o, 63488.0, -1.0, ALU.add, ALU.max, [], ["y%d" % t], 48, by)
+                    tt(A("ee", SL[s, a0:a1]), ps(bA, 128 * a0, 128 * a1), A("m16", SL[a0:a1]), ALU.mult)
+                mm([(ps(bH, c1 + 64 + 64 * a0, c1 + 64 + 64 * a1), mat("bd"), A("ee", SL[s, a0:a1, 0]))])
+                for a in grp:
+                    ts(A("fs", SL[s, :, a]), ps(bH, c1 + 64 + 64 * a, c1 + 128 + 64 * a), h1, h2, ALU.add, ALU.is_equal)
+                for m in range(3):
+                    b0 = a0 if m == 0 or last else 0
+                    if a1 == 2 or m == 0 or last:
+                        tt(A("mk", SL[m, :, 2 * s + b0:2 * s + a1]), A("nmf", SL[s, m, :, b0:a1]), A("fs", SL[s, :, b0:a1]), ALU.mult)
+                if last:
+                    for a in grp:
+                        mm([(top8(ps(bB, 192 * a + 64 * m + r, 192 * a + 64 * m + 64, 4)), A("w8", k), x) for m in range(3) for r in range(4)
+                            for k, x in ((2, A("fs", SL[s, r, a])), (0, A("mk", SL[m, r, 2 * s + a])))])
+                        ts(top8(A("yl", SL[:, 2 * s + a])), top8(ps(bB, 192 * a, 192 * a + 192)), -2048.0, -1.0, ALU.add, ALU.max)
+                    continue
+                w0, w1 = 4 * SG * a0, 4 * SG * a1
+                lst = []
+                for a in grp:
+                    o = ps(bA, 4 * SG * a, 4 * SG * (a + 1))
+                    lst += [(o, mat("idb"), A("cpd"))] + [(o, win(xi, x0 + 128 * a, x), A("wb", SL[4 * x:4 * x + 4])) for x in range(2)]
+                    lst += [(ps(bA, SG * (4 * a + r) + 2, SG * (4 * a + r) + 34), mat("bd"), A("ee", SL[s, a, 1, :, r % 2])) for r in range(4)]
+                mm(lst)
+                act(A("wab", SL[s, w0:w1]), ps(bA, w0, w1), ACT.Abs)
+                scan(A("scn", SL[s, w0:w1]), A("wab", SL[s, w0:w1]), A("d1", SL[0:4 * SG * len(grp)]), 0.0, ALU.min, ALU.add)
+                ts(A("so16", SL[s, 4 * a0:4 * a1]), A("scn", SL[s, w0 + SG - 1:w1:SG]), 256.0, None, ALU.mult)
+                mm([(ps(bH, c1 + 64 + 64 * a, c1 + 128 + 64 * a), mat(m), x) for a in grp
+                    for m, x in (("idb", A("nmf", SL[s, 0, :, a])), ("idn", A("mk", SL[0, :, 2 * s + a])), ("id2k", A("fs", SL[s, :, a])))])
+                ts(A("ncol", SL[s, 64 * a0:64 * a1]), ps(bH, c1 + 64 + 64 * a0, c1 + 64 + 64 * a1), 2048.0, None, ALU.add)
+                cp(("ind", A(tb, SL[1024 * a0:1024 * a1]), A("so16", SL[s, 4 * a0:4 * a1])), A("ncol", SL[s, 64 * a0:64 * a1]))
+            if not last:
+                state()
+        if last:
+            dma("Y", [(A("yn", SL[768 * t:768 * t + 768]), top8(A("yl")))], "out%d" % (3 * t), 2.0)
+            break
+        mm([(ps(7, 416 + p, 464, 4), win("yb", 256 * p, x), A("wt", SL[3, :, 4 * x:4 * x + 4])) for p in range(4) for x in range(2)]
+           + [(ps(7, 416, 464), A("z1", SL[15 - u:143 - u]), A("mk", SL[:, :, :, u])) for u in range(16)])
+        ts(A("ybuf", SL[48 * t:48 * t + 48]), ps(7, 416, 464), -2048.0, -1.0, ALU.add, ALU.max)
         for m in range(3):
             k = 3 * t + m
-            dma("S" if last and m == 1 else "Y", [(T.yn[:, 256 * k:256 * k + 256], T.ybuf[:, 16 * k:16 * k + 16])], ["y%d" % t], [], "out%d" % k, 2.0)
+            dma("S" if last and m == 1 else "Y", [(A("yn", SL[256 * k:256 * k + 256]), A("ybuf", SL[16 * k:16 * k + 16]))], "out%d" % k, 2.0)
     return ops
 
 
+def timing(o, c):
+    cy, pcy, rg, rs, _, _, lat_r, issue, way = c
+    k, x = o["kind"], o["x"]
+    dur = {"v": 0.015 + max(64, x) * cy, "vg": 0.05 + max(64, x * rg) * cy, "vs": 0.05 + max(64, x * rs) * cy, "s": 0.1 + max(64, x) * cy,
+           "sg": 0.065 + x * rg * cy, "g": 0.13 + 2 * x * cy, "p": 0.03 + x * pcy, "fix": x, "gd": issue, "rd": 0.3}[k]
+    return dur + o["more"], {"gd": way, "rd": lat_r + x}.get(k, o["lat"])
+
+
 def find_deps(ops):
-    writer, readers, bank = {}, {}, {}
+    writers, readers, bank = {}, {}, {}
     deps = []
     for i, o in enumerate(ops):
         d = {}
-        for r in o["rd"]:
-            if r in writer:
-                d[writer[r]] = True
-        for w in o["wr"]:
-            if w in writer:
-                d[writer[w]] = True
-            for j in readers.get(w, []):
-                d[j] = True
+        for a in o["wr"]:
+            m = cover(a)
+            for j, mj in readers.get(a[0], []):
+                if m & mj:
+                    d[j] = "a"
+        for a in o["rd"] + o["wr"]:
+            m = cover(a)
+            for j, mj in writers.get(a[0], []):
+                if m & mj:
+                    d[j] = "r"
         if o["bank"] is not None:
             if o["bank"] in bank:
-                d.setdefault(bank[o["bank"]], False)
+                d.setdefault(bank[o["bank"]], "s")
             bank[o["bank"]] = i
         for j in o.get("after", []):
-            d.setdefault(j, False)
+            d.setdefault(j, "s")
         d.pop(i, None)
         deps.append(d)
-        for r in o["rd"]:
-            readers.setdefault(r, []).append(i)
-        for w in o["wr"]:
-            writer[w] = i; readers[w] = []
+        for a in o["wr"]:
+            m = cover(a)
+            writers[a[0]] = [(j, mj & ~m) for j, mj in writers.get(a[0], []) if mj & ~m] + [(i, m)]
+            readers[a[0]] = [(j, mj & ~m) for j, mj in readers.get(a[0], []) if mj & ~m]
+        for a in o["rd"]:
+            readers.setdefault(a[0], []).append((i, cover(a)))
     return deps
 
 
-def order_queues(variants, deps):
-    ops = variants[0]; n = len(ops)
+def order_queues(ops, deps):
+    n = len(ops)
     eng = ["VSPGY".index(o["eng"]) for o in ops]
     tabs = []
-    for v, c in zip(variants, COSTS):
-        pre = [[(j, FIRST_CALL if j in v[i].get("after", []) and not h else v[j]["lat"] + c[4] if (eng[j] != eng[i] or (h and v[j]["sem"])) else (c[5] if h and eng[i] != 2 else 0.0))
+    for c in COSTS:
+        tm = [timing(o, c) for o in ops]
+        pre = [[(j, FIRST_CALL if j in ops[i].get("after", []) and h == "s" else
+                 (1.5 if h == "a" and ops[j]["arr"] else tm[j][1]) + c[4] if (eng[j] != eng[i] or (h != "s" and ops[j]["sem"])) else (c[5] if h != "s" and eng[i] != 2 else 0.0))
                 for j, h in deps[i].items()] for i in range(n)]
         suc = [[] for _ in range(n)]
         for i in range(n):
             for j, gp in pre[i]:
                 suc[j].append((i, gp))
-        tabs.append(([o["dur"] for o in v], [o["lat"] for o in v], pre, suc))
+        tabs.append(([x[0] for x in tm], [x[1] for x in tm], pre, suc))
 
     def place(seq, dur, edges, head):
         fin = [0.0] * n; busy = [([], []) for _ in range(5)]
@@ -603,17 +682,23 @@ def order_queues(variants, deps):
     rng = np.random.default_rng(SEED)
     scale = [w / c[0] / (1.0 + c[2]) for w, c in zip(WEIGHT, COSTS)]
     zero = [0.0] * n
-    dur, lat, pre, suc = tabs[0]
     best = None
     for it in range(SEARCH):
-        if it < 12:
-            key = [0.0 if o["typ"][0] is None else (6.0 + it) * (o["typ"][0][1] + o["typ"][0][0] / NS) + 0.01 * o["typ"][1] for o in ops]
+        dur, lat, pre, suc = tabs[PLACE[it % len(PLACE)]]
+        if it < 40:
+            key = [0.0] * n; per = 12.0 + it // 4
+            for i in range(n - 1, -1, -1):
+                key[i] = min([key[j] - gp for j, gp in suc[i]] + [RO * per + 3 - lat[i]]) - dur[i]
+                if "at" in ops[i]:
+                    key[i] = min(key[i], ops[i]["at"] * per)
         else:
-            size = float(rng.choice([0.1, 0.4, 1.5]))
-            noise = rng.normal(size=n) * size * (rng.random(n) < float(rng.choice([0.02, 0.1, 0.5])))
+            sz = float(rng.choice(NOISE))
+            noise = rng.normal(size=n) * sz * (rng.random(n) < float(rng.choice([0.02, 0.1, 0.5])))
+            if WINDOW:
+                noise = noise * (np.abs(np.array(best[2]) - rng.random() * 100) < WINDOW)
             key = [float(x) for x in np.array(best[2]) + noise]
         fin = place(legal(key, pre, True), dur, pre, zero)
-        for _ in range(2):
+        for _ in range(PASSES[it // 4 % len(PASSES)]):
             back = place(legal([-x for x in fin], suc, False), dur, suc, lat)
             fin = place(legal([-x for x in back], pre, True), dur, pre, zero)
         start = [fin[i] - dur[i] for i in range(n)]
@@ -651,10 +736,52 @@ def order_queues(variants, deps):
         if any(j in tied for j in deps[v]):
             return None
         return order[:pu] + ahead + [v, u] + behind + order[pv + 1:]
+
+    def tails(order, tab):
+        d, lt, _, sc_ = tab
+        tl = [0.0] * n; nx = [0.0] * 5
+        for i in reversed(order):
+            t0 = max(nx[eng[i]], lt[i])
+            for j, gp in sc_[i]:
+                if tl[j] + gp > t0:
+                    t0 = tl[j] + gp
+            tl[i] = nx[eng[i]] = t0 + d[i]
+        return tl
+
+    def bound(new, p0, p1, tab, fin, tl):
+        d, _, pr, sc_ = tab
+        loc = {}; free = {}; top_ = 0.0
+        for i in new[p0:p1 + 1]:
+            e = eng[i]
+            if e not in free:
+                q = p0 - 1
+                while q >= 0 and eng[new[q]] != e:
+                    q -= 1
+                free[e] = fin[new[q]] if q >= 0 else 0.0
+            t0 = free[e]
+            for j, gp in pr[i]:
+                f = loc.get(j, fin[j]) + gp
+                if f > t0:
+                    t0 = f
+            loc[i] = free[e] = t0 + d[i]
+        for i, f in loc.items():
+            for j, gp in sc_[i]:
+                if j not in loc and f + gp + tl[j] > top_:
+                    top_ = f + gp + tl[j]
+        for e, f in free.items():
+            q = p1 + 1
+            while q < n and eng[new[q]] != e:
+                q += 1
+            if q < n and f + tl[new[q]] > top_:
+                top_ = f + tl[new[q]]
+        return top_
     cur = best[1]; res = [replay(cur, tab) for tab in tabs]; csc = best[0]; top = (csc, cur)
+    tls = [tails(cur, tab) for tab in tabs]; ways = {}
     for it in range(SWAPS):
-        k = int(rng.integers(len(tabs)))
-        arcs = critical(cur, tabs[k], res[k][0])
+        k = int(rng.integers(2 * len(tabs)))
+        if k not in ways:
+            ways[k] = critical(cur, tabs[k // 2], res[k // 2][0])
+        arcs = ways[k]
         if not arcs:
             continue
         u, v = arcs[int(rng.integers(len(arcs)))]
@@ -679,10 +806,17 @@ def order_queues(variants, deps):
         p0 = 0
         while new[p0] == cur[p0]:
             p0 += 1
+        p1 = n - 1
+        while new[p1] == cur[p1]:
+            p1 -= 1
+        limit = csc + HEAT * (1.0 - it / SWAPS) * float(rng.exponential()) * scale[0]
+        if sum(bound(new, p0, p1, tab, r[0], tl) * w for tab, r, tl, w in zip(tabs, res, tls, scale)) > limit + 1e-9:
+            continue
         nres = [replay(new, tab, r[0], p0) for tab, r in zip(tabs, res)]
         sc = sum(r[1] * w for r, w in zip(nres, scale))
-        if sc <= csc + HEAT * (1.0 - it / SWAPS) * float(rng.exponential()) * scale[0]:
+        if sc <= limit:
             cur, res, csc = new, nres, sc
+            tls = [tails(cur, tab) for tab in tabs]; ways = {}
             if sc < top[0]:
                 top = (sc, cur)
     return top[1], [replay(top[1], tab) for tab in tabs]
@@ -691,44 +825,51 @@ def order_queues(variants, deps):
 def rank_program(g, core, T, topo):
     if T.rank_of(core) is None:
         return
-    variants = [build_ops(g, core, T, topo, c) for c in COSTS]
-    ops = variants[0]
-    deps = find_deps(ops)
+    ops = build_ops(g, core, T, topo)
     if "all" not in ORDER:
-        ORDER["all"] = order_queues(variants, deps)[0]
-    order = ORDER["all"]
+        ORDER["deps"] = find_deps(ops)
+        ORDER["all"], ORDER["times"] = order_queues(ops, ORDER["deps"])
+    order, deps = ORDER["all"], ORDER["deps"]
     queue = {"V": g.vector, "S": g.scalar, "P": g.tensor, "G": g, "Y": g.sync}
     pos = {i: k for k, i in enumerate(order)}
-    waits = {}; seen = {}; need = set()
+    waits = {}; seen = {e: {} for e in "VSPGY"}; knew = {}; need = set()
     for i in order:
         e = ops[i]["eng"]; w = {}
-        for j, hard in deps[i].items():
+        for j, h in deps[i].items():
             f = ops[j]["eng"]
-            if ops[j]["sem"] or (f == e and (e == "P" or not hard)):
+            if ops[j]["sem"] or (f == e and (e == "P" or h == "s")):
                 continue
-            if pos[j] > seen.get((e, f), -1) and pos[j] > pos.get(w.get(f), -1):
+            if pos[j] > seen[e].get(f, -1) and pos[j] > pos.get(w.get(f), -1):
                 w[f] = j
+        for f in list(w):
+            if any(x != f and knew[w[x]].get(f, -1) >= pos[w[f]] for x in w):
+                del w[f]
         for f, j in w.items():
-            seen[(e, f)] = pos[j]; need.add(j)
-        waits[i] = w
+            need.add(j)
+            for x, v in list(knew[j].items()) + [(f, pos[j])]:
+                seen[e][x] = max(seen[e].get(x, -1), v)
+        waits[i] = w; knew[i] = dict(seen[e])
+    ORDER["waits"] = sum(len(w) for w in waits.values())
     count = {}; num = {e: 0 for e in "VSPG"}
     for i in order:
         if i in need:
             num[ops[i]["eng"]] += 1; count[i] = num[ops[i]["eng"]]
-    done = set(); total = {}; waited = {}
+    done = {}; total = {}; waited = {}
     for i in order:
         o = ops[i]; e = o["eng"]; q = queue[e]
-        sems = [ops[j]["sem"] for j, hard in deps[i].items() if hard and ops[j]["sem"] and ops[j]["sem"][0] != "sent"] + o["ext"]
-        for (nm, v) in sems:
-            if (e, nm) not in done:
-                done.add((e, nm)); q.wait_ge(T.sem[nm], v); waited[nm] = v
+        for j, h in deps[i].items():
+            if h != "s" and ops[j]["sem"]:
+                nm, v = ops[j]["arr"] if h == "r" and ops[j]["arr"] else ops[j]["sem"]
+                if done.get((e, nm), 0) < v:
+                    done[(e, nm)] = v; q.wait_ge(T.sem[nm], v); waited[nm] = max(v, waited.get(nm, 0))
         for f, j in waits[i].items():
             q.wait_ge(T.sem["c" + f], count[j])
         ins = o["fn"]()
         if i in need:
             ins.then_inc(T.sem["c" + e], 1)
-        if o["sem"]:
-            total[o["sem"][0]] = total.get(o["sem"][0], 0) + o["sem"][1]
+        for x in (o["sem"], o["arr"]):
+            if x:
+                total[x[0]] = max(total.get(x[0], 0), x[1])
     for nm, v in total.items():
         if waited.get(nm, 0) < v:
             g.wait_ge(T.sem[nm], v)

import numpy as np
from concourse.mybir import AluOpType, ActivationFunctionType

ALU = AluOpType
ACT = ActivationFunctionType
RO, NB = 5, 451
W, W2 = 233.0, 233.25
MAGIC = 1.5 * 2.0 ** 39
M23, M26 = 1.5 * 2.0 ** 23, 1.5 * 2.0 ** 26
BIG = 8192.0
C0, CS = 64, 456
NEXT = [[1, 2, 3, 4], [0, 4, 2, 3], [0, 1, 2, 4], [0, 1, 4, 3]]
PAIRS = [(0, 1), (0, 2), (0, 3), (1, 2), (1, 3), (2, 3)]
LATER = [(4, 5), (4, 6), (4, 7), (5, 6), (5, 7), (6, 7)]
TWINS = [(0, 1, -1), (0, 2, 7), (0, 3, 6), (1, 2, 6), (1, 3, 7), (2, 3, 6), (4, 0, 5), (4, 1, 6), (4, 2, 7), (3, 4, 6),
         (5, 0, 6), (5, 1, 7), (2, 5, 7), (3, 5, 7), (6, -1, 7)]
QROW = {(min(x, z), max(x, z)): k for k, (x, y, z) in enumerate(TWINS) if z >= 0}
XW = [264, 520, 264, 264, 264]
XOFF = [0, 264, 784, 1048, 1312, 1576]
SG = 35

KIND = [x.split() for x in ("P00a P00a P00a P00a", "P00a P01a P00a P00a", "P00a P01a P00a P00a", "P00a P01a P00a P00a", "P01b P01b P01d P01d")]
SIGN_ON = "VVVVV"
E_ON = "V"
SCALE_V = ["mq", "wb", "hc", "ri", "pi", "k15", "k3", "k0"]
P_PART = 1400
C_CUT = [(0, 48), (48, 64)]
LOADS = [2.0, 2.6, 3.6, 5.8]
D_AT = [0, 2, 2, 2, 2]
ZERO_S = ["dpf", "yb", "vb", "xo0", "xo1", "mats13", "mats17"]
SPLIT_POST = ["11", "11", "11", "11", "11"]
FIRST_CALL = 1.0
FIRST_HOLD = 6.0
COSTS = [(0.00087, 0.00047, 1.45, 3.4, 0.25, 0.14, 4.8, 0.8, 2.5), (0.00087, 0.00045, 1.5, 3.8, 0.13, 0.08, 3.5, 0.8, 2.5),
         (0.00083, 0.00044, 1.1, 2.0, 0.17, 0.1, 4.0, 0.8, 2.5), (0.0011, 0.00055, 1.95, 5.0, 0.1, 0.06, 3.0, 0.8, 2.5)]
WEIGHT = [0.3, 1.2, 2.0, 0.7]
SEARCH = 8000
SEED = 1
SWAPS = 12000
HEAT = 0.05
PASSES = [1]
NOISE = [0.4, 1.5]
WINDOW = 5
PLACE = [0]
STEPS = [0, 0, 1, 2, 3, 5]
ORDER = {}

MATS = ["gab", "gac", "gbc", "c35", "rdo", "rdd", "ri", "pg", "mdo", "mdd", "mf", "ms6", "ms10", "mh0", "mh1", "mh2", "mh3", "mh4", "mh5", "mq6", "mq7",
        "id4k", "cq",
        "idb", "idn", "id2k", "bd", "pn", "hc", "k0", "k3", "pi", "gbn", "rf6", "rf10", "bdx", "bdy", "pm", "pmn", "id64", "i64"]
NZ = 21

SCRATCH = {
    "cv": ("sbuf", [128, 4112], "bfloat16"), "ob": ("sbuf", [128, 8, 64, 4], "bfloat16"),
    "dpf": ("sbuf", [128, 64, 16, 4], "float32"), "dpo": ("sbuf", [128, 3, 64, 4], "bfloat16"), "lo": ("sbuf", [128, 2, 128], "float32"),
    "gab": ("sbuf", [128, 4, 2048], "bfloat16"), "gcc": ("sbuf", [128, 4, 1024], "bfloat16"),
    "xx": ("sbuf", [128, 4, 1024], "float32"), "yy": ("sbuf", [128, 4, 1024], "float32"), "pab": ("sbuf", [128, 4, 1024], "bfloat16"),
    "coli": ("sbuf", [128, RO, 4, 16], "uint16"), "colo": ("sbuf", [128, RO, 4, 16], "uint16"), "nm": ("sbuf", [128, 768], "uint16"),
    "nf": ("sbuf", [128, 4, 192], "bfloat16"), "rr": ("sbuf", [128, 4, 128], "float16"),
    "vb": ("sbuf", [128, 1040], "bfloat16"), "yb": ("sbuf", [128, 1040], "float16"),
    "hq": ("sbuf", [128, 3, 256], "float16"), "ee": ("sbuf", [128, 2, 2, 2, 2, 2, 16], "float16"),
    "fs": ("sbuf", [128, 2, 4, 2, 16], "bfloat16"), "nmf": ("sbuf", [128, 2, 3, 4, 2, 16], "float16"), "mk": ("sbuf", [128, 3, 4, 4, 16], "float16"),
    "wab": ("sbuf", [128, 2, 2 * 4 * SG], "float16"), "scn": ("sbuf", [128, 2, 2 * 4 * SG], "float16"),
    "so16": ("sbuf", [128, 2, 8], "uint16"), "ncol": ("sbuf", [128, 2, 128], "int32"), "yf": ("sbuf", [128, 2, 384], "float16"),
    "ybuf": ("sbuf", [128, 48 * RO], "float32"),
    "mats": ("sbuf", [128, len(MATS), 8, 16], "bfloat16"), "mq": ("sbuf", [128, 6, 8, 16], "float16"),
    "wt": ("sbuf", [128, 4, 3, 8], "bfloat16"), "wb": ("sbuf", [128, 8, SG], "bfloat16"),
    "pu": ("sbuf", [128, 4, 2, 1024], "bfloat16"), "yl": ("sbuf", [128, 192, 4], "float32"), "w8": ("sbuf", [128, 4, 8], "bfloat16"), "wy": ("sbuf", [128, 3, 8], "float32"),
    "pidx": ("sbuf", [128, 8], "int32"), "pand": ("sbuf", [128, 8], "int32"), "pc": ("sbuf", [128, 64], "float32"),
    "xr": ("sbuf", [128, 144], "float32"), "xc": ("sbuf", [128, 8, 16], "bfloat16"), "gr": ("sbuf", [128, 8, 16], "bfloat16"), "z1": ("sbuf", [128, 144], "bfloat16"),
    "g8": ("sbuf", [128, 3, 8], "float32"), "c38": ("sbuf", [128, 3, 8], "float32"), "gm8": ("sbuf", [128, 3, 8], "float32"),
    "m16": ("sbuf", [128, 2, 2, 64], "bfloat16"), "pw": ("sbuf", [128, 2, 16], "float32"), "uge": ("sbuf", [128, 4], "float32"),
    "ci": ("sbuf", [128, 2, 2, 32], "bfloat16"), "cpd": ("sbuf", [128, 2, 2, SG], "float16"), "d1": ("sbuf", [128, 8 * SG], "float16"),
    "zz": ("sbuf", [128, 520], "bfloat16"), "me": ("sbuf", [128, 2, 64], "bfloat16"), "t4": ("sbuf", [128, 12], "float32"), "z8": ("sbuf", [128, 144], "bfloat16"), "cb": ("sbuf", [128, 2, 48], "bfloat16"),
}
for _s in range(2):
    SCRATCH["tb%d" % _s] = ("sbuf", [128, 2048], "int32")
    SCRATCH["xi%d" % _s] = ("sbuf", [128, XOFF[RO]], "float16")
    SCRATCH["xo%d" % _s] = ("sbuf", [128, 520], "float16")
for _b in range(8):
    SCRATCH["ps%d" % _b] = ("psum", [128, 512], "float32")

SEMAPHORES = (["cV", "cS", "cP", "cG", "lob0", "lob1", "lcv", "sent", "sx0", "sx1", "ah10", "ah11", "ah20", "ah21"] + ["lt%d" % p for p in range(4)]
              + ["ac%d_%d" % (t, p) for t in range(1, RO) for p in range(4)] + ["ay%d_%d" % (t, s) for t in range(1, RO) for s in range(2)]
              + ["out%d" % k for k in range(3 * RO - 2)])

SL = np.s_
MASKS = {}


def source(case, pair):
    x, y = sorted((NEXT[case][pair[0]], NEXT[case][pair[1]]))
    return 6 + x if y == 4 else PAIRS.index((x, y))


def cover(ap):
    key = (ap[0], str(ap[1]))
    if key not in MASKS:
        shape = SCRATCH[ap[0]][1][1:]
        hit = np.zeros(shape, bool); hit[ap[1][1:]] = True
        MASKS[key] = int.from_bytes(np.packbits(hit.ravel(), bitorder="little").tobytes(), "little")
    return MASKS[key]


def size(ap):
    return bin(cover(ap)).count("1")


def lines(entries):
    out = []; left = sorted(entries, key=lambda e: (e[2], e[1]))
    while left:
        r, c, w = left[0]; best = [left[0]]
        for r2, c2, w2 in left[1:]:
            if w2 == w and c2 > c:
                run = [left[0]]
                while (r + (r2 - r) * len(run), c + (c2 - c) * len(run), w) in left:
                    run.append((r + (r2 - r) * len(run), c + (c2 - c) * len(run), w))
                if len(run) > len(best):
                    best = run
        out.append(best); left = [e for e in left if e not in best]
    return out


def build_ops(g, core, T, topo):
    ops = []; tag = [None, 0]; first = []; sent = {}
    V, S, P = g.vector, g.scalar, g.tensor
    n = len(T.cores); rank = T.rank_of(core)
    nxt = T.cores[(rank + 1) % n]; prv = T.cores[(rank - 1) % n]

    def A(name, idx=()):
        return (name, (slice(None),) + (idx if isinstance(idx, tuple) else (idx,)))

    def top8(ap):
        return (ap[0], (slice(0, 8),) + ap[1][1:])

    def R(x):
        if not isinstance(x, tuple):
            return x
        if x[0] == "ind":
            return R(x[1]).indirect(R(x[2]))
        return T[x[0]][x[1]]

    def parts(lst):
        out = []
        for x in lst:
            if isinstance(x, tuple):
                out += [x[1], x[2]] if x[0] == "ind" else [x]
        return out

    def op(eng, fn, rd, wr, kind, x, sem=None, lat=0.0):
        rd = parts(rd); wi = [w for w in wr if w[0] == "ind"]
        rd += [w[2] for w in wi]; wr = [w[1] if w[0] == "ind" else w for w in wr]
        bank = [a[0] for a in rd + wr if a[0] in SCRATCH and SCRATCH[a[0]][0] == "psum"]
        ops.append({"eng": eng, "fn": fn, "rd": [a for a in rd if a[0] in SCRATCH and a[0] not in bank], "wr": [a for a in wr if a[0] in SCRATCH and a[0] not in bank],
                    "kind": kind, "x": x, "bank": bank[0] if bank else None, "sem": sem, "lat": lat, "arr": None, "more": 0.0,
                    "typ": (tag[0], len(ops) - tag[1])})

    def two(*aps):
        return all(SCRATCH[a[0]][2] in ("bfloat16", "float16", "uint16") for a in aps)

    def ts(out, in0, s1, s2, o0, o1=None):
        x = size(out) / (2 if two(out, in0) else 1)
        if o1 is None:
            op("V", lambda: V.tensor_scalar(R(out), R(in0), R(s1), None, o0), [in0, s1], [out], "v", x)
        else:
            op("V", lambda: V.tensor_scalar(R(out), R(in0), R(s1), R(s2), o0, o1), [in0, s1, s2], [out], "v", x)

    def tt(out, in0, in1, o):
        if in0[0] == "ind":
            kind, x = "vg", size(out)
        else:
            kind, x = "v", size(out) * (1 if two(out, in0, in1) or in0[0][0:2] == "ps" or in1[0][0:2] == "ps" else 2)
        op("V", lambda: V.tensor_tensor(R(out), R(in0), R(in1), o), [in0, in1], [out], kind, x)

    def cp(out, in_):
        kind, x = ("vs", size(in_)) if out[0] == "ind" else ("vg", size(out)) if in_[0] == "ind" else ("v", size(out))
        op("V", lambda: V.tensor_copy(R(out), R(in_)), [in_], [out], kind, x)

    def ms(ap, c):
        if ap[0] in ZERO_S or (ap[0] == "mats" and "mats%d" % ap[1][1].start in ZERO_S):
            return act(ap, A("zz", SL[0:size(ap)]), ACT.Copy)
        op("V", lambda: V.memset(R(ap), c), [], [ap], "v", size(ap) / (2 if two(ap) else 1))

    def scan(out, d0, d1, ini, o0, o1):
        op("V", lambda: V.tensor_tensor_scan(R(out), R(d0), R(d1), ini, o0, o1), [d0, d1], [out], "v", size(out) / (2 if two(out, d0, d1) else 1))

    def act(out, in_, func, bias=0.0, scale=1.0):
        if out[0] in SCALE_V or (out[0] == "mats" and MATS[out[1][1]] in SCALE_V):
            return ts(out, in_, scale, None, ALU.mult)
        op("S", lambda: S.activation(R(out), R(in_), func, bias=R(bias), scale=R(scale)), [in_, bias, scale], [out],
           "sg" if in_[0] == "ind" else "s", size(out))

    def io(out, pat, base, cm=0):
        if SCRATCH[out[0]][2] == "int32":
            op("G", lambda: g.iota(R(out), pat, base, cm), [], [out], "g", size(out))
        else:
            op("G", lambda: g.iota(R(out), pat, base, cm, allow_small_or_imprecise_dtypes=True), [], [out], "g", size(out))

    def put(ap, pat, base, w):
        op("G", lambda: g.affine_select(R(ap), R(ap), pat, ALU.not_equal, float(w), base, 1), [ap], [ap], "g", size(ap))
        ops[-1]["more"] = 0.04

    def mm(lst, start=True, stop=True):
        cyc = [max(min(64, size(l)), size(o)) * (4 if SCRATCH[l[0]][2] == "float32" else 1) for o, l, r in lst]
        if sum(cyc) > P_PART and len(lst) > 1:
            k = min(range(1, len(lst)), key=lambda x: abs(2 * sum(cyc[0:x]) - sum(cyc)))
            mm(lst[0:k], start, False); mm(lst[k:], False, stop)
            return

        def fn():
            ins = None
            for k, (o, l, r) in enumerate(lst):
                ins = P.matmul(R(o), R(l), R(r), start and k == 0, stop and k == len(lst) - 1)
            return ins
        op("P", fn, [x[1] for x in lst] + [x[2] for x in lst], [lst[0][0]], "p",
           sum(max(min(64, size(l)), size(o)) * (4 if SCRATCH[l[0]][2] == "float32" else 1) for o, l, r in lst))

    def dma(eng, pairs, sem, lat):
        q = {"Y": g.sync, "S": g.scalar}[eng]

        def fn():
            for (o, i) in pairs:
                q.dma_start(R(o), R(i)).then_inc(T.sem[sem], 16)
        op(eng, fn, [x[1] for x in pairs], [x[0] for x in pairs], "fix", 0.06 * len(pairs), sem=(sem, 16 * len(pairs)), lat=lat)
        ops[-1]["bank"] = "queue" + eng

    def gdma(out, in_, sem, add):
        if add:
            op("G", lambda: g.dma_start(R(out), R(in_), accum_op=ALU.add).then_inc(T.sem[sem], 16), [in_, out], [out], "gd", 0, sem=(sem, 16))
        else:
            op("G", lambda: g.dma_start(R(out), R(in_)).then_inc(T.sem[sem], 16), [in_], [out], "gd", 0, sem=(sem, 16))

    def rdma(out, in_, sem, local, more):
        rid, pid, _ = topo.addr(nxt)
        use = topo.engines(core, nxt)
        sent[local] = sent.get(local, 0) + len(use)
        op("G", lambda: g.remote_dma(R(out), R(in_), T.sem[sem], T.sem[local], pid, rid, sum(1 << e for e in use)), [in_], [out],
           "rd", more, sem=(local, sent[local]))
        ops[-1]["arr"] = (sem, len(topo.engines(prv, core)))
        ops[-1]["after"] = first[0:1]
        first.append(len(ops) - 1)

    def mat(name, idx=()):
        return A("mats", (MATS.index(name),) + (idx if isinstance(idx, tuple) else (idx,)))

    def ps(b, a, z, step=1):
        return A("ps%d" % b, SL[a:z:step])

    def tload(p, lat):
        dma("Y", [(A("tb%d" % (p // 2), SL[1024 * (p % 2) + C0 + CS * s:1024 * (p % 2) + C0 + CS * s + NB]), A("tsee", SL[NB * (4 * s + p):NB * (4 * s + p + 1)]))
                  for s in range(2)], "lt%d" % p, lat)
    dma("Y", [(A("ob", SL[0:4]), A("obs", SL[0:1024]))], "lob0", 2.0)
    dma("Y", [(A("ob", SL[4:8]), A("obs", SL[1024:2048]))], "lob1", 2.6)
    tload(0, 3.6)
    dma("Y", [(A("cv", SL[0:4096]), A("cvec"))], "lcv", 5.8)
    for p in range(1, 4):
        tload(p, 5.8 + p)

    ncol = [6]

    def pcol(in0, s1, s2, o0, o1=None):
        c = A("pc", SL[ncol[0]:ncol[0] + 1]); ncol[0] += 1
        ts(c, in0, s1, s2, o0, o1)
        return c
    U, K4, G16, KQ = [A("pc", SL[k:k + 1]) for k in range(4)]
    io(A("pidx", SL[0:1]), [[0, 1]], 0, 1)
    for k, a in enumerate((15, 3, 112, 127)):
        ts(A("pand", SL[k:k + 1]), A("pidx", SL[0:1]), a, None, ALU.bitwise_and)
    ts(A("pand", SL[4:5]), A("pidx", SL[0:1]), 64, None, ALU.bitwise_and)
    ts(A("pand", SL[5:6]), A("pidx", SL[0:1]), 2, 15, ALU.arith_shift_right, ALU.bitwise_and)
    cp(A("pc", SL[0:6]), A("pand", SL[0:6]))
    ky = pcol(K4, 16.0, A("pc", SL[4:5]), ALU.mult, ALU.add)
    io(mat("bdx"), [[64, 2], [0, 16], [16, 4]], 0)
    io(A("g8"), [[0, 3], [16, 8]], 0)
    io(A("gr"), [[16, 8], [0, 16]], 0)
    io(A("xc"), [[1, 128]], 0)
    io(A("m16"), [[0, 16], [1, 16]], 0)
    io(A("xr"), [[1, 144]], -15)
    io(A("c38"), [[1, 3], [16, 8]], 0)
    ms(A("zz"), 0.0)
    ms(A("dpf", SL[:, 15]), 0.0)
    ms(A("cv", SL[4096:4112]), 0.0)
    for a, b in ((7, 10), (0, 4), (4, 7), (10, 13), (13, 17), (17, NZ)):
        ms(A("mats", SL[a:b]), 0.0)
    ms(A("wt", 1), 0.0); ms(A("wb"), 0.0); ms(A("d1"), 0.0)
    for s in range(2):
        ms(A("xi%d" % s, SL[0:257:2]), 0.0); ms(A("xo%d" % s, SL[0:513:2]), 0.0)
    ms(A("vb", SL[0:1040:2]), 0.0); ms(A("yb", SL[0:1040:2]), 0.0)
    ts(A("w8", 0), A("g8", 0), G16, None, ALU.is_equal)
    ts(A("w8", 1), A("g8", 0), G16, W / 4096, ALU.is_equal, ALU.mult)
    ts(A("w8", 2), A("g8", 0), G16, 4096.0, ALU.is_equal, ALU.mult)
    ts(A("wy", 0), A("g8", 0), G16, W2 / 4096, ALU.is_equal, ALU.mult)
    ts(A("wy", SL[1:3]), A("g8", SL[1:3]), G16, 1.0 / 4096, ALU.is_equal, ALU.mult)
    if any(x[0] == "U" for y in KIND for x in y):
        act(A("w8", 3), A("w8", 1), ACT.Identity, 0.0, 64.0)
    ts(A("gm8"), A("g8"), G16, 0.125, ALU.is_equal, ALU.mult)
    ts(mat("bd"), A("gr"), G16, None, ALU.is_equal)
    ts(mat("idb"), A("xc"), KQ, None, ALU.is_equal)
    ts(mat("bdx"), mat("bdx"), G16, None, ALU.is_equal)
    ts(mat("bdy"), A("gr"), ky, None, ALU.is_equal)
    ts(mat("pm"), A("xc"), A("pc", SL[5:6]), ky, ALU.subtract, ALU.is_equal)
    ts(A("m16"), A("m16"), U, None, ALU.is_equal)

    def e(k):
        return A("m16", SL[0, 0, k:k + 1])
    s2 = pcol(e(0), M26, None, ALU.mult)
    si = pcol(e(14), 2049.0, pcol(s2, -256.0, None, ALU.add), ALU.mult, ALU.add)
    ts(A("uge", SL[0:3]), A("xr", SL[19:28:4]), U, None, ALU.is_le)
    sr = pcol(U, 6.0, -2048.0, ALU.is_lt, ALU.mult)
    sr = pcol(sr, 6144.0, s2, ALU.add, ALU.add)
    sr = pcol(e(15), -8192.0, pcol(e(14), -6143.0, sr, ALU.mult, ALU.add), ALU.mult, ALU.add)
    wq = [pcol(e(15), e(3), W, ALU.subtract, ALU.mult),
          pcol(e(14), -102.5, pcol(e(15), e(4), W2, ALU.subtract, ALU.mult), ALU.mult, ALU.add)]
    w5 = pcol(e(5), -1.0 / 4096, None, ALU.mult)
    for c, d in ((1800, -140.5), (1801, 140.5)):
        wq.append(pcol(e(14), d / 4096, pcol(e(15), c / 2048.0, w5, ALU.mult, ALU.add), ALU.mult, ALU.add))
    if any(x[0] == "U" for y in KIND for x in y):
        wq += [pcol(e(15), e(k), W, ALU.subtract, ALU.mult) for k in (4, 5)]
    for q in range(len(wq)):
        act(A("mq", q), mat("bdx"), ACT.Identity, 0.0, wq[q])
    k3 = pcol(K4, 3.0, None, ALU.is_equal)
    cb = pcol(A("uge", SL[0:1]), -2 * BIG, None, ALU.mult)
    cb = pcol(A("uge", SL[1:2]), 2 * BIG, cb, ALU.mult, ALU.add)
    cb = pcol(A("uge", SL[2:3]), -BIG, cb, ALU.mult, ALU.add)
    cY = pcol(k3, 2048.0, cb, ALU.mult, ALU.add)
    ts(A("pw", 0), A("xr", SL[15:31]), U, 0.25, ALU.is_ge, ALU.max)
    scan(A("pw", 1), A("pw", 0), A("xr", SL[0:16]), 2.0 ** 15, ALU.mult, ALU.max)
    hcol = A("pw", SL[1, 15:16])
    h1 = pcol(hcol, M23, None, ALU.mult); h2 = pcol(hcol, M23 + 1.0, None, ALU.mult)
    e0 = pcol(e(0), 1.0, None, ALU.mult)
    for nm, src, w in (("id64", "idb", 64.0), ("i64", "idb", 1.0 / 64), ("idn", "idb", -1.0), ("id2k", "idb", 2048.0), ("pn", "bd", -BIG), ("hc", "bd", hcol), ("k0", "bd", e0), ("k3", "bd", k3)):
        act(mat(nm), mat(src), ACT.Identity, 0.0, w)
    for nm, src, cols, w in (("c35", "bd", SL[:, 0:1], -3.5 / 4096), ("gab", "bdy", SL[:, 1:5], 1.0), ("gac", "bdy", SL[:, 0:6:5], 1.0), ("gac", "bdy", SL[:, 3:5], -1.0),
                             ("gbc", "bdy", SL[:, 0:3], -1.0), ("gbc", "bdy", SL[:, 5:6], -1.0), ("pmn", "pm", SL[:, :], -1.0), ("gbn", "gbc", SL[:, :], -1.0),
                             ("ri", "k3", SL[:, 0:6], -0.5)):
        act(mat(nm, cols), mat(src, cols), ACT.Identity, 0.0, w)
    for a, b, w in ((1, 2, 1.0 / 2048), (2, 18, -1.0), (18, 34, -1.0)):
        act(A("wb", SL[:, a:b]), mat("k0", SL[:, 0:b - a]), ACT.Identity, 0.0, w)
    kp = pcol(K4, G16, None, ALU.add)
    ts(mat("rdo", SL[:, 0:3]), A("xc", SL[:, 0:3]), kp, None, ALU.is_equal)
    tt(mat("rdo", SL[:, 0:6]), mat("rdo", SL[:, 0:6]), mat("ri", SL[:, 0:6]), ALU.add)
    io(mat("pi"), [[16, 8], [4, 4], [0, 4]], 3)
    for cols, w in ((SL[:, 0:4], -2.0), (SL[:, 4:16], 2.0)):
        ts(mat("pi", cols), mat("pi", cols), KQ, w, ALU.is_equal, ALU.mult)
    for nm, c, cols in (("rdd", 3.0, SL[:, 3:6]), ("rf6", 6.0, SL[:, :]), ("rf10", 10.0, SL[:, :])):
        ts(mat(nm, cols), A("xc", cols), c, kp, ALU.subtract, ALU.is_equal)
    ts(A("c38"), A("c38"), kp, pcol(k3, 0.5, None, ALU.mult), ALU.is_equal, ALU.subtract)
    tt(A("wt", 0), A("c38"), A("gm8"), ALU.mult)
    ts(A("wt", 3), A("gm8"), k3, -4.0, ALU.mult, ALU.mult)
    ts(A("z8"), A("xr"), G16, 0.125, ALU.is_equal, ALU.mult)
    act(A("z1"), A("z8"), ACT.Identity, 0.0, 8.0)
    io(A("cb", 0), [[0, 6], [CS, 2], [0, 4]], 0)
    ms(A("cb", 1), -0.4375)
    put(A("wt", 1), [[0, 3], [-16, 8]], -14, -0.4375)
    put(A("wt", SL[1, :, 1:8:2]), [[0, 3], [-32, 4]], -31, -CS / 2048.0)
    for run in lines([(source(0, PAIRS[k]), k, 0.125) for k in range(3)]):
        put(A("wt", SL[1, run[0][1]:run[-1][1] + 1]), [[run[0][0] - run[-1][0] if len(run) > 1 else 0, len(run)], [-16, 8]], -run[0][0], 0.125)

    def sparse(name, cnt, step, entries):
        k = MATS.index(name)
        for run in lines(entries):
            (r, c, w), m = run[0], len(run)
            dr, dc = (run[1][0] - r, run[1][1] - c) if m > 1 else (0, 1)
            put(A("mats", SL[k:k + cnt, :, c:c + dc * (m - 1) + 1:dc]), [[-step, cnt], [-16, 8], [-dr, m]], -r, w)
    sparse("pg", 1, 0, [(r, 4 * c + k, w * BIG) for r, c, w in ((0, 1, 1), (1, 1, 1), (2, 2, -1), (3, 2, -1), (4, 3, 1), (5, 3, -1)) for k in range(4)])
    for nm, b in (("mdo", 0), ("mdd", 3)):
        sparse(nm, 1, 0, [(source(c, PAIRS[b + k]), 4 * c + k, 1 if c else -1) for c in range(4) for k in range(3)])
    sparse("mf", 1, 0, [(source(0, PAIRS[k]), k, 1) for k in range(6)] + [(14, 0, -3.5)])
    sparse("ms6", 2, 4, [(6 + NEXT[c][k], 4 * c + k, 1) for c in range(4) for k in range(4) if NEXT[c][k] < 4])
    for x, cnt in ((0, 3), (3, 2), (5, 1)):
        sparse("mh%d" % x, cnt, 1, [(QROW[LATER[x]], 4 * c + NEXT[c].index(4), 1) for c in range(4)])
    for j in (6, 7):
        sparse("mq%d" % j, 1, 0, [(QROW[(NEXT[c][k], j)], 4 * c + k, 1) for c in range(4) for k in range(4) if NEXT[c][k] < 4])
    ts(mat("id4k"), A("xc"), KQ, 4096.0, ALU.is_equal, ALU.mult)
    act(mat("cq"), mat("bd"), ACT.Identity, 0.0, -0.4375)
    sh0 = pcol(e(0), 2048.0, -2048.0, ALU.mult, ALU.add)
    sh1 = pcol(sh0, M23, None, ALU.add)
    for b in range(2):
        io(A("ci", b), [[0, 2], [1, 2], [2, 16]], -b)
    ts(A("ci"), A("ci"), pcol(U, 2.0, None, ALU.mult), -1.0, ALU.subtract, ALU.max)
    if E_ON == "S":
        ts(A("ci"), A("ci"), 1.0, 1.25, ALU.min, ALU.add)
        ts(A("cpd", SL[:, :, 2:34]), A("ci"), -BIG, None, ALU.mult)
        for q in range(2):
            act(A("me", q), A("m16", SL[0, 0]), ACT.Identity, -65536.0, 65536.0 + 10240 * q)
    else:
        ts(A("cpd", SL[:, :, 2:34]), A("ci"), 1.0, -BIG, ALU.min, ALU.mult)
    ms(A("cpd", SL[:, :, 0:1]), 0.0); ms(A("cpd", SL[:, :, 34:35]), 16.0); ms(A("d1", SL[0:8 * SG:SG]), 16.0)
    io(A("t4", SL[0:4]), [[-32, 2], [CS - 16, 2]], 256 + C0)
    io(A("t4", SL[4:12]), [[1024, 2], [16, 4]], 0)
    ts(A("cpd", SL[:, :, 1:2]), A("t4", SL[0:4]), U, 1.0 / 256, ALU.subtract, ALU.mult)
    ts(A("d1", SL[34:8 * SG:SG]), A("t4", SL[4:12]), U, 1.0 / 256, ALU.add, ALU.mult)

    def win(name, base, e):
        return A(name, SL[base + 1 - e:base + 129 - e])

    def odd(name, base, cnt):
        return A(name, SL[base + 1:base + 2 * cnt:2])

    def star(j):
        return A("ob", j)
    for k in range(3):
        tt(A("dpo", k), star(0), star(k + 1), ALU.mult)
    mm([(ps(3, 0, 48), mat("idb"), A("cb", x)) for x in range(2)]
       + [(ps(3, 0, 48), A("z8", SL[15 - v:143 - v]), A("dpo", SL[:, 4 * v:4 * v + 4])) for v in range(16)])
    for p in range(4):
        ts(A("coli", SL[0, p, 0:12]), ps(3, p, 48, 4), M23 + C0, M23, ALU.add, ALU.subtract)
    packs = sorted(set(x[1:] for x in TWINS), key=lambda x: [v[1:] for v in TWINS].index(x))
    for s in range(2):
        for k0 in range(0, len(packs), 2):
            b = ((0, 1, 2, 0, 1, 2), (4, 6, 3, 4, 6, 3))[s][k0 // 2]; c = 256 * (k0 // 6)
            mm([(ps(b, c + 128 * k, c + 128 * k + 128), mat(m), A("ob", SL[j, :, 2 * s:2 * s + 2]))
                for k in range(2) for m, j in zip(("idb", "id4k"), packs[k0 + k]) if j >= 0])
            for r, x in enumerate(TWINS):
                if x[1:] in packs[k0:k0 + 2]:
                    k = packs.index(x[1:]) - k0
                    tt(A("dpf", SL[:, r, 2 * s:2 * s + 2]), A("ob", SL[x[0], :, 2 * s:2 * s + 2]), ps(b, c + 128 * k, c + 128 * k + 128), ALU.mult)
        o = ps(5 + 2 * s, 0, 128); hp = A("hq", SL[0, 128 * s:128 * s + 128])
        mm([(o, mat(m), A("m16", 0)) for m in ("cq", "c35")]
           + [(ps(5 + 2 * s, 64 * a + u, 64 * a + 64, 8), A("dpf", SL[8 * u:8 * u + 8, :, 2 * s + a]), A("wy", 1)) for a in range(2) for u in range(8)])
        ts(hp, o, sh1, M23, ALU.add, ALU.subtract)
        tt(A("lo", s), o, hp, ALU.subtract)
        ts(A("lo", s), A("lo", s), sh0, 4096.0, ALU.add, ALU.mult)
        ts(odd("xi%d" % s, 0, 128), A("lo", s), si, s2, ALU.add, ALU.subtract)
    for t in range(2):
        for s in range(2):
            rdma(A("hq", SL[t + 1, 128 * s:128 * s + 128]), A("hq", SL[t, 128 * s:128 * s + 128]), "ah%d%d" % (t + 1, s), "sent", 2.0)
            ops[-1]["more"] = FIRST_HOLD * (t + s == 0)

    cw = A("cv", SL[0:4112])
    for t in range(RO):
        last = t == RO - 1
        for s in range(2):
            tag[0], tag[1] = (s, t), len(ops)
            xi, xo, tb, x0 = "xi%d" % s, "xo%d" % s, "tb%d" % s, XOFF[t]
            bA, bB = 4 + 2 * s, 5 + 2 * s
            for a in range(2):
                p = 2 * s + a; kind = KIND[t][p]; bk = 2 + a; n0 = 192 * p; y0 = 256 * p

                def names(k, a0=0, z0=64):
                    return ("ind", cw, A("nm", SL[n0 + 64 * k + a0:n0 + 64 * k + z0]))
                cp(A("nm", SL[n0:n0 + 192]), ("ind", A(tb, SL[1024 * a:1024 * a + 1024]), A("coli", SL[t, p, 0:12])))
                ops[-1]["at"] = t + p / 4
                kind, nw, nt, cut = kind[0], int(kind[1]), int(kind[2]), kind[3]; npl = 4 - nt

                def ab(k, r0, r1):
                    return A("gab", SL[p, 1024 * k + 256 * r0:1024 * k + 256 * r1])
                if nt == 0 and cut in "ab":
                    act(A("gab", p), names(0, 0, 128), ACT.Copy, 0.0, 64.0)
                elif npl:
                    for k in range(2):
                        act(ab(k, 0, npl), names(k, 0, 16 * npl), ACT.Copy, 0.0, 64.0)
                if nt:
                    act(ab(0, npl, 4), names(0, 16 * npl, 64), ACT.Copy, 0.0, 4096.0)
                if nw:
                    cp(A("gcc", SL[p, 0:256 * nw]), names(2, 0, 16 * nw))
                for c0, c1 in ([(nw, npl)] if cut in "ac" or npl - nw < 2 else [(nw, npl - 1), (npl - 1, npl)]):
                    if c1 > c0:
                        act(A("gcc", SL[p, 256 * c0:256 * c1]), names(2, 16 * c0, 16 * c1), ACT.Copy)
                ts(A("nmf", SL[s, :, :, a]), A("nm", SL[n0:n0 + 192]), -2048.0, None, ALU.add)
                for r in range(4):
                    tt(A("pab", SL[p, r:1024:4]), ab(1, r, r + 1) if r < npl else names(1, 16 * r, 16 * r + 16), ab(0, r, r + 1), ALU.mult)
                mm([(ps(bk, u, 64, 8), A("pab", SL[p, 128 * u:128 * u + 128]), A("w8", 1)) for u in range(8)], True, False)
                for h in range(2):
                    r1 = min(2 * h + 2, npl)
                    if kind == "P" and r1 > 2 * h:
                        o = ps(h, 0, 256 * (r1 - 2 * h))
                        mm([(o, mat("id64"), ab(0, 2 * h, r1)), (o, mat("i64"), ab(1, 2 * h, r1))])
                    for r in range(2 * h, 2 * h + 2):
                        o = A("yy", SL[p, r:1024:4]); q = SL[p, 256 * r:256 * r + 256]
                        if kind == "U":
                            for x in range(2):
                                tt(A("pu", SL[p, x, r:1024:4]), A("gcc", q), ab(x, r, r + 1), ALU.mult)
                        elif r < npl:
                            tt(o, A("gcc", q), ps(h, 256 * (r % 2), 256 * (r % 2) + 256), ALU.mult)
                        else:
                            tt(A("xx", q), names(1, 16 * r, 16 * r + 16), ab(0, r, r + 1), ALU.add)
                            tt(o, names(2, 16 * r, 16 * r + 16), A("xx", q), ALU.mult)
                xp = odd(xi, x0 + 128 * a, 64)
                if kind == "U":
                    mm([(ps(bk, 64 * (h + 1) + u, 64 * (h + 2), 8), A("pu", SL[p, h, 128 * u:128 * u + 128]), A("w8", 3)) for h in range(2) for u in range(8)]
                       + [(ps(bk, 64 * q, 64 * q + 64), A("mq", (0, 4, 5)[q]), xp) for q in range(3)], False, True)
                    ts(A("nf", p), ps(bk, 0, 192), MAGIC, MAGIC, ALU.add, ALU.not_equal)
                    fl = [A("nf", SL[p, 64 * q:64 * q + 64]) for q in range(3)]
                else:
                    mm([(ps(bk, 64 + u, 256, 8), A("yy", SL[p, 128 * u:128 * u + 128]), A("wy")) for u in range(8)]
                       + [(ps(bk, 64 * q, 64 * q + 64), A("mq", q), xp) for q in range(4)], False, True)
                    ts(A("nf", SL[p, 0:128]), ps(bk, 0, 128), MAGIC, MAGIC, ALU.add, ALU.not_equal)
                    ts(A("rr", p), ps(bk, 128, 256), M23, M23, ALU.add, ALU.subtract)
                    fl = [A("nf", SL[p, 0:64]), A("nf", SL[p, 64:128]), A("rr", SL[p, 0:64]), A("rr", SL[p, 64:128])]
                mm([(ps(bk, 256, 320), mat(m), x) for m, x in zip(("pmn", "pmn", "pmn", "pm"), fl)]
                   + ([] if last else [(ps(bk, 320, 384), mat(m), x) for m, x in zip(("gab", "gac", "gbc", "gbn"), fl)]))
                nv = 64 if last else 128
                if SIGN_ON[t] == "V":
                    ts(odd("vb", y0, nv), ps(bk, 256, 256 + nv), 0.0, None, ALU.is_ge)
                else:
                    act(odd("vb", y0, nv), ps(bk, 256, 256 + nv), ACT.Sigmoid, 100.0, 200.0)
                vh, vd = odd("vb", y0, 64), odd("vb", y0 + 128, 64)
                if not last:
                    mm([(ps(bk, 64 * b, 64 * b + 64), mat(m), x) for b in range(2) for m, x in ((("mdo", "mdd")[b], xp), ("pg", vd), ("pn", vh))])
                    ts(odd("yb", y0, 128), ps(bk, 0, 128), cY, -2048.0, ALU.add, ALU.max)
                    mm([(ps(bk, 384, 396), win(b, b0, x), A("wt", SL[k, :, 4 * x:4 * x + 4])) for k, b, b0 in ((1, xi, x0 + 128 * a), (0, "yb", y0)) for x in range(2)])
                    co = A("colo", SL[t, p, 0:12])
                    ts(co, ps(bk, 384, 396), M23 + 768 + C0, M23, ALU.add, ALU.subtract)
                    rdma(A("coli", SL[t + 1, p, 0:12]), co, "ac%d_%d" % (t + 1, p), "sent", 0.0)

            def state():
                wf = 3 - t; hq = A("hq", SL[min(t, 2), 128 * s:128 * s + 128])
                yo = [odd("yb", 256 * (2 * s + a), 64) for a in range(2)]
                src = [("ms10", odd(xi, x0, 128)), ("ms6", odd(xi, x0 + 256, 128)) if t else ("mq6", hq), ("mq7", hq)]
                lst = []
                for j in range(wf):
                    o = ps(bB, 128 * j, 128 * j + 128)
                    lst += ([(o, mat(src[j][0]), src[j][1]), (o, mat("mh%d" % LATER.index((t + 4, t + 5 + j))), hq)]
                            + [(ps(bB, 128 * j + 64 * a, 128 * j + 64 * a + 64), mat("pi"), yo[a]) for a in range(2)])
                if wf:
                    mm(lst)
                    ts(A("yf", SL[s, 0:128 * wf]), ps(bB, 0, 128 * wf), -4096.0, -2048.0, ALU.add, ALU.max)
                mm([(ps(bB, 0, 128), mat("mf"), odd(xi, x0, 128))]
                   + [(ps(bB, 64 * a, 64 * a + 64), mat(m), x) for a in range(2)
                      for m, x in (("rdo", yo[a]), ("rdd", odd("yb", 256 * (2 * s + a) + 128, 64)))]
                   + [(ps(bB, 128 * (j // 2), 128 * (j // 2) + 128), mat(("rf6", "rf10")[j % 2]), A("yf", SL[s, 128 * j:128 * j + 128])) for j in range(wf)])
                nx = 256 if t == 0 else 128
                ts(odd(xo, 0, nx), ps(bB, 0, nx), sr, s2, ALU.add, ALU.subtract)
                rdma(A(xi, SL[XOFF[t + 1]:XOFF[t + 1] + 2 * nx + 1]), A(xo, SL[0:2 * nx + 1]), "ay%d_%d" % (t + 1, s), "sx%d" % s, 0.5)

            for grp in ([[0], [1]] if SPLIT_POST[t][s] == "1" else [[0, 1]]):
                a0, a1 = grp[0], grp[-1] + 1
                bH = 2 + a0 if len(grp) == 1 else bB; c1 = 448 - 64 * a1
                lst = []
                for a in grp:
                    y0 = 256 * (2 * s + a)
                    c0 = (64 if last else 128) * a
                    lst += [(ps(bA, c0, c0 + 64), win("vb", y0, x), mat("hc", SL[4 * x:4 * x + 4])) for x in range(2)]
                    if not last:
                        lst += [(ps(bA, c0 + 64, c0 + 128), win(b, b0, x), mat(m, SL[4 * x:4 * x + 4]))
                                for m, b, b0 in (("k0", xi, x0 + 128 * a), ("k3", "yb", y0)) for x in range(2)]
                        if E_ON == "S":
                            lst.append((ps(bA, c0, c0 + 128), mat("idb"), A("me")))
                mm(lst)
                if last:
                    tt(A("ee", SL[s, a0:a1, 0]), ps(bA, 64 * a0, 64 * a1), A("m16", SL[0, a0:a1]), ALU.mult)
                elif E_ON == "S":
                    act(A("ee", SL[s, a0:a1]), ps(bA, 128 * a0, 128 * a1), ACT.Relu)
                else:
                    tt(A("ee", SL[s, a0:a1]), ps(bA, 128 * a0, 128 * a1), A("m16", SL[a0:a1]), ALU.mult)
                mm([(ps(bH, c1 + 64 + 64 * a0, c1 + 64 + 64 * a1), mat("bd"), A("ee", SL[s, a0:a1, 0]))])
                for a in grp:
                    ts(A("fs", SL[s, :, a]), ps(bH, c1 + 64 + 64 * a, c1 + 128 + 64 * a), h1, h2, ALU.add, ALU.is_equal)
                for m in range(3):
                    b0 = a0 if m == 0 or last else 0
                    if a1 == 2 or m == 0 or last:
                        tt(A("mk", SL[m, :, 2 * s + b0:2 * s + a1]), A("nmf", SL[s, m, :, b0:a1]), A("fs", SL[s, :, b0:a1]), ALU.mult)
                if last:
                    for a in grp:
                        mm([(top8(ps(bB, 192 * a + 64 * m + r, 192 * a + 64 * m + 64, 4)), A("w8", k), x) for m in range(3) for r in range(4)
                            for k, x in ((2, A("fs", SL[s, r, a])), (0, A("mk", SL[m, r, 2 * s + a])))])
                        ts(top8(A("yl", SL[:, 2 * s + a])), top8(ps(bB, 192 * a, 192 * a + 192)), -2048.0, -1.0, ALU.add, ALU.max)
                    continue
                w0, w1 = 4 * SG * a0, 4 * SG * a1
                lst = []
                for a in grp:
                    o = ps(bA, 4 * SG * a, 4 * SG * (a + 1))
                    lst += [(o, mat("idb"), A("cpd"))] + [(o, win(xi, x0 + 128 * a, x), A("wb", SL[4 * x:4 * x + 4])) for x in range(2)]
                    lst += [(ps(bA, SG * (4 * a + r) + 2, SG * (4 * a + r) + 34), mat("bd"), A("ee", SL[s, a, 1, :, r % 2])) for r in range(4)]
                mm(lst)
                act(A("wab", SL[s, w0:w1]), ps(bA, w0, w1), ACT.Abs)
                scan(A("scn", SL[s, w0:w1]), A("wab", SL[s, w0:w1]), A("d1", SL[0:4 * SG * len(grp)]), 0.0, ALU.min, ALU.add)
                ts(A("so16", SL[s, 4 * a0:4 * a1]), A("scn", SL[s, w0 + SG - 1:w1:SG]), 256.0, None, ALU.mult)
                mm([(ps(bH, c1 + 64 + 64 * a, c1 + 128 + 64 * a), mat(m), x) for a in grp
                    for m, x in (("idb", A("nmf", SL[s, 0, :, a])), ("idn", A("mk", SL[0, :, 2 * s + a])), ("id2k", A("fs", SL[s, :, a])))])
                ts(A("ncol", SL[s, 64 * a0:64 * a1]), ps(bH, c1 + 64 + 64 * a0, c1 + 64 + 64 * a1), 2048.0, None, ALU.add)
                cp(("ind", A(tb, SL[1024 * a0:1024 * a1]), A("so16", SL[s, 4 * a0:4 * a1])), A("ncol", SL[s, 64 * a0:64 * a1]))
            if not last:
                state()
        if last:
            dma("Y", [(A("yn", SL[768 * t:768 * t + 768]), top8(A("yl")))], "out%d" % (3 * t), 2.0)
            break
        mm([(ps(7, 416 + p, 464, 4), win("yb", 256 * p, x), A("wt", SL[3, :, 4 * x:4 * x + 4])) for p in range(4) for x in range(2)]
           + [(ps(7, 416, 464), A("z1", SL[15 - u:143 - u]), A("mk", SL[:, :, :, u])) for u in range(16)])
        ts(A("ybuf", SL[48 * t:48 * t + 48]), ps(7, 416, 464), -2048.0, -1.0, ALU.add, ALU.max)
        for m in range(3):
            k = 3 * t + m
            dma("S" if last and m == 1 else "Y", [(A("yn", SL[256 * k:256 * k + 256]), A("ybuf", SL[16 * k:16 * k + 16]))], "out%d" % k, 2.0)
    return ops


def timing(o, c):
    cy, pcy, rg, rs, _, _, lat_r, issue, way = c
    k, x = o["kind"], o["x"]
    dur = {"v": 0.015 + max(64, x) * cy, "vg": 0.05 + max(64, x * rg) * cy, "vs": 0.05 + max(64, x * rs) * cy, "s": 0.1 + max(64, x) * cy,
           "sg": 0.065 + x * rg * cy, "g": 0.13 + 2 * x * cy, "p": 0.03 + x * pcy, "fix": x, "gd": issue, "rd": 0.3}[k]
    return dur + o["more"], {"gd": way, "rd": lat_r + x}.get(k, o["lat"])


def find_deps(ops):
    writers, readers, bank = {}, {}, {}
    deps = []
    for i, o in enumerate(ops):
        d = {}
        for a in o["wr"]:
            m = cover(a)
            for j, mj in readers.get(a[0], []):
                if m & mj:
                    d[j] = "a"
        for a in o["rd"] + o["wr"]:
            m = cover(a)
            for j, mj in writers.get(a[0], []):
                if m & mj:
                    d[j] = "r"
        if o["bank"] is not None:
            if o["bank"] in bank:
                d.setdefault(bank[o["bank"]], "s")
            bank[o["bank"]] = i
        for j in o.get("after", []):
            d.setdefault(j, "s")
        d.pop(i, None)
        deps.append(d)
        for a in o["wr"]:
            m = cover(a)
            writers[a[0]] = [(j, mj & ~m) for j, mj in writers.get(a[0], []) if mj & ~m] + [(i, m)]
            readers[a[0]] = [(j, mj & ~m) for j, mj in readers.get(a[0], []) if mj & ~m]
        for a in o["rd"]:
            readers.setdefault(a[0], []).append((i, cover(a)))
    return deps


def order_queues(ops, deps):
    n = len(ops)
    eng = ["VSPGY".index(o["eng"]) for o in ops]
    tabs = []
    for c in COSTS:
        tm = [timing(o, c) for o in ops]
        pre = [[(j, FIRST_CALL if j in ops[i].get("after", []) and h == "s" else
                 (1.5 if h == "a" and ops[j]["arr"] else tm[j][1]) + c[4] if (eng[j] != eng[i] or (h != "s" and ops[j]["sem"])) else (c[5] if h != "s" and eng[i] != 2 else 0.0))
                for j, h in deps[i].items()] for i in range(n)]
        suc = [[] for _ in range(n)]
        for i in range(n):
            for j, gp in pre[i]:
                suc[j].append((i, gp))
        tabs.append(([x[0] for x in tm], [x[1] for x in tm], pre, suc))

    def place(seq, dur, edges, head):
        fin = [0.0] * n; busy = [([], []) for _ in range(5)]
        for i in seq:
            t0 = head[i]
            for j, gp in edges[i]:
                if fin[j] + gp > t0:
                    t0 = fin[j] + gp
            st, en = busy[eng[i]]; d = dur[i]
            k = len(st)
            while k > 0 and en[k - 1] > t0:
                k -= 1
            while k < len(st) and t0 + d > st[k] + 1e-9:
                t0 = max(t0, en[k]); k += 1
            st.insert(k, t0); en.insert(k, t0 + d); fin[i] = t0 + d
        return fin

    ends = [i for i in range(n) if not tabs[0][3][i]]

    def replay(order, tab, old=None, p0=0):
        d, lt, pr, _ = tab
        fin = list(old) if p0 else [0.0] * n
        free = [0.0] * 5
        for i in order[:p0]:
            free[eng[i]] = fin[i]
        for i in order[p0:]:
            t0 = free[eng[i]]
            for j, gp in pr[i]:
                if fin[j] + gp > t0:
                    t0 = fin[j] + gp
            fin[i] = free[eng[i]] = t0 + d[i]
        return fin, max([fin[i] + lt[i] for i in ends])

    def legal(key, edges, ahead):
        key = list(key)
        for i in (range(n) if ahead else range(n - 1, -1, -1)):
            for j, _ in edges[i]:
                if key[j] >= key[i]:
                    key[i] = key[j] + 1e-6
        return sorted(range(n), key=lambda i: key[i])
    rng = np.random.default_rng(SEED)
    scale = [w / c[0] / (1.0 + c[2]) for w, c in zip(WEIGHT, COSTS)]
    zero = [0.0] * n
    best = None
    for it in range(SEARCH):
        dur, lat, pre, suc = tabs[PLACE[it % len(PLACE)]]
        if it < 40:
            key = [0.0] * n; per = 12.0 + it // 4
            for i in range(n - 1, -1, -1):
                key[i] = min([key[j] - gp for j, gp in suc[i]] + [RO * per + 3 - lat[i]]) - dur[i]
                if "at" in ops[i]:
                    key[i] = min(key[i], ops[i]["at"] * per)
        else:
            sz = float(rng.choice(NOISE))
            noise = rng.normal(size=n) * sz * (rng.random(n) < float(rng.choice([0.02, 0.1, 0.5])))
            if WINDOW:
                noise = noise * (np.abs(np.array(best[2]) - rng.random() * 100) < WINDOW)
            key = [float(x) for x in np.array(best[2]) + noise]
        fin = place(legal(key, pre, True), dur, pre, zero)
        for _ in range(PASSES[it // 4 % len(PASSES)]):
            back = place(legal([-x for x in fin], suc, False), dur, suc, lat)
            fin = place(legal([-x for x in back], pre, True), dur, pre, zero)
        start = [fin[i] - dur[i] for i in range(n)]
        order = legal(start, pre, True)
        sc = sum(replay(order, tab)[1] * w for tab, w in zip(tabs, scale))
        if best is None or sc <= best[0]:
            best = (sc, order, start)

    def critical(order, tab, fin):
        d, lt, pr, _ = tab
        prev = {}; lastq = [-1] * 5
        for i in order:
            prev[i] = lastq[eng[i]]; lastq[eng[i]] = i
        i = max(range(n), key=lambda x: fin[x] + lt[x]); arcs = []
        while True:
            t0 = fin[i] - d[i]; p = prev[i]
            nx = [j for j, gp in pr[i] if abs(fin[j] + gp - t0) < 1e-9]
            if p >= 0 and abs(fin[p] - t0) < 1e-9 and p not in deps[i] and (not nx or rng.random() < 0.5):
                arcs.append((p, i)); i = p
            elif nx:
                i = nx[0]
            elif p >= 0 and abs(fin[p] - t0) < 1e-9:
                i = p
            else:
                return arcs

    def swap(order, u, v):
        pu, pv = order.index(u), order.index(v)
        tied = {u}; tq = set(); ahead = []; behind = []
        for x in order[pu + 1:pv]:
            if eng[x] in tq or any(j in tied for j in deps[x]):
                tied.add(x); tq.add(eng[x]); behind.append(x)
            else:
                ahead.append(x)
        if any(j in tied for j in deps[v]):
            return None
        return order[:pu] + ahead + [v, u] + behind + order[pv + 1:]

    def tails(order, tab):
        d, lt, _, sc_ = tab
        tl = [0.0] * n; nx = [0.0] * 5
        for i in reversed(order):
            t0 = max(nx[eng[i]], lt[i])
            for j, gp in sc_[i]:
                if tl[j] + gp > t0:
                    t0 = tl[j] + gp
            tl[i] = nx[eng[i]] = t0 + d[i]
        return tl

    def bound(new, p0, p1, tab, fin, tl):
        d, _, pr, sc_ = tab
        loc = {}; free = {}; top_ = 0.0
        for i in new[p0:p1 + 1]:
            e = eng[i]
            if e not in free:
                q = p0 - 1
                while q >= 0 and eng[new[q]] != e:
                    q -= 1
                free[e] = fin[new[q]] if q >= 0 else 0.0
            t0 = free[e]
            for j, gp in pr[i]:
                f = loc.get(j, fin[j]) + gp
                if f > t0:
                    t0 = f
            loc[i] = free[e] = t0 + d[i]
        for i, f in loc.items():
            for j, gp in sc_[i]:
                if j not in loc and f + gp + tl[j] > top_:
                    top_ = f + gp + tl[j]
        for e, f in free.items():
            q = p1 + 1
            while q < n and eng[new[q]] != e:
                q += 1
            if q < n and f + tl[new[q]] > top_:
                top_ = f + tl[new[q]]
        return top_
    cur = best[1]; res = [replay(cur, tab) for tab in tabs]; csc = best[0]; top = (csc, cur)
    tls = [tails(cur, tab) for tab in tabs]; ways = {}
    for it in range(SWAPS):
        k = int(rng.integers(2 * len(tabs)))
        if k not in ways:
            ways[k] = critical(cur, tabs[k // 2], res[k // 2][0])
        arcs = ways[k]
        if not arcs:
            continue
        u, v = arcs[int(rng.integers(len(arcs)))]
        new = swap(cur, u, v)
        if new is None:
            continue
        early = rng.random() < 0.5
        for _ in range(int(rng.choice(STEPS))):
            if early:
                p = new.index(v) - 1
                while p >= 0 and eng[new[p]] != eng[v]:
                    p -= 1
                more = swap(new, new[p], v) if p >= 0 and new[p] not in deps[v] else None
            else:
                p = new.index(u) + 1
                while p < n and eng[new[p]] != eng[u]:
                    p += 1
                more = swap(new, u, new[p]) if p < n and u not in deps[new[p]] else None
            if more is None:
                break
            new = more
        p0 = 0
        while new[p0] == cur[p0]:
            p0 += 1
        p1 = n - 1
        while new[p1] == cur[p1]:
            p1 -= 1
        limit = csc + HEAT * (1.0 - it / SWAPS) * float(rng.exponential()) * scale[0]
        if sum(bound(new, p0, p1, tab, r[0], tl) * w for tab, r, tl, w in zip(tabs, res, tls, scale)) > limit + 1e-9:
            continue
        nres = [replay(new, tab, r[0], p0) for tab, r in zip(tabs, res)]
        sc = sum(r[1] * w for r, w in zip(nres, scale))
        if sc <= limit:
            cur, res, csc = new, nres, sc
            tls = [tails(cur, tab) for tab in tabs]; ways = {}
            if sc < top[0]:
                top = (sc, cur)
    return top[1], [replay(top[1], tab) for tab in tabs]


def rank_program(g, core, T, topo):
    if T.rank_of(core) is None:
        return
    ops = build_ops(g, core, T, topo)
    if "all" not in ORDER:
        ORDER["deps"] = find_deps(ops)
        ORDER["all"], ORDER["times"] = order_queues(ops, ORDER["deps"])
    order, deps = ORDER["all"], ORDER["deps"]
    queue = {"V": g.vector, "S": g.scalar, "P": g.tensor, "G": g, "Y": g.sync}
    pos = {i: k for k, i in enumerate(order)}
    waits = {}; seen = {e: {} for e in "VSPGY"}; knew = {}; need = set()
    for i in order:
        e = ops[i]["eng"]; w = {}
        for j, h in deps[i].items():
            f = ops[j]["eng"]
            if ops[j]["sem"] or (f == e and (e == "P" or h == "s")):
                continue
            if pos[j] > seen[e].get(f, -1) and pos[j] > pos.get(w.get(f), -1):
                w[f] = j
        for f in list(w):
            if any(x != f and knew[w[x]].get(f, -1) >= pos[w[f]] for x in w):
                del w[f]
        for f, j in w.items():
            need.add(j)
            for x, v in list(knew[j].items()) + [(f, pos[j])]:
                seen[e][x] = max(seen[e].get(x, -1), v)
        waits[i] = w; knew[i] = dict(seen[e])
    ORDER["waits"] = sum(len(w) for w in waits.values())
    count = {}; num = {e: 0 for e in "VSPG"}
    for i in order:
        if i in need:
            num[ops[i]["eng"]] += 1; count[i] = num[ops[i]["eng"]]
    done = {}; total = {}; waited = {}
    for i in order:
        o = ops[i]; e = o["eng"]; q = queue[e]
        for j, h in deps[i].items():
            if h != "s" and ops[j]["sem"]:
                nm, v = ops[j]["arr"] if h == "r" and ops[j]["arr"] else ops[j]["sem"]
                if done.get((e, nm), 0) < v:
                    done[(e, nm)] = v; q.wait_ge(T.sem[nm], v); waited[nm] = max(v, waited.get(nm, 0))
        for f, j in waits[i].items():
            q.wait_ge(T.sem["c" + f], count[j])
        ins = o["fn"]()
        if i in need:
            ins.then_inc(T.sem["c" + e], 1)
        for x in (o["sem"], o["arr"]):
            if x:
                total[x[0]] = max(total.get(x[0], 0), x[1])
    for nm, v in total.items():
        if waited.get(nm, 0) < v:
            g.wait_ge(T.sem[nm], v)
